import numpy as np
import ml_dtypes


def mxq(x, axis, fmt="e4m3"):
    dtype, down = {"e4m3": (ml_dtypes.float8_e4m3fn, 7), "e5m2": (ml_dtypes.float8_e5m2, 14)}[fmt]
    v = np.moveaxis(np.asarray(x, np.float32).astype(ml_dtypes.bfloat16).astype(np.float64), axis, -1)
    blocks = v.reshape(v.shape[:-1] + (-1, 32))
    amax = np.abs(blocks).max(-1, keepdims=True)
    byte = np.maximum(np.where(amax > 0, np.frexp(amax)[1] - 1 + 127, 0) - down, 1)
    scale = np.exp2(byte - 127.0)
    codes = (blocks / scale).astype(np.float32).astype(dtype).astype(np.float64)
    return np.moveaxis((codes * scale).reshape(v.shape), -1, axis)


WIDE = False


def mx_kscale(k):
    if not WIDE:
        return np.ones(k)
    levels = np.array([10, -10, 5, -5, 0])
    if k % 512:
        return np.exp2(np.random.permutation(np.resize(levels, k // 32))).repeat(32)
    a = np.empty((k // 512, 16))
    for p in range(k // 512):
        a[p, :8] = np.random.permutation(np.resize(levels, 8))
        for g in range(8):
            far = levels[np.abs(levels - a[p, g]) >= 10]
            a[p, g + 8] = far[np.random.randint(len(far))]
    return np.exp2(a.ravel()).repeat(32)


def f64(x):
    return np.asarray(x).astype(np.float64)


def striped(idx):
    return np.tile(idx.reshape(-1, 16).T, (8, 1)).astype(np.uint16)


def unstriped(offs):
    return offs[:16].T.reshape(-1).astype(np.int64)


def pack_weight(w):
    k, n = w.shape
    w = f64(np.asarray(w, np.float32).astype(ml_dtypes.bfloat16)).reshape(k // 32, 32, n)
    amax = np.abs(w).max(1)
    byte = np.clip(np.where(amax > 0, np.frexp(amax)[1] - 1 + 127 - 7, 1), 1, 254)
    scaled = (w * np.exp2(127.0 - byte)[:, None, :]).reshape(k, n).astype(np.float32)
    words = np.ascontiguousarray(scaled.reshape(k // 512, 128, 4, n).transpose(0, 1, 3, 2)).astype(ml_dtypes.float8_e4m3fn).view(np.uint8)
    return words, np.ascontiguousarray(byte.astype(np.uint8).reshape(k // 512, 16, n))


def unpack_weight(words, scales):
    g, p, n, _ = words.shape
    vals = np.ascontiguousarray(words).view(ml_dtypes.float8_e4m3fn).astype(np.float64) * np.repeat(np.exp2(scales.astype(np.float64) - 127.0), 8, axis=1)[..., None]
    return vals.transpose(0, 1, 3, 2).reshape(g * 512, n)


E2M1 = np.array([0.0, 0.5, 1.0, 1.5, 2.0, 3.0, 4.0, 6.0, -0.0, -0.5, -1.0, -1.5, -2.0, -3.0, -4.0, -6.0])


def pack_fp4(w):
    k, n = w.shape
    w = f64(np.asarray(w, np.float32).astype(ml_dtypes.bfloat16)).reshape(k // 32, 32, n)
    amax = np.abs(w).max(1)
    mant, ex = np.frexp(amax / 6.0)
    byte = np.clip(np.where(amax > 0, np.where(mant > 0.5, ex, ex - 1) + 127, 1), 1, 254)
    scaled = (w * np.exp2(127.0 - byte)[:, None, :]).reshape(k, n).astype(np.float32)
    c = np.ascontiguousarray(scaled.reshape(k // 512, 128, 4, n).transpose(0, 1, 3, 2)).astype(ml_dtypes.float4_e2m1fn).view(np.uint8) & 0xF
    words = (c[..., 0::2] | (c[..., 1::2] << 4)).reshape(k // 512, 128, 2 * n)
    return np.ascontiguousarray(words), np.ascontiguousarray(byte.astype(np.uint8).reshape(k // 512, 16, n))


def unpack_fp4(words, scales):
    g, _, n = scales.shape
    words = np.ascontiguousarray(words).reshape(g, 128, n, 2)
    nib = np.empty((g, 128, n, 4), np.uint8)
    nib[..., 0::2] = words & 0xF
    nib[..., 1::2] = words >> 4
    vals = E2M1[nib] * np.repeat(np.exp2(scales.astype(np.float64) - 127.0), 8, axis=1)[..., None]
    return vals.transpose(0, 1, 3, 2).reshape(g * 512, n)


def relu(v):
    return np.maximum(v, 0.0)


K, T, H, N = 512, 1024, 512, 256


def setup_inputs():
    n = np.random.standard_normal
    s = mx_kscale(K)[:, None]
    u = mx_kscale(H)
    packed_xT = pack_weight(n((K, T)) * s)
    packed_w3 = pack_fp4(n((H, N)) / np.sqrt(H) / u[:, None])
    return {
        "x_words": packed_xT[0],
        "x_scales": packed_xT[1],
        "w1": (n((K, H)) / np.sqrt(2 * K) / s * u).astype(np.float32),
        "w2": (n((K, H)) / np.sqrt(2 * K) / s * u).astype(np.float32),
        "w3_words": packed_w3[0],
        "w3_scales": packed_w3[1],
        "pos1": striped(np.random.permutation(T)),
        "pos2": striped(np.random.permutation(T)),
    }


def reference(x_words, x_scales, w1, w2, w3_words, w3_scales, pos1, pos2):
    xq = unpack_weight(x_words, x_scales)
    y = mxq(f64(w1), 0, "e4m3").T @ xq
    e = mxq(f64(w2), 0, "e4m3").T @ xq
    z = np.maximum(relu(y + e[:, unstriped(pos1)]), relu(y + e[:, unstriped(pos2)]))
    return unpack_fp4(w3_words, w3_scales).T @ mxq(z, 0, "e4m3")

@@ -1,0 +1,181 @@
+from contextlib import ExitStack
+
+import concourse.mybir as mybir
+
+K, T, H, N = 512, 1024, 512, 256
+FLOPS = 2 * K * H * T * 2 + 2 * H * N * T
+
+F32 = mybir.dt.float32
+BF16 = mybir.dt.bfloat16
+I32 = mybir.dt.int32
+U32 = mybir.dt.uint32
+U16 = mybir.dt.uint16
+U8 = mybir.dt.uint8
+FP8X4 = mybir.dt.float8_e4m3fn_x4
+FP4X4 = mybir.dt.float4_e2m1fn_x4
+ADD = mybir.AluOpType.add
+MAX = mybir.AluOpType.max
+RELU = mybir.ActivationFunctionType.Relu
+COPY = mybir.ActivationFunctionType.Copy
+
+P = 128
+PACK = 4
+HALF = T // 2
+CHUNKS = ((0, 512), (512, 256), (768, 128), (896, 128))
+
+
+def tile_picked_wedgecv_relu_l_kernel(
+    tc, x_words, x_scales, w1, w2, w3_words, w3_scales, pos1, pos2, out
+):
+    nc = tc.nc
+    with ExitStack() as ctx:
+        keep = ctx.enter_context(tc.tile_pool(name="keep", bufs=1))
+        ring = ctx.enter_context(tc.tile_pool(name="ring", bufs=2))
+        first = ctx.enter_context(tc.psum_pool(name="first", bufs=6))
+        last = ctx.enter_context(tc.psum_pool(name="last", bufs=2))
+
+        x_sc = keep.tile([P, T], U8, name="x_sc", align_bytes=64)
+        w3_sc = keep.tile([P, N], U8, name="w3_sc", align_bytes=64)
+        nc.gpsimd.memset(x_sc[:].bitcast(U32), 0)
+        nc.gpsimd.memset(w3_sc[:].bitcast(U32), 0)
+
+        w2_raw = keep.tile([P, PACK, H], F32, name="w2_raw")
+        w1_raw = keep.tile([P, PACK, H], F32, name="w1_raw")
+        nc.sync.dma_start(out=w2_raw[:], in_=w2.rearrange("(p j) c -> p j c", j=PACK))
+        nc.sync.dma_start(out=w1_raw[:], in_=w1.rearrange("(p j) c -> p j c", j=PACK))
+        x_src = x_words[0].rearrange("p n r -> p (n r)").bitcast(I32)
+        x_cd = [keep.tile([P, HALF], U32, name="x_cd%d" % h, align_bytes=64) for h in range(2)]
+        for h in range(2):
+            nc.sync.dma_start(out=x_cd[h][:].bitcast(I32), in_=x_src[:, h * HALF : (h + 1) * HALF])
+        for r in range(4):
+            nc.scalar.dma_start(out=x_sc[r:P:32, :].bitcast(I32), in_=x_scales[0][r:16:4, :].bitcast(I32))
+        lists = [keep.tile([P, T // 16], U16, name="list%d" % d) for d in range(2)]
+        nc.sync.dma_start(lists[0][:], pos1)
+        nc.sync.dma_start(lists[1][:], pos2)
+        w3_cd = keep.tile([P, 2 * N], U8, name="w3_cd", align_bytes=64)
+        nc.sync.dma_start(out=w3_cd[:].bitcast(I32), in_=w3_words[0].bitcast(I32))
+        for r in range(4):
+            nc.sync.dma_start(out=w3_sc[r:P:32, :].bitcast(I32), in_=w3_scales[0][r:16:4, :].bitcast(I32))
+
+        w2_bf = keep.tile([P, PACK * H], BF16, name="w2_bf", align_bytes=64)
+        w2_cd = keep.tile([P, H], U32, name="w2_cd", align_bytes=64)
+        w2_sc = keep.tile([P, H], U8, name="w2_sc", align_bytes=64)
+        nc.vector.tensor_copy(
+            out=w2_bf[:].rearrange("p (t m j) -> p m j t", t=4, j=4),
+            in_=w2_raw[:].rearrange("p j (m t) -> p m j t", t=4),
+        )
+        nc.vector.quantize_mx(out=w2_cd[:].bitcast(FP8X4), scales=w2_sc[:], in_=w2_bf[:])
+
+        w1_bf = [keep.tile([P, 2 * H], BF16, name="w1_bf%d" % u, align_bytes=64) for u in range(2)]
+        w1_cd = [keep.tile([P, 2 * P], U32, name="w1_cd%d" % u, align_bytes=64) for u in range(2)]
+        w1_sc = [keep.tile([P, 2 * P], U8, name="w1_sc%d" % u, align_bytes=64) for u in range(2)]
+        w1_src = w1_raw[:].rearrange("p j (m t) -> p m j t", t=4)
+        nc.vector.tensor_copy(
+            out=w1_bf[0][:].rearrange("p (t m j) -> p m j t", t=2, j=4), in_=w1_src[:, :, :, 0:2]
+        )
+        nc.scalar.activation(
+            out=w1_bf[1][:].rearrange("p (t m j) -> p m j t", t=2, j=4), in_=w1_src[:, :, :, 2:4], func=COPY
+        )
+        for u in range(2):
+            nc.vector.quantize_mx(out=w1_cd[u][:].bitcast(FP8X4), scales=w1_sc[u][:], in_=w1_bf[u][:])
+
+        e = [keep.tile([P, T], F32, name="e%d" % t) for t in range(PACK)]
+        y = [keep.tile([P, T], F32, name="y%d" % t) for t in range(PACK)]
+
+        def project(dst, codes, scales, h, on_vector):
+            cols = slice(h * HALF, (h + 1) * HALF)
+            acc = first.tile([P, HALF], F32, name="acc")
+            nc.tensor.matmul_mx(
+                out=acc[:],
+                lhsT=codes.bitcast(FP8X4),
+                lhsT_scale=scales,
+                rhs=x_cd[h][:].bitcast(FP8X4),
+                rhs_scale=x_sc[:, cols],
+                start=True,
+                stop=True,
+            )
+            if on_vector:
+                nc.vector.tensor_copy(out=dst[:, cols], in_=acc[:])
+            else:
+                nc.scalar.copy(out=dst[:, cols], in_=acc[:])
+
+        def make_e(t, h, on_vector=False):
+            m = slice(t * P, (t + 1) * P)
+            project(e[t], w2_cd[:, m], w2_sc[:, m], h, on_vector)
+
+        def make_y(t, h):
+            m = slice((t % 2) * P, (t % 2 + 1) * P)
+            project(y[t], w1_cd[t // 2][:, m], w1_sc[t // 2][:, m], h, False)
+
+        edges, rounded, z_cd, z_sc = {}, {}, {}, {}
+
+        def gather(c, t, d):
+            v0, n = CHUNKS[c]
+            if (c, d) not in edges:
+                edges[(c, d)] = ring.tile([P, PACK, n], F32, name="edge%d_%d" % (c, d), tag="edge%d" % d)
+            nc.vector.tensor_tensor(
+                edges[(c, d)][:, t, :],
+                e[t][:].indirect(lists[d][:, v0 // 16 : (v0 + n) // 16]),
+                y[t][:, v0 : v0 + n],
+                ADD,
+            )
+
+        def round_edges(c, d):
+            n = CHUNKS[c][1]
+            rounded[(c, d)] = keep.tile([P, PACK * n], BF16, name="round%d_%d" % (c, d), align_bytes=64)
+            nc.scalar.activation(
+                out=rounded[(c, d)][:].rearrange("p (c i t) -> p c t i", i=4, t=4),
+                in_=edges[(c, d)][:].rearrange("p t (c i) -> p c t i", i=4),
+                func=RELU,
+            )
+
+        def largest(c):
+            n = CHUNKS[c][1]
+            z = keep.tile([P, PACK * n], BF16, name="z%d" % c, align_bytes=64)
+            nc.vector.tensor_tensor(z[:], rounded[(c, 0)][:], rounded[(c, 1)][:], MAX)
+            z_cd[c] = keep.tile([P, n], U32, name="z_cd%d" % c, align_bytes=64)
+            z_sc[c] = keep.tile([P, n], U8, name="z_sc%d" % c, align_bytes=64)
+            nc.vector.quantize_mx(out=z_cd[c][:].bitcast(FP8X4), scales=z_sc[c][:], in_=z[:])
+
+        out_v = out.rearrange("(h p) v -> p h v", p=P)
+
+        def finish(c):
+            v0, n = CHUNKS[c]
+            res = keep.tile([P, 2, n], F32, name="res%d" % c)
+            for h in range(2):
+                acc = last.tile([P, n], F32, name="acc_out")
+                nc.tensor.matmul_mx(
+                    out=acc[:],
+                    lhsT=w3_cd[:, 2 * P * h : 2 * P * (h + 1)].bitcast(FP4X4),
+                    lhsT_scale=w3_sc[:, P * h : P * (h + 1)],
+                    rhs=z_cd[c][:].bitcast(FP8X4),
+                    rhs_scale=z_sc[c][:],
+                    start=True,
+                    stop=True,
+                )
+                nc.scalar.copy(out=res[:, h, :], in_=acc[:])
+            nc.sync.dma_start(out=out_v[:, :, v0 : v0 + n], in_=res[:])
+
+        make_e(0, 0, on_vector=True)
+        make_y(0, 0)
+        make_e(0, 1)
+        for t in range(PACK):
+            if t + 1 < PACK:
+                make_e(t + 1, 0)
+                make_e(t + 1, 1)
+                make_y(t + 1, 0)
+            gather(0, t, 0)
+            gather(0, t, 1)
+        for t in range(PACK):
+            make_y(t, 1)
+        round_edges(0, 0)
+        round_edges(0, 1)
+        for c in range(1, len(CHUNKS)):
+            for d in range(2):
+                for t in range(PACK):
+                    gather(c, t, d)
+                round_edges(c, d)
+            largest(c - 1)
+            finish(c - 1)
+        largest(len(CHUNKS) - 1)
+        finish(len(CHUNKS) - 1)

@@ -1,6 +1,7 @@
 from contextlib import ExitStack
 
 import concourse.mybir as mybir
+from concourse.masks import make_identity
 
 K, T, H, N = 512, 1024, 512, 256
 FLOPS = 2 * K * H * T * 2 + 2 * H * N * T
@@ -14,6 +15,7 @@ U8 = mybir.dt.uint8
 FP8X4 = mybir.dt.float8_e4m3fn_x4
 FP4X4 = mybir.dt.float4_e2m1fn_x4
 ADD = mybir.AluOpType.add
+SUB = mybir.AluOpType.subtract
 MAX = mybir.AluOpType.max
 RELU = mybir.ActivationFunctionType.Relu
 COPY = mybir.ActivationFunctionType.Copy
@@ -30,89 +32,144 @@ def tile_picked_wedgecv_relu_l_kernel(
     nc = tc.nc
     with ExitStack() as ctx:
         keep = ctx.enter_context(tc.tile_pool(name="keep", bufs=1))
-        ring = ctx.enter_context(tc.tile_pool(name="ring", bufs=2))
-        first = ctx.enter_context(tc.psum_pool(name="first", bufs=6))
-        last = ctx.enter_context(tc.psum_pool(name="last", bufs=2))
+        first = ctx.enter_context(tc.psum_pool(name="first", bufs=4))
+        turn = ctx.enter_context(tc.psum_pool(name="turn", bufs=4))
 
         x_sc = keep.tile([P, T], U8, name="x_sc", align_bytes=64)
         w3_sc = keep.tile([P, N], U8, name="w3_sc", align_bytes=64)
+        ident = keep.tile([P, P], F32, name="ident")
         nc.gpsimd.memset(x_sc[:].bitcast(U32), 0)
         nc.gpsimd.memset(w3_sc[:].bitcast(U32), 0)
+        make_identity(nc, ident[:])
 
         w2_raw = keep.tile([P, PACK, H], F32, name="w2_raw")
-        w1_raw = keep.tile([P, PACK, H], F32, name="w1_raw")
-        nc.sync.dma_start(out=w2_raw[:], in_=w2.rearrange("(p j) c -> p j c", j=PACK))
-        nc.sync.dma_start(out=w1_raw[:], in_=w1.rearrange("(p j) c -> p j c", j=PACK))
-        x_src = x_words[0].rearrange("p n r -> p (n r)").bitcast(I32)
-        x_cd = [keep.tile([P, HALF], U32, name="x_cd%d" % h, align_bytes=64) for h in range(2)]
-        for h in range(2):
-            nc.sync.dma_start(out=x_cd[h][:].bitcast(I32), in_=x_src[:, h * HALF : (h + 1) * HALF])
-        for r in range(4):
-            nc.scalar.dma_start(out=x_sc[r:P:32, :].bitcast(I32), in_=x_scales[0][r:16:4, :].bitcast(I32))
+        w1_raw = keep.tile([P, PACK, H], F32, name="w1_raw", tag="w1_raw")
+        x_cd = keep.tile([P, T], U32, name="x_cd", align_bytes=64)
         lists = [keep.tile([P, T // 16], U16, name="list%d" % d) for d in range(2)]
+        nc.sync.dma_start(out=w2_raw[:], in_=w2.rearrange("(p j) c -> p j c", j=PACK))
+        for r in range(4):
+            nc.sync.dma_start(out=x_sc[r:P:32, :].bitcast(I32), in_=x_scales[0][r:16:4, :].bitcast(I32))
+        nc.sync.dma_start(out=x_cd[:].bitcast(I32), in_=x_words[0].rearrange("p n r -> p (n r)").bitcast(I32))
         nc.sync.dma_start(lists[0][:], pos1)
         nc.sync.dma_start(lists[1][:], pos2)
+        nc.sync.dma_start(out=w1_raw[:], in_=w1.rearrange("(p j) c -> p j c", j=PACK))
         w3_cd = keep.tile([P, 2 * N], U8, name="w3_cd", align_bytes=64)
         nc.sync.dma_start(out=w3_cd[:].bitcast(I32), in_=w3_words[0].bitcast(I32))
         for r in range(4):
             nc.sync.dma_start(out=w3_sc[r:P:32, :].bitcast(I32), in_=w3_scales[0][r:16:4, :].bitcast(I32))
 
-        w2_bf = keep.tile([P, PACK * H], BF16, name="w2_bf", align_bytes=64)
-        w2_cd = keep.tile([P, H], U32, name="w2_cd", align_bytes=64)
-        w2_sc = keep.tile([P, H], U8, name="w2_sc", align_bytes=64)
-        nc.vector.tensor_copy(
-            out=w2_bf[:].rearrange("p (t m j) -> p m j t", t=4, j=4),
-            in_=w2_raw[:].rearrange("p j (m t) -> p m j t", t=4),
-        )
-        nc.vector.quantize_mx(out=w2_cd[:].bitcast(FP8X4), scales=w2_sc[:], in_=w2_bf[:])
+        w_raw = {1: w1_raw, 2: w2_raw}
+        w_bf, w_cd, w_sc = {}, {}, {}
 
-        w1_bf = [keep.tile([P, 2 * H], BF16, name="w1_bf%d" % u, align_bytes=64) for u in range(2)]
-        w1_cd = [keep.tile([P, 2 * P], U32, name="w1_cd%d" % u, align_bytes=64) for u in range(2)]
-        w1_sc = [keep.tile([P, 2 * P], U8, name="w1_sc%d" % u, align_bytes=64) for u in range(2)]
-        w1_src = w1_raw[:].rearrange("p j (m t) -> p m j t", t=4)
-        nc.vector.tensor_copy(
-            out=w1_bf[0][:].rearrange("p (t m j) -> p m j t", t=2, j=4), in_=w1_src[:, :, :, 0:2]
-        )
-        nc.scalar.activation(
-            out=w1_bf[1][:].rearrange("p (t m j) -> p m j t", t=2, j=4), in_=w1_src[:, :, :, 2:4], func=COPY
-        )
-        for u in range(2):
-            nc.vector.quantize_mx(out=w1_cd[u][:].bitcast(FP8X4), scales=w1_sc[u][:], in_=w1_bf[u][:])
+        def cast(w, u):
+            w_bf[w, u] = keep.tile([P, 2 * H], BF16, name="w%d_bf%d" % (w, u), align_bytes=64)
+            dst = w_bf[w, u][:].rearrange("p (t m j) -> p m j t", t=2, j=4)
+            src = w_raw[w][:].rearrange("p j (m t) -> p m j t", t=4)[:, :, :, 2 * u : 2 * u + 2]
+            if u == 0:
+                nc.vector.tensor_copy(out=dst, in_=src)
+            else:
+                nc.scalar.activation(out=dst, in_=src, func=COPY)
+
+        def quantise_w(w, u):
+            w_cd[w, u] = keep.tile([P, 2 * P], U32, name="w%d_cd%d" % (w, u), tag="w%d_cd%d" % (w, u), align_bytes=64)
+            w_sc[w, u] = keep.tile([P, 2 * P], U8, name="w%d_sc%d" % (w, u), align_bytes=64)
+            nc.vector.quantize_mx(out=w_cd[w, u][:].bitcast(FP8X4), scales=w_sc[w, u][:], in_=w_bf[w, u][:])
 
         e = [keep.tile([P, T], F32, name="e%d" % t) for t in range(PACK)]
         y = [keep.tile([P, T], F32, name="y%d" % t) for t in range(PACK)]
+        on_s, on_v = nc.scalar.copy, nc.vector.tensor_copy
 
-        def project(dst, codes, scales, h, on_vector):
+        banks = {}
+
+        def product(w, t, h):
             cols = slice(h * HALF, (h + 1) * HALF)
-            acc = first.tile([P, HALF], F32, name="acc")
+            m = slice((t % 2) * P, (t % 2 + 1) * P)
+            acc = first.tile([P, HALF], F32, name="acc", tag="acc")
             nc.tensor.matmul_mx(
                 out=acc[:],
-                lhsT=codes.bitcast(FP8X4),
-                lhsT_scale=scales,
-                rhs=x_cd[h][:].bitcast(FP8X4),
+                lhsT=w_cd[w, t // 2][:, m].bitcast(FP8X4),
+                lhsT_scale=w_sc[w, t // 2][:, m],
+                rhs=x_cd[:, cols].bitcast(FP8X4),
                 rhs_scale=x_sc[:, cols],
                 start=True,
                 stop=True,
             )
-            if on_vector:
-                nc.vector.tensor_copy(out=dst[:, cols], in_=acc[:])
+            banks[w, t, h] = acc
+
+        def bring(w, t, h, copy=on_s):
+            copy(out=(y if w == 1 else e)[t][:, h * HALF : (h + 1) * HALF], in_=banks[w, t, h][:])
+
+        def project(w, t, h, copy=on_s):
+            product(w, t, h)
+            bring(w, t, h, copy)
+
+        nA = CHUNKS[0][1]
+        g, diff = {}, {}
+        gain = {}
+        z_t = keep.tile([P, nA // P, 2, 2 * P], BF16, name="z_t", tag="z_t", align_bytes=64)
+
+        def gather_pair(t):
+            pieces = [slice(a, a + nA // 2) for a in (0, nA // 2)]
+            g[t] = keep.tile([P, nA], F32, name="g%d" % t, tag="w1_raw" if t == 1 else "g%d" % t)
+            diff[t] = keep.tile([P, nA], F32, name="diff%d" % t, tag="diff%d" % t)
+            for s in pieces:
+                nc.vector.tensor_copy(g[t][:, s], e[t][:].indirect(lists[0][:, s.start // 16 : s.stop // 16]))
+            for s in pieces:
+                nc.vector.tensor_tensor(
+                    diff[t][:, s], e[t][:].indirect(lists[1][:, s.start // 16 : s.stop // 16]), g[t][:, s], SUB
+                )
+
+        def relu_diff(t, parts=1):
+            if t < 2:
+                gain[t] = keep.tile([P, nA], F32, name="gain%d" % t, tag=("gain0", "w2_cd1")[t], align_bytes=64)[:]
+            elif t == 2:
+                gain[t] = keep.tile([P, nA], F32, name="gain2", tag="w1_cd1", align_bytes=64)[:]
             else:
-                nc.scalar.copy(out=dst[:, cols], in_=acc[:])
+                gain[t] = keep.tile([P, nA], F32, name="gain3", tag="w1_raw")[:]
+            for a in range(0, nA, nA // parts):
+                s = slice(a, a + nA // parts)
+                nc.scalar.activation(out=gain[t][:, s], in_=diff[t][:, s], func=RELU)
 
-        def make_e(t, h, on_vector=False):
-            m = slice(t * P, (t + 1) * P)
-            project(e[t], w2_cd[:, m], w2_sc[:, m], h, on_vector)
+        turned = {}
 
-        def make_y(t, h):
-            m = slice((t % 2) * P, (t % 2 + 1) * P)
-            project(y[t], w1_cd[t // 2][:, m], w1_sc[t // 2][:, m], h, False)
+        def add_turned(src, t, opens=False, closes=False):
+            u, k = divmod(t, 2)
+            for b0 in range(0, nA // P, 2):
+                if opens:
+                    turned[u, b0] = turn.tile([P, 2, 2, P], F32, name="turned")
+                for b in range(2):
+                    cols = slice((b0 + b) * P, (b0 + b + 1) * P)
+                    nc.tensor.matmul(
+                        turned[u, b0][:, b, k, :], lhsT=src[t][:, cols], rhs=ident[:],
+                        is_transpose=True, start=(opens and b == 0), stop=(closes and b == 1),
+                    )
 
-        edges, rounded, z_cd, z_sc = {}, {}, {}, {}
+        def round_turned(u):
+            for b0 in range(0, nA // P, 2):
+                nc.scalar.activation(
+                    out=z_t[:, b0 : b0 + 2, u, :].rearrange("p b (m k) -> p b m k", k=2),
+                    in_=turned[u, b0][:].rearrange("p b k m -> p b m k"),
+                    func=RELU,
+                )
+
+        edges, rounded, z, z_cd, z_sc = {}, {}, {}, {}, {}
+
+        def turn_back():
+            z[0] = keep.tile([P, PACK * nA], BF16, name="z0", tag="z0", align_bytes=64)
+            words = z[0][:].bitcast(F32).rearrange("p (b v u) -> p b v u", v=P, u=2)
+            for b0 in range(0, nA // P, 2):
+                acc = first.tile([P, 2, 2, P], F32, name="words", tag="acc")
+                for b in range(2):
+                    for u in range(2):
+                        nc.tensor.transpose(acc[:, b, u, :], z_t[:, b0 + b, u, :].bitcast(F32), ident[:])
+                nc.scalar.copy(out=words[:, b0 : b0 + 2], in_=acc[:].rearrange("p b u v -> p b v u"))
+
+        SLOT = {(1, 0): 0, (1, 1): 1, (2, 0): 2, (2, 1): 0, (3, 0): 1, (3, 1): 2}
 
         def gather(c, t, d):
             v0, n = CHUNKS[c]
             if (c, d) not in edges:
-                edges[(c, d)] = ring.tile([P, PACK, n], F32, name="edge%d_%d" % (c, d), tag="edge%d" % d)
+                edges[(c, d)] = keep.tile([P, PACK, n], F32, name="edge%d_%d" % (c, d), tag="edge%d" % SLOT[(c, d)])
             nc.vector.tensor_tensor(
                 edges[(c, d)][:, t, :],
                 e[t][:].indirect(lists[d][:, v0 // 16 : (v0 + n) // 16]),
@@ -122,20 +179,25 @@ def tile_picked_wedgecv_relu_l_kernel(
 
         def round_edges(c, d):
             n = CHUNKS[c][1]
-            rounded[(c, d)] = keep.tile([P, PACK * n], BF16, name="round%d_%d" % (c, d), align_bytes=64)
+            if d == 0:
+                tag = {1: "z_t", 2: "z0", 3: "round3"}[c]
+                rounded[c] = keep.tile([P, 2, PACK * n], BF16, name="round%d" % c, tag=tag, align_bytes=64)
             nc.scalar.activation(
-                out=rounded[(c, d)][:].rearrange("p (c i t) -> p c t i", i=4, t=4),
+                out=rounded[c][:, d, :].rearrange("p (c i t) -> p c t i", i=4, t=4),
                 in_=edges[(c, d)][:].rearrange("p t (c i) -> p c t i", i=4),
                 func=RELU,
             )
 
         def largest(c):
             n = CHUNKS[c][1]
-            z = keep.tile([P, PACK * n], BF16, name="z%d" % c, align_bytes=64)
-            nc.vector.tensor_tensor(z[:], rounded[(c, 0)][:], rounded[(c, 1)][:], MAX)
+            z[c] = keep.tile([P, PACK * n], BF16, name="z%d" % c, align_bytes=64)
+            nc.vector.tensor_tensor(z[c][:], rounded[c][:, 0, :], rounded[c][:, 1, :], MAX)
+
+        def quantise(c):
+            n = CHUNKS[c][1]
             z_cd[c] = keep.tile([P, n], U32, name="z_cd%d" % c, align_bytes=64)
             z_sc[c] = keep.tile([P, n], U8, name="z_sc%d" % c, align_bytes=64)
-            nc.vector.quantize_mx(out=z_cd[c][:].bitcast(FP8X4), scales=z_sc[c][:], in_=z[:])
+            nc.vector.quantize_mx(out=z_cd[c][:].bitcast(FP8X4), scales=z_sc[c][:], in_=z[c][:])
 
         out_v = out.rearrange("(h p) v -> p h v", p=P)
 
@@ -143,7 +205,7 @@ def tile_picked_wedgecv_relu_l_kernel(
             v0, n = CHUNKS[c]
             res = keep.tile([P, 2, n], F32, name="res%d" % c)
             for h in range(2):
-                acc = last.tile([P, n], F32, name="acc_out")
+                acc = first.tile([P, n], F32, name="acc_out", tag="acc")
                 nc.tensor.matmul_mx(
                     out=acc[:],
                     lhsT=w3_cd[:, 2 * P * h : 2 * P * (h + 1)].bitcast(FP4X4),
@@ -156,26 +218,78 @@ def tile_picked_wedgecv_relu_l_kernel(
                 nc.scalar.copy(out=res[:, h, :], in_=acc[:])
             nc.sync.dma_start(out=out_v[:, :, v0 : v0 + n], in_=res[:])
 
-        make_e(0, 0, on_vector=True)
-        make_y(0, 0)
-        make_e(0, 1)
+        def gathers(c, d, ts=range(PACK)):
+            for t in ts:
+                gather(c, t, d)
+
+        cast(2, 0)
+        cast(2, 1)
+        quantise_w(2, 0)
+        project(2, 0, 0, on_v)
+        project(2, 0, 1)
+        quantise_w(2, 1)
+        gather_pair(0)
+        for t in (1, 2):
+            project(2, t, 0)
+            project(2, t, 1)
+        cast(1, 0)
+        cast(1, 1)
+        relu_diff(0)
+        project(2, 3, 0)
+        project(2, 3, 1)
+        quantise_w(1, 0)
+        quantise_w(1, 1)
+        gather_pair(1)
+        for h in range(2):
+            for t in range(PACK):
+                product(1, t, h)
         for t in range(PACK):
-            if t + 1 < PACK:
-                make_e(t + 1, 0)
-                make_e(t + 1, 1)
-                make_y(t + 1, 0)
-            gather(0, t, 0)
-            gather(0, t, 1)
-        for t in range(PACK):
-            make_y(t, 1)
-        round_edges(0, 0)
-        round_edges(0, 1)
-        for c in range(1, len(CHUNKS)):
-            for d in range(2):
-                for t in range(PACK):
-                    gather(c, t, d)
-                round_edges(c, d)
-            largest(c - 1)
-            finish(c - 1)
-        largest(len(CHUNKS) - 1)
-        finish(len(CHUNKS) - 1)
+            bring(1, t, 0)
+        add_turned(g, 0, opens=True)
+        add_turned(y, 0)
+        add_turned(gain, 0)
+        add_turned(g, 1)
+        add_turned(y, 1)
+        relu_diff(1)
+        add_turned(gain, 1, closes=True)
+        gather_pair(2)
+        bring(1, 0, 1)
+        bring(1, 1, 1)
+        gather_pair(3)
+        relu_diff(2)
+        add_turned(y, 2, opens=True)
+        add_turned(y, 3)
+        add_turned(g, 2)
+        add_turned(gain, 2)
+        add_turned(g, 3)
+        bring(1, 2, 1)
+        bring(1, 3, 1)
+        round_turned(0)
+        relu_diff(3, parts=2)
+        add_turned(gain, 3, closes=True)
+        round_turned(1)
+        turn_back()
+        gathers(1, 0)
+        round_edges(1, 0)
+        gathers(1, 1)
+        round_edges(1, 1)
+        gathers(2, 0)
+        quantise(0)
+        finish(0)
+        round_edges(2, 0)
+        gathers(2, 1)
+        round_edges(2, 1)
+        largest(1)
+        gathers(3, 0, range(1))
+        quantise(1)
+        gathers(3, 0, range(1, PACK))
+        finish(1)
+        round_edges(3, 0)
+        gathers(3, 1)
+        round_edges(3, 1)
+        largest(2)
+        quantise(2)
+        finish(2)
+        largest(3)
+        quantise(3)
+        finish(3)

@@ -65,7 +65,7 @@ def tile_picked_wedgecv_relu_l_kernel(
             w_bf[w, u] = keep.tile([P, 2 * H], BF16, name="w%d_bf%d" % (w, u), align_bytes=64)
             dst = w_bf[w, u][:].rearrange("p (t m j) -> p m j t", t=2, j=4)
             src = w_raw[w][:].rearrange("p j (m t) -> p m j t", t=4)[:, :, :, 2 * u : 2 * u + 2]
-            if u == 0:
+            if u == 0 or w == 1:
                 nc.vector.tensor_copy(out=dst, in_=src)
             else:
                 nc.scalar.activation(out=dst, in_=src, func=COPY)
@@ -103,21 +103,38 @@ def tile_picked_wedgecv_relu_l_kernel(
             product(w, t, h)
             bring(w, t, h, copy)
 
+        def first_e():
+            for q in range(4):
+                cols = slice(q * 256, (q + 1) * 256)
+                acc = first.tile([P, 256], F32, name="acc", tag="acc")
+                nc.tensor.matmul_mx(
+                    out=acc[:],
+                    lhsT=w_cd[2, 0][:, :P].bitcast(FP8X4),
+                    lhsT_scale=w_sc[2, 0][:, :P],
+                    rhs=x_cd[:, cols].bitcast(FP8X4),
+                    rhs_scale=x_sc[:, cols],
+                    start=True,
+                    stop=True,
+                )
+                (on_s, on_v)[q % 2](out=e[0][:, cols], in_=acc[:])
+
         nA = CHUNKS[0][1]
-        g, diff = {}, {}
+        g, diff = {0: keep.tile([P, nA], F32, name="g0")[:]}, {}
         gain = {}
         z_t = keep.tile([P, nA // P, 2, 2 * P], BF16, name="z_t", tag="z_t", align_bytes=64)
 
-        def gather_pair(t):
-            pieces = [slice(a, a + nA // 2) for a in (0, nA // 2)]
-            g[t] = keep.tile([P, nA], F32, name="g%d" % t, tag="w1_raw" if t == 1 else "g%d" % t)
-            diff[t] = keep.tile([P, nA], F32, name="diff%d" % t, tag="diff%d" % t)
-            for s in pieces:
-                nc.vector.tensor_copy(g[t][:, s], e[t][:].indirect(lists[0][:, s.start // 16 : s.stop // 16]))
-            for s in pieces:
-                nc.vector.tensor_tensor(
-                    diff[t][:, s], e[t][:].indirect(lists[1][:, s.start // 16 : s.stop // 16]), g[t][:, s], SUB
-                )
+        def after_casts():
+            late = keep.tile([P, PACK, nA], F32, name="late", tag="w1_raw")
+            diff[0] = late[:, 0, :]
+            for t in range(1, PACK):
+                g[t] = late[:, t, :]
+                diff[t] = keep.tile([P, nA], F32, name="diff%d" % t)[:]
+
+        def gather_first(t):
+            nc.vector.tensor_copy(g[t], e[t][:].indirect(lists[0][:, : nA // 16]))
+
+        def gather_diff(t):
+            nc.vector.tensor_tensor(diff[t], e[t][:].indirect(lists[1][:, : nA // 16]), g[t], SUB)
 
         def relu_diff(t, parts=1):
             if t < 2:
@@ -225,47 +242,49 @@ def tile_picked_wedgecv_relu_l_kernel(
         cast(2, 0)
         cast(2, 1)
         quantise_w(2, 0)
-        project(2, 0, 0, on_v)
-        project(2, 0, 1)
+        first_e()
         quantise_w(2, 1)
-        gather_pair(0)
-        for t in (1, 2):
+        gather_first(0)
+        for t in range(1, PACK):
             project(2, t, 0)
             project(2, t, 1)
         cast(1, 0)
         cast(1, 1)
-        relu_diff(0)
-        project(2, 3, 0)
-        project(2, 3, 1)
         quantise_w(1, 0)
         quantise_w(1, 1)
-        gather_pair(1)
+        after_casts()
+        gather_diff(0)
+        gather_first(1)
+        gather_first(2)
+        gather_diff(1)
+        gather_first(3)
+        gather_diff(2)
+        gather_diff(3)
         for h in range(2):
             for t in range(PACK):
                 product(1, t, h)
-        for t in range(PACK):
-            bring(1, t, 0)
+        bring(1, 0, 0)
+        bring(1, 1, 0)
+        relu_diff(0)
+        bring(1, 2, 0)
+        bring(1, 3, 0)
         add_turned(g, 0, opens=True)
         add_turned(y, 0)
         add_turned(gain, 0)
         add_turned(g, 1)
         add_turned(y, 1)
+        for t in range(PACK):
+            bring(1, t, 1)
         relu_diff(1)
         add_turned(gain, 1, closes=True)
-        gather_pair(2)
-        bring(1, 0, 1)
-        bring(1, 1, 1)
-        gather_pair(3)
-        relu_diff(2)
         add_turned(y, 2, opens=True)
         add_turned(y, 3)
         add_turned(g, 2)
-        add_turned(gain, 2)
         add_turned(g, 3)
-        bring(1, 2, 1)
-        bring(1, 3, 1)
         round_turned(0)
-        relu_diff(3, parts=2)
+        relu_diff(2)
+        add_turned(gain, 2)
+        relu_diff(3)
         add_turned(gain, 3, closes=True)
         round_turned(1)
         turn_back()

@@ -23,6 +23,7 @@ COPY = mybir.ActivationFunctionType.Copy
 P = 128
 PACK = 4
 HALF = T // 2
+SHARE = 88
 CHUNKS = ((0, 512), (512, 256), (768, 128), (896, 128))
 
 
@@ -38,18 +39,20 @@ def tile_picked_wedgecv_relu_l_kernel(
         x_sc = keep.tile([P, T], U8, name="x_sc", align_bytes=64)
         w3_sc = keep.tile([P, N], U8, name="w3_sc", align_bytes=64)
         ident = keep.tile([P, P], F32, name="ident")
-        nc.gpsimd.memset(x_sc[:].bitcast(U32), 0)
+        nc.vector.memset(x_sc[:].bitcast(U32), 0)
         nc.gpsimd.memset(w3_sc[:].bitcast(U32), 0)
         make_identity(nc, ident[:])
 
         w2_raw = keep.tile([P, PACK, H], F32, name="w2_raw")
         w1_raw = keep.tile([P, PACK, H], F32, name="w1_raw", tag="w1_raw")
-        x_cd = keep.tile([P, T], U32, name="x_cd", align_bytes=64)
+        x_cd = [keep.tile([P, HALF], U32, name="x_cd%d" % h, align_bytes=64) for h in range(2)]
         lists = [keep.tile([P, T // 16], U16, name="list%d" % d) for d in range(2)]
         nc.sync.dma_start(out=w2_raw[:], in_=w2.rearrange("(p j) c -> p j c", j=PACK))
         for r in range(4):
             nc.sync.dma_start(out=x_sc[r:P:32, :].bitcast(I32), in_=x_scales[0][r:16:4, :].bitcast(I32))
-        nc.sync.dma_start(out=x_cd[:].bitcast(I32), in_=x_words[0].rearrange("p n r -> p (n r)").bitcast(I32))
+        x_src = x_words[0].rearrange("p n r -> p (n r)").bitcast(I32)
+        for h in range(2):
+            nc.sync.dma_start(out=x_cd[h][:].bitcast(I32), in_=x_src[:, h * HALF : (h + 1) * HALF])
         nc.sync.dma_start(lists[0][:], pos1)
         nc.sync.dma_start(lists[1][:], pos2)
         nc.sync.dma_start(out=w1_raw[:], in_=w1.rearrange("(p j) c -> p j c", j=PACK))
@@ -65,15 +68,22 @@ def tile_picked_wedgecv_relu_l_kernel(
             w_bf[w, u] = keep.tile([P, 2 * H], BF16, name="w%d_bf%d" % (w, u), align_bytes=64)
             dst = w_bf[w, u][:].rearrange("p (t m j) -> p m j t", t=2, j=4)
             src = w_raw[w][:].rearrange("p j (m t) -> p m j t", t=4)[:, :, :, 2 * u : 2 * u + 2]
-            if u == 0 or w == 1:
-                nc.vector.tensor_copy(out=dst, in_=src)
+            if u == 0 and w == 2:
+                nc.vector.tensor_copy(out=dst[:, :SHARE], in_=src[:, :SHARE])
+                nc.scalar.activation(out=dst[:, SHARE:], in_=src[:, SHARE:], func=COPY)
             else:
                 nc.scalar.activation(out=dst, in_=src, func=COPY)
 
         def quantise_w(w, u):
             w_cd[w, u] = keep.tile([P, 2 * P], U32, name="w%d_cd%d" % (w, u), tag="w%d_cd%d" % (w, u), align_bytes=64)
             w_sc[w, u] = keep.tile([P, 2 * P], U8, name="w%d_sc%d" % (w, u), align_bytes=64)
-            nc.vector.quantize_mx(out=w_cd[w, u][:].bitcast(FP8X4), scales=w_sc[w, u][:], in_=w_bf[w, u][:])
+            step = P if (w, u) == (2, 0) else 2 * P
+            for a in range(0, 2 * P, step):
+                nc.vector.quantize_mx(
+                    out=w_cd[w, u][:, a : a + step].bitcast(FP8X4),
+                    scales=w_sc[w, u][:, a : a + step],
+                    in_=w_bf[w, u][:, PACK * a : PACK * (a + step)],
+                )
 
         e = [keep.tile([P, T], F32, name="e%d" % t) for t in range(PACK)]
         y = [keep.tile([P, T], F32, name="y%d" % t) for t in range(PACK)]
@@ -89,7 +99,7 @@ def tile_picked_wedgecv_relu_l_kernel(
                 out=acc[:],
                 lhsT=w_cd[w, t // 2][:, m].bitcast(FP8X4),
                 lhsT_scale=w_sc[w, t // 2][:, m],
-                rhs=x_cd[:, cols].bitcast(FP8X4),
+                rhs=x_cd[h][:].bitcast(FP8X4),
                 rhs_scale=x_sc[:, cols],
                 start=True,
                 stop=True,
@@ -111,7 +121,7 @@ def tile_picked_wedgecv_relu_l_kernel(
                     out=acc[:],
                     lhsT=w_cd[2, 0][:, :P].bitcast(FP8X4),
                     lhsT_scale=w_sc[2, 0][:, :P],
-                    rhs=x_cd[:, cols].bitcast(FP8X4),
+                    rhs=x_cd[q // 2][:, (q % 2) * 256 : (q % 2 + 1) * 256].bitcast(FP8X4),
                     rhs_scale=x_sc[:, cols],
                     start=True,
                     stop=True,
@@ -119,33 +129,33 @@ def tile_picked_wedgecv_relu_l_kernel(
                 (on_s, on_v)[q % 2](out=e[0][:, cols], in_=acc[:])
 
         nA = CHUNKS[0][1]
-        g, diff = {0: keep.tile([P, nA], F32, name="g0")[:]}, {}
+        g, diff = {}, {}
         gain = {}
         z_t = keep.tile([P, nA // P, 2, 2 * P], BF16, name="z_t", tag="z_t", align_bytes=64)
 
-        def after_casts():
-            late = keep.tile([P, PACK, nA], F32, name="late", tag="w1_raw")
-            diff[0] = late[:, 0, :]
-            for t in range(1, PACK):
-                g[t] = late[:, t, :]
-                diff[t] = keep.tile([P, nA], F32, name="diff%d" % t)[:]
-
-        def gather_first(t):
-            nc.vector.tensor_copy(g[t], e[t][:].indirect(lists[0][:, : nA // 16]))
-
-        def gather_diff(t):
-            nc.vector.tensor_tensor(diff[t], e[t][:].indirect(lists[1][:, : nA // 16]), g[t], SUB)
-
-        def relu_diff(t, parts=1):
+        def gather_first(t, parts=1):
             if t < 2:
-                gain[t] = keep.tile([P, nA], F32, name="gain%d" % t, tag=("gain0", "w2_cd1")[t], align_bytes=64)[:]
+                g[t] = keep.tile([P, nA], F32, name="g%d" % t)[:]
             elif t == 2:
-                gain[t] = keep.tile([P, nA], F32, name="gain2", tag="w1_cd1", align_bytes=64)[:]
-            else:
-                gain[t] = keep.tile([P, nA], F32, name="gain3", tag="w1_raw")[:]
+                both = keep.tile([P, 2, nA], F32, name="g23", tag="w1_raw")
+                g[2], g[3] = both[:, 0, :], both[:, 1, :]
             for a in range(0, nA, nA // parts):
-                s = slice(a, a + nA // parts)
-                nc.scalar.activation(out=gain[t][:, s], in_=diff[t][:, s], func=RELU)
+                b = a + nA // parts
+                nc.vector.tensor_copy(g[t][:, a:b], e[t][:].indirect(lists[0][:, a // 16 : b // 16]))
+
+        def gather_diff(t, parts=1):
+            diff[t] = keep.tile([P, nA], F32, name="diff%d" % t)[:]
+            for a in range(0, nA, nA // parts):
+                b = a + nA // parts
+                nc.vector.tensor_tensor(diff[t][:, a:b], e[t][:].indirect(lists[1][:, a // 16 : b // 16]), g[t][:, a:b], SUB)
+
+        def relu_diff(t):
+            if t < 2:
+                gain[t] = keep.tile([P, nA], F32, name="gain%d" % t)[:]
+            elif t == 2:
+                both = keep.tile([P, 2, nA], F32, name="gain23", tag="w1_cd1", align_bytes=64)
+                gain[2], gain[3] = both[:, 0, :], both[:, 1, :]
+            nc.scalar.activation(out=gain[t], in_=diff[t], func=RELU)
 
         turned = {}
 
@@ -244,48 +254,49 @@ def tile_picked_wedgecv_relu_l_kernel(
         quantise_w(2, 0)
         first_e()
         quantise_w(2, 1)
-        gather_first(0)
-        for t in range(1, PACK):
-            project(2, t, 0)
-            project(2, t, 1)
+        gather_first(0, parts=2)
+        gather_diff(0, parts=2)
+        project(2, 1, 0)
+        project(2, 1, 1)
         cast(1, 0)
         cast(1, 1)
         quantise_w(1, 0)
         quantise_w(1, 1)
-        after_casts()
-        gather_diff(0)
-        gather_first(1)
+        gather_first(1, parts=2)
+        gather_diff(1, parts=2)
+        for t in (3, 2):
+            project(2, t, 0)
+            project(2, t, 1)
         gather_first(2)
-        gather_diff(1)
         gather_first(3)
         gather_diff(2)
         gather_diff(3)
-        for h in range(2):
+        for h in (1, 0):
             for t in range(PACK):
                 product(1, t, h)
+        for t in range(PACK):
+            bring(1, t, 1)
+        relu_diff(0)
         bring(1, 0, 0)
         bring(1, 1, 0)
-        relu_diff(0)
+        relu_diff(1)
         bring(1, 2, 0)
         bring(1, 3, 0)
         add_turned(g, 0, opens=True)
-        add_turned(y, 0)
-        add_turned(gain, 0)
         add_turned(g, 1)
+        add_turned(gain, 0)
+        add_turned(y, 0)
         add_turned(y, 1)
-        for t in range(PACK):
-            bring(1, t, 1)
-        relu_diff(1)
         add_turned(gain, 1, closes=True)
-        add_turned(y, 2, opens=True)
-        add_turned(y, 3)
-        add_turned(g, 2)
+        add_turned(g, 2, opens=True)
         add_turned(g, 3)
-        round_turned(0)
+        add_turned(y, 2)
+        add_turned(y, 3)
         relu_diff(2)
         add_turned(gain, 2)
         relu_diff(3)
         add_turned(gain, 3, closes=True)
+        round_turned(0)
         round_turned(1)
         turn_back()
         gathers(1, 0)

@@ -22,9 +22,11 @@ COPY = mybir.ActivationFunctionType.Copy
 
 P = 128
 PACK = 4
+STRIPE = 16
 HALF = T // 2
-SHARE = 88
-CHUNKS = ((0, 512), (512, 256), (768, 128), (896, 128))
+QUARTER = T // 4
+VECTOR_SHARE = 88
+TURNED, SECOND, THIRD, LAST, LATE = (0, 512), (512, 256), (768, 128), (896, 128), (768, 256)
 
 
 def tile_picked_wedgecv_relu_l_kernel(
@@ -33,8 +35,8 @@ def tile_picked_wedgecv_relu_l_kernel(
     nc = tc.nc
     with ExitStack() as ctx:
         keep = ctx.enter_context(tc.tile_pool(name="keep", bufs=1))
-        first = ctx.enter_context(tc.psum_pool(name="first", bufs=4))
-        turn = ctx.enter_context(tc.psum_pool(name="turn", bufs=4))
+        ring = ctx.enter_context(tc.psum_pool(name="ring", bufs=4))
+        sums = ctx.enter_context(tc.psum_pool(name="sums", bufs=4))
 
         x_sc = keep.tile([P, T], U8, name="x_sc", align_bytes=64)
         w3_sc = keep.tile([P, N], U8, name="w3_sc", align_bytes=64)
@@ -46,7 +48,7 @@ def tile_picked_wedgecv_relu_l_kernel(
         w2_raw = keep.tile([P, PACK, H], F32, name="w2_raw")
         w1_raw = keep.tile([P, PACK, H], F32, name="w1_raw", tag="w1_raw")
         x_cd = [keep.tile([P, HALF], U32, name="x_cd%d" % h, align_bytes=64) for h in range(2)]
-        lists = [keep.tile([P, T // 16], U16, name="list%d" % d) for d in range(2)]
+        lists = [keep.tile([P, T // STRIPE], U16, name="list%d" % d) for d in range(2)]
         nc.sync.dma_start(out=w2_raw[:], in_=w2.rearrange("(p j) c -> p j c", j=PACK))
         for r in range(4):
             nc.sync.dma_start(out=x_sc[r:P:32, :].bitcast(I32), in_=x_scales[0][r:16:4, :].bitcast(I32))
@@ -64,20 +66,17 @@ def tile_picked_wedgecv_relu_l_kernel(
         w_raw = {1: w1_raw, 2: w2_raw}
         w_bf, w_cd, w_sc = {}, {}, {}
 
-        def cast(w, u):
+        def cast(w, u, on_vector=0):
             w_bf[w, u] = keep.tile([P, 2 * H], BF16, name="w%d_bf%d" % (w, u), align_bytes=64)
-            dst = w_bf[w, u][:].rearrange("p (t m j) -> p m j t", t=2, j=4)
-            src = w_raw[w][:].rearrange("p j (m t) -> p m j t", t=4)[:, :, :, 2 * u : 2 * u + 2]
-            if u == 0 and w == 2:
-                nc.vector.tensor_copy(out=dst[:, :SHARE], in_=src[:, :SHARE])
-                nc.scalar.activation(out=dst[:, SHARE:], in_=src[:, SHARE:], func=COPY)
-            else:
-                nc.scalar.activation(out=dst, in_=src, func=COPY)
+            dst = w_bf[w, u][:].rearrange("p (s m j) -> p m j s", s=2, j=PACK)
+            src = w_raw[w][:].rearrange("p j (m t) -> p m j t", t=PACK)[:, :, :, 2 * u : 2 * u + 2]
+            if on_vector:
+                nc.vector.tensor_copy(out=dst[:, :on_vector], in_=src[:, :on_vector])
+            nc.scalar.activation(out=dst[:, on_vector:], in_=src[:, on_vector:], func=COPY)
 
-        def quantise_w(w, u):
+        def quantise_w(w, u, step=2 * P):
             w_cd[w, u] = keep.tile([P, 2 * P], U32, name="w%d_cd%d" % (w, u), tag="w%d_cd%d" % (w, u), align_bytes=64)
             w_sc[w, u] = keep.tile([P, 2 * P], U8, name="w%d_sc%d" % (w, u), align_bytes=64)
-            step = P if (w, u) == (2, 0) else 2 * P
             for a in range(0, 2 * P, step):
                 nc.vector.quantize_mx(
                     out=w_cd[w, u][:, a : a + step].bitcast(FP8X4),
@@ -87,201 +86,169 @@ def tile_picked_wedgecv_relu_l_kernel(
 
         e = [keep.tile([P, T], F32, name="e%d" % t) for t in range(PACK)]
         y = [keep.tile([P, T], F32, name="y%d" % t) for t in range(PACK)]
-        on_s, on_v = nc.scalar.copy, nc.vector.tensor_copy
 
-        banks = {}
-
-        def product(w, t, h):
-            cols = slice(h * HALF, (h + 1) * HALF)
+        def product(w, t, v0, n):
             m = slice((t % 2) * P, (t % 2 + 1) * P)
-            acc = first.tile([P, HALF], F32, name="acc", tag="acc")
+            acc = ring.tile([P, n], F32, name="acc", tag="acc")
             nc.tensor.matmul_mx(
                 out=acc[:],
                 lhsT=w_cd[w, t // 2][:, m].bitcast(FP8X4),
                 lhsT_scale=w_sc[w, t // 2][:, m],
-                rhs=x_cd[h][:].bitcast(FP8X4),
-                rhs_scale=x_sc[:, cols],
+                rhs=x_cd[v0 // HALF][:, v0 % HALF : v0 % HALF + n].bitcast(FP8X4),
+                rhs_scale=x_sc[:, v0 : v0 + n],
                 start=True,
                 stop=True,
             )
-            banks[w, t, h] = acc
+            return acc
 
-        def bring(w, t, h, copy=on_s):
-            copy(out=(y if w == 1 else e)[t][:, h * HALF : (h + 1) * HALF], in_=banks[w, t, h][:])
+        def make_e(t, n=HALF, copies=(nc.scalar.copy,)):
+            for q, v0 in enumerate(range(0, T, n)):
+                acc = product(2, t, v0, n)
+                copies[q % len(copies)](out=e[t][:, v0 : v0 + n], in_=acc[:])
 
-        def project(w, t, h, copy=on_s):
-            product(w, t, h)
-            bring(w, t, h, copy)
+        y_bank = {}
 
-        def first_e():
-            for q in range(4):
-                cols = slice(q * 256, (q + 1) * 256)
-                acc = first.tile([P, 256], F32, name="acc", tag="acc")
-                nc.tensor.matmul_mx(
-                    out=acc[:],
-                    lhsT=w_cd[2, 0][:, :P].bitcast(FP8X4),
-                    lhsT_scale=w_sc[2, 0][:, :P],
-                    rhs=x_cd[q // 2][:, (q % 2) * 256 : (q % 2 + 1) * 256].bitcast(FP8X4),
-                    rhs_scale=x_sc[:, cols],
-                    start=True,
-                    stop=True,
-                )
-                (on_s, on_v)[q % 2](out=e[0][:, cols], in_=acc[:])
+        def bring_y(t, h):
+            nc.scalar.copy(out=y[t][:, h * HALF : (h + 1) * HALF], in_=y_bank[t, h][:])
 
-        nA = CHUNKS[0][1]
-        g, diff = {}, {}
-        gain = {}
-        z_t = keep.tile([P, nA // P, 2, 2 * P], BF16, name="z_t", tag="z_t", align_bytes=64)
+        def looked_up(t, d, v0, n):
+            return e[t][:].indirect(lists[d][:, v0 // STRIPE : (v0 + n) // STRIPE])
 
-        def gather_first(t, parts=1):
-            if t < 2:
-                g[t] = keep.tile([P, nA], F32, name="g%d" % t)[:]
-            elif t == 2:
-                both = keep.tile([P, 2, nA], F32, name="g23", tag="w1_raw")
-                g[2], g[3] = both[:, 0, :], both[:, 1, :]
-            for a in range(0, nA, nA // parts):
-                b = a + nA // parts
-                nc.vector.tensor_copy(g[t][:, a:b], e[t][:].indirect(lists[0][:, a // 16 : b // 16]))
+        g, diff, gain, turned = {}, {}, {}, {}
+        z_t = keep.tile([P, HALF // P, 2, 2 * P], BF16, name="z_t", tag="z_t", align_bytes=64)
 
-        def gather_diff(t, parts=1):
-            diff[t] = keep.tile([P, nA], F32, name="diff%d" % t)[:]
-            for a in range(0, nA, nA // parts):
-                b = a + nA // parts
-                nc.vector.tensor_tensor(diff[t][:, a:b], e[t][:].indirect(lists[1][:, a // 16 : b // 16]), g[t][:, a:b], SUB)
+        def gather_first(t, n=HALF):
+            for v0 in range(0, HALF, n):
+                nc.vector.tensor_copy(g[t][:, v0 : v0 + n], looked_up(t, 0, v0, n))
+
+        def gather_diff(t, n=HALF):
+            diff[t] = keep.tile([P, HALF], F32, name="diff%d" % t)[:]
+            for v0 in range(0, HALF, n):
+                nc.vector.tensor_tensor(diff[t][:, v0 : v0 + n], looked_up(t, 1, v0, n), g[t][:, v0 : v0 + n], SUB)
+
+        def gather_in_halves(t):
+            g[t] = keep.tile([P, HALF], F32, name="g%d" % t)[:]
+            gather_first(t, QUARTER)
+            gather_diff(t, QUARTER)
 
         def relu_diff(t):
-            if t < 2:
-                gain[t] = keep.tile([P, nA], F32, name="gain%d" % t)[:]
-            elif t == 2:
-                both = keep.tile([P, 2, nA], F32, name="gain23", tag="w1_cd1", align_bytes=64)
-                gain[2], gain[3] = both[:, 0, :], both[:, 1, :]
             nc.scalar.activation(out=gain[t], in_=diff[t], func=RELU)
 
-        turned = {}
-
         def add_turned(src, t, opens=False, closes=False):
-            u, k = divmod(t, 2)
-            for b0 in range(0, nA // P, 2):
+            u, s = divmod(t, 2)
+            for b0 in range(0, HALF // P, 2):
                 if opens:
-                    turned[u, b0] = turn.tile([P, 2, 2, P], F32, name="turned")
+                    turned[u, b0] = sums.tile([P, 2, 2, P], F32, name="turned")
                 for b in range(2):
                     cols = slice((b0 + b) * P, (b0 + b + 1) * P)
                     nc.tensor.matmul(
-                        turned[u, b0][:, b, k, :], lhsT=src[t][:, cols], rhs=ident[:],
-                        is_transpose=True, start=(opens and b == 0), stop=(closes and b == 1),
+                        turned[u, b0][:, b, s, :],
+                        lhsT=src[t][:, cols],
+                        rhs=ident[:],
+                        is_transpose=True,
+                        start=(opens and b == 0),
+                        stop=(closes and b == 1),
                     )
 
         def round_turned(u):
-            for b0 in range(0, nA // P, 2):
+            for b0 in range(0, HALF // P, 2):
                 nc.scalar.activation(
-                    out=z_t[:, b0 : b0 + 2, u, :].rearrange("p b (m k) -> p b m k", k=2),
-                    in_=turned[u, b0][:].rearrange("p b k m -> p b m k"),
+                    out=z_t[:, b0 : b0 + 2, u, :].rearrange("v b (p s) -> v b p s", s=2),
+                    in_=turned[u, b0][:].rearrange("v b s p -> v b p s"),
                     func=RELU,
                 )
 
-        edges, rounded, z, z_cd, z_sc = {}, {}, {}, {}, {}
+        z, z_cd, z_sc = {}, {}, {}
 
         def turn_back():
-            z[0] = keep.tile([P, PACK * nA], BF16, name="z0", tag="z0", align_bytes=64)
-            words = z[0][:].bitcast(F32).rearrange("p (b v u) -> p b v u", v=P, u=2)
-            for b0 in range(0, nA // P, 2):
-                acc = first.tile([P, 2, 2, P], F32, name="words", tag="acc")
+            z[TURNED] = keep.tile([P, PACK * HALF], BF16, name="z_turned", tag="z_turned", align_bytes=64)
+            words = z[TURNED][:].bitcast(F32).rearrange("p (b v u) -> p b v u", v=P, u=2)
+            for b0 in range(0, HALF // P, 2):
+                acc = ring.tile([P, 2, 2, P], F32, name="words", tag="acc")
                 for b in range(2):
                     for u in range(2):
                         nc.tensor.transpose(acc[:, b, u, :], z_t[:, b0 + b, u, :].bitcast(F32), ident[:])
                 nc.scalar.copy(out=words[:, b0 : b0 + 2], in_=acc[:].rearrange("p b u v -> p b v u"))
 
-        SLOT = {(1, 0): 0, (1, 1): 1, (2, 0): 2, (2, 1): 0, (3, 0): 1, (3, 1): 2}
+        def edge_tile(span, d, tag):
+            return keep.tile([P, PACK, span[1]], F32, name="edge%d_%d" % (span[0], d), tag=tag)
 
-        def gather(c, t, d):
-            v0, n = CHUNKS[c]
-            if (c, d) not in edges:
-                edges[(c, d)] = keep.tile([P, PACK, n], F32, name="edge%d_%d" % (c, d), tag="edge%d" % SLOT[(c, d)])
-            nc.vector.tensor_tensor(
-                edges[(c, d)][:, t, :],
-                e[t][:].indirect(lists[d][:, v0 // 16 : (v0 + n) // 16]),
-                y[t][:, v0 : v0 + n],
-                ADD,
-            )
+        def gather_edges(edges, span, d, tiles=range(PACK)):
+            v0, n = span
+            for t in tiles:
+                nc.vector.tensor_tensor(edges[:, t, :], looked_up(t, d, v0, n), y[t][:, v0 : v0 + n], ADD)
 
-        def round_edges(c, d):
-            n = CHUNKS[c][1]
-            if d == 0:
-                tag = {1: "z_t", 2: "z0", 3: "round3"}[c]
-                rounded[c] = keep.tile([P, 2, PACK * n], BF16, name="round%d" % c, tag=tag, align_bytes=64)
+        def round_edges(dst, edges):
             nc.scalar.activation(
-                out=rounded[c][:, d, :].rearrange("p (c i t) -> p c t i", i=4, t=4),
-                in_=edges[(c, d)][:].rearrange("p t (c i) -> p c t i", i=4),
+                out=dst.rearrange("p (c i t) -> p c t i", i=4, t=PACK),
+                in_=edges[:].rearrange("p t (c i) -> p c t i", i=4),
                 func=RELU,
             )
 
-        def largest(c):
-            n = CHUNKS[c][1]
-            z[c] = keep.tile([P, PACK * n], BF16, name="z%d" % c, align_bytes=64)
-            nc.vector.tensor_tensor(z[c][:], rounded[c][:, 0, :], rounded[c][:, 1, :], MAX)
+        def largest(span, a, b):
+            z[span] = keep.tile([P, PACK * span[1]], BF16, name="z%d" % span[0], align_bytes=64)
+            nc.vector.tensor_tensor(z[span][:], a, b, MAX)
 
-        def quantise(c):
-            n = CHUNKS[c][1]
-            z_cd[c] = keep.tile([P, n], U32, name="z_cd%d" % c, align_bytes=64)
-            z_sc[c] = keep.tile([P, n], U8, name="z_sc%d" % c, align_bytes=64)
-            nc.vector.quantize_mx(out=z_cd[c][:].bitcast(FP8X4), scales=z_sc[c][:], in_=z[c][:])
+        def quantise_z(span):
+            z_cd[span] = keep.tile([P, span[1]], U32, name="z_cd%d" % span[0], align_bytes=64)
+            z_sc[span] = keep.tile([P, span[1]], U8, name="z_sc%d" % span[0], align_bytes=64)
+            nc.vector.quantize_mx(out=z_cd[span][:].bitcast(FP8X4), scales=z_sc[span][:], in_=z[span][:])
 
-        out_v = out.rearrange("(h p) v -> p h v", p=P)
+        out_v = out.rearrange("(a p) v -> p a v", p=P)
 
-        def finish(c):
-            v0, n = CHUNKS[c]
-            res = keep.tile([P, 2, n], F32, name="res%d" % c)
-            for h in range(2):
-                acc = first.tile([P, n], F32, name="acc_out", tag="acc")
+        def finish(span):
+            v0, n = span
+            res = keep.tile([P, N // P, n], F32, name="res%d" % v0)
+            for a in range(N // P):
+                acc = ring.tile([P, n], F32, name="acc_out", tag="acc")
                 nc.tensor.matmul_mx(
                     out=acc[:],
-                    lhsT=w3_cd[:, 2 * P * h : 2 * P * (h + 1)].bitcast(FP4X4),
-                    lhsT_scale=w3_sc[:, P * h : P * (h + 1)],
-                    rhs=z_cd[c][:].bitcast(FP8X4),
-                    rhs_scale=z_sc[c][:],
+                    lhsT=w3_cd[:, 2 * P * a : 2 * P * (a + 1)].bitcast(FP4X4),
+                    lhsT_scale=w3_sc[:, P * a : P * (a + 1)],
+                    rhs=z_cd[span][:].bitcast(FP8X4),
+                    rhs_scale=z_sc[span][:],
                     start=True,
                     stop=True,
                 )
-                nc.scalar.copy(out=res[:, h, :], in_=acc[:])
+                nc.scalar.copy(out=res[:, a, :], in_=acc[:])
             nc.sync.dma_start(out=out_v[:, :, v0 : v0 + n], in_=res[:])
 
-        def gathers(c, d, ts=range(PACK)):
-            for t in ts:
-                gather(c, t, d)
-
-        cast(2, 0)
+        cast(2, 0, on_vector=VECTOR_SHARE)
         cast(2, 1)
-        quantise_w(2, 0)
-        first_e()
+        quantise_w(2, 0, step=P)
+        make_e(0, QUARTER, (nc.scalar.copy, nc.vector.tensor_copy))
         quantise_w(2, 1)
-        gather_first(0, parts=2)
-        gather_diff(0, parts=2)
-        project(2, 1, 0)
-        project(2, 1, 1)
+
+        gather_in_halves(0)
+        make_e(1)
         cast(1, 0)
         cast(1, 1)
         quantise_w(1, 0)
         quantise_w(1, 1)
-        gather_first(1, parts=2)
-        gather_diff(1, parts=2)
-        for t in (3, 2):
-            project(2, t, 0)
-            project(2, t, 1)
+        gather_in_halves(1)
+        make_e(3)
+        make_e(2)
+        g_late = keep.tile([P, 2, HALF], F32, name="g_late", tag="w1_raw")
+        g[2], g[3] = g_late[:, 0, :], g_late[:, 1, :]
         gather_first(2)
         gather_first(3)
         gather_diff(2)
         gather_diff(3)
+
         for h in (1, 0):
             for t in range(PACK):
-                product(1, t, h)
+                y_bank[t, h] = product(1, t, h * HALF, HALF)
         for t in range(PACK):
-            bring(1, t, 1)
+            bring_y(t, 1)
+        gain[0] = keep.tile([P, HALF], F32, name="gain0")[:]
         relu_diff(0)
-        bring(1, 0, 0)
-        bring(1, 1, 0)
+        bring_y(0, 0)
+        bring_y(1, 0)
+        gain[1] = keep.tile([P, HALF], F32, name="gain1")[:]
         relu_diff(1)
-        bring(1, 2, 0)
-        bring(1, 3, 0)
+        bring_y(2, 0)
+        bring_y(3, 0)
+
         add_turned(g, 0, opens=True)
         add_turned(g, 1)
         add_turned(gain, 0)
@@ -292,34 +259,46 @@ def tile_picked_wedgecv_relu_l_kernel(
         add_turned(g, 3)
         add_turned(y, 2)
         add_turned(y, 3)
+        gain_late = keep.tile([P, 2, HALF], F32, name="gain_late", tag="w1_cd1", align_bytes=64)
+        gain[2], gain[3] = gain_late[:, 0, :], gain_late[:, 1, :]
         relu_diff(2)
         add_turned(gain, 2)
         relu_diff(3)
         add_turned(gain, 3, closes=True)
         round_turned(0)
         round_turned(1)
+
+        second0 = edge_tile(SECOND, 0, "edge_a")
+        gather_edges(second0, SECOND, 0)
+        second0_bf = keep.tile([P, PACK * SECOND[1]], BF16, name="second0_bf", tag="w1_cd1", align_bytes=64)
+        round_edges(second0_bf[:], second0)
         turn_back()
-        gathers(1, 0)
-        round_edges(1, 0)
-        gathers(1, 1)
-        round_edges(1, 1)
-        gathers(2, 0)
-        quantise(0)
-        finish(0)
-        round_edges(2, 0)
-        gathers(2, 1)
-        round_edges(2, 1)
-        largest(1)
-        gathers(3, 0, range(1))
-        quantise(1)
-        gathers(3, 0, range(1, PACK))
-        finish(1)
-        round_edges(3, 0)
-        gathers(3, 1)
-        round_edges(3, 1)
-        largest(2)
-        quantise(2)
-        finish(2)
-        largest(3)
-        quantise(3)
-        finish(3)
+        second1 = edge_tile(SECOND, 1, "edge_b")
+        gather_edges(second1, SECOND, 1)
+        late0 = edge_tile(LATE, 0, "edge_c")
+        gather_edges(late0, LATE, 0)
+        quantise_z(TURNED)
+        second1_bf = keep.tile([P, PACK * SECOND[1]], BF16, name="second1_bf", tag="z_t", align_bytes=64)
+        late_bf = keep.tile([P, 3, PACK * THIRD[1]], BF16, name="late_bf", tag="z_turned", align_bytes=64)
+        last1_bf = keep.tile([P, PACK * LAST[1]], BF16, name="last1_bf", align_bytes=64)
+        round_edges(second1_bf[:], second1)
+        round_edges(late_bf[:, 0:2, :].rearrange("p a b -> p (a b)"), late0)
+        finish(TURNED)
+
+        largest(SECOND, second0_bf[:], second1_bf[:])
+        third1 = edge_tile(THIRD, 1, "edge_b")
+        gather_edges(third1, THIRD, 1, range(1))
+        quantise_z(SECOND)
+        gather_edges(third1, THIRD, 1, range(1, PACK))
+        finish(SECOND)
+        round_edges(late_bf[:, 2, :], third1)
+        last1 = edge_tile(LAST, 1, "edge_c")
+        gather_edges(last1, LAST, 1)
+        round_edges(last1_bf[:], last1)
+
+        largest(THIRD, late_bf[:, 0, :], late_bf[:, 2, :])
+        quantise_z(THIRD)
+        finish(THIRD)
+        largest(LAST, late_bf[:, 1, :], last1_bf[:])
+        quantise_z(LAST)
+        finish(LAST)

@@ -101,8 +101,8 @@ def tile_picked_wedgecv_relu_l_kernel(
             )
             return acc
 
-        def make_e(t, n=HALF, copies=(nc.scalar.copy,)):
-            for q, v0 in enumerate(range(0, T, n)):
+        def make_e(t, n=HALF, copies=(nc.scalar.copy,), start=0, stop=T):
+            for q, v0 in enumerate(range(start, stop, n)):
                 acc = product(2, t, v0, n)
                 copies[q % len(copies)](out=e[t][:, v0 : v0 + n], in_=acc[:])
 
@@ -196,21 +196,33 @@ def tile_picked_wedgecv_relu_l_kernel(
 
         out_v = out.rearrange("(a p) v -> p a v", p=P)
 
+        def last_product(span, a, acc):
+            nc.tensor.matmul_mx(
+                out=acc,
+                lhsT=w3_cd[:, 2 * P * a : 2 * P * (a + 1)].bitcast(FP4X4),
+                lhsT_scale=w3_sc[:, P * a : P * (a + 1)],
+                rhs=z_cd[span][:].bitcast(FP8X4),
+                rhs_scale=z_sc[span][:],
+                start=True,
+                stop=True,
+            )
+
+        def finish_by_rows(span, copies):
+            v0, n = span
+            for a in range(N // P):
+                res = keep.tile([P, n], F32, name="res%d_%d" % (v0, a))
+                acc = ring.tile([P, n], F32, name="acc_out", tag="acc")
+                last_product(span, a, acc[:])
+                copies[a](out=res[:], in_=acc[:])
+                nc.sync.dma_start(out=out_v[:, a, v0 : v0 + n], in_=res[:])
+
         def finish(span):
             v0, n = span
             res = keep.tile([P, N // P, n], F32, name="res%d" % v0)
+            acc = ring.tile([P, N // P, n], F32, name="acc_out", tag="acc")
             for a in range(N // P):
-                acc = ring.tile([P, n], F32, name="acc_out", tag="acc")
-                nc.tensor.matmul_mx(
-                    out=acc[:],
-                    lhsT=w3_cd[:, 2 * P * a : 2 * P * (a + 1)].bitcast(FP4X4),
-                    lhsT_scale=w3_sc[:, P * a : P * (a + 1)],
-                    rhs=z_cd[span][:].bitcast(FP8X4),
-                    rhs_scale=z_sc[span][:],
-                    start=True,
-                    stop=True,
-                )
-                nc.scalar.copy(out=res[:, a, :], in_=acc[:])
+                last_product(span, a, acc[:, a, :])
+            nc.scalar.copy(out=res[:], in_=acc[:])
             nc.sync.dma_start(out=out_v[:, :, v0 : v0 + n], in_=res[:])
 
         cast(2, 0, on_vector=VECTOR_SHARE)
@@ -221,13 +233,14 @@ def tile_picked_wedgecv_relu_l_kernel(
 
         gather_in_halves(0)
         make_e(1)
+        make_e(2)
+        make_e(3, stop=HALF)
         cast(1, 0)
         cast(1, 1)
         quantise_w(1, 0)
         quantise_w(1, 1)
         gather_in_halves(1)
-        make_e(3)
-        make_e(2)
+        make_e(3, start=HALF)
         g_late = keep.tile([P, 2, HALF], F32, name="g_late", tag="w1_raw")
         g[2], g[3] = g_late[:, 0, :], g_late[:, 1, :]
         gather_first(2)
@@ -283,7 +296,7 @@ def tile_picked_wedgecv_relu_l_kernel(
         last1_bf = keep.tile([P, PACK * LAST[1]], BF16, name="last1_bf", align_bytes=64)
         round_edges(second1_bf[:], second1)
         round_edges(late_bf[:, 0:2, :].rearrange("p a b -> p (a b)"), late0)
-        finish(TURNED)
+        finish_by_rows(TURNED, (nc.scalar.copy, nc.scalar.copy))
 
         largest(SECOND, second0_bf[:], second1_bf[:])
         third1 = edge_tile(THIRD, 1, "edge_b")
@@ -301,4 +314,4 @@ def tile_picked_wedgecv_relu_l_kernel(
         finish(THIRD)
         largest(LAST, late_bf[:, 1, :], last1_bf[:])
         quantise_z(LAST)
-        finish(LAST)
+        finish_by_rows(LAST, (nc.scalar.copy, nc.vector.tensor_copy))

@@ -56,8 +56,8 @@ def tile_picked_wedgecv_relu_l_kernel(
         for h in range(2):
             nc.sync.dma_start(out=x_cd[h][:].bitcast(I32), in_=x_src[:, h * HALF : (h + 1) * HALF])
         nc.sync.dma_start(lists[0][:], pos1)
-        nc.sync.dma_start(lists[1][:], pos2)
         nc.sync.dma_start(out=w1_raw[:], in_=w1.rearrange("(p j) c -> p j c", j=PACK))
+        nc.sync.dma_start(lists[1][:], pos2)
         w3_cd = keep.tile([P, 2 * N], U8, name="w3_cd", align_bytes=64)
         nc.sync.dma_start(out=w3_cd[:].bitcast(I32), in_=w3_words[0].bitcast(I32))
         for r in range(4):
@@ -117,19 +117,12 @@ def tile_picked_wedgecv_relu_l_kernel(
         g, diff, gain, turned = {}, {}, {}, {}
         z_t = keep.tile([P, HALF // P, 2, 2 * P], BF16, name="z_t", tag="z_t", align_bytes=64)
 
-        def gather_first(t, n=HALF):
-            for v0 in range(0, HALF, n):
-                nc.vector.tensor_copy(g[t][:, v0 : v0 + n], looked_up(t, 0, v0, n))
+        def gather_first(t):
+            nc.vector.tensor_copy(g[t], looked_up(t, 0, 0, HALF))
 
-        def gather_diff(t, n=HALF):
+        def gather_diff(t):
             diff[t] = keep.tile([P, HALF], F32, name="diff%d" % t)[:]
-            for v0 in range(0, HALF, n):
-                nc.vector.tensor_tensor(diff[t][:, v0 : v0 + n], looked_up(t, 1, v0, n), g[t][:, v0 : v0 + n], SUB)
-
-        def gather_in_halves(t):
-            g[t] = keep.tile([P, HALF], F32, name="g%d" % t)[:]
-            gather_first(t, QUARTER)
-            gather_diff(t, QUARTER)
+            nc.vector.tensor_tensor(diff[t], looked_up(t, 1, 0, HALF), g[t], SUB)
 
         def relu_diff(t):
             nc.scalar.activation(out=gain[t], in_=diff[t], func=RELU)
@@ -231,15 +224,19 @@ def tile_picked_wedgecv_relu_l_kernel(
         make_e(0, QUARTER, (nc.scalar.copy, nc.vector.tensor_copy))
         quantise_w(2, 1)
 
-        gather_in_halves(0)
+        for t in range(2):
+            g[t] = keep.tile([P, HALF], F32, name="g%d" % t)[:]
+        gather_first(0)
         make_e(1)
+        gather_first(1)
+        gather_diff(0)
+        gather_diff(1)
         make_e(2)
         make_e(3, stop=HALF)
         cast(1, 0)
         cast(1, 1)
         quantise_w(1, 0)
         quantise_w(1, 1)
-        gather_in_halves(1)
         make_e(3, start=HALF)
         g_late = keep.tile([P, 2, HALF], F32, name="g_late", tag="w1_raw")
         g[2], g[3] = g_late[:, 0, :], g_late[:, 1, :]

@@ -26,6 +26,7 @@ STRIPE = 16
 HALF = T // 2
 QUARTER = T // 4
 VECTOR_SHARE = 88
+VECTOR_SHARE_W1 = 64
 TURNED, SECOND, THIRD, LAST, LATE = (0, 512), (512, 256), (768, 128), (896, 128), (768, 256)
 
 
@@ -229,11 +230,11 @@ def tile_picked_wedgecv_relu_l_kernel(
         gather_first(0)
         make_e(1)
         gather_first(1)
-        gather_diff(0)
-        gather_diff(1)
         make_e(2)
         make_e(3, stop=HALF)
-        cast(1, 0)
+        cast(1, 0, on_vector=VECTOR_SHARE_W1)
+        gather_diff(0)
+        gather_diff(1)
         cast(1, 1)
         quantise_w(1, 0)
         quantise_w(1, 1)

@@ -16,6 +16,7 @@ FP8X4 = mybir.dt.float8_e4m3fn_x4
 FP4X4 = mybir.dt.float4_e2m1fn_x4
 ADD = mybir.AluOpType.add
 SUB = mybir.AluOpType.subtract
+MULT = mybir.AluOpType.mult
 MAX = mybir.AluOpType.max
 RELU = mybir.ActivationFunctionType.Relu
 COPY = mybir.ActivationFunctionType.Copy
@@ -26,7 +27,6 @@ STRIPE = 16
 HALF = T // 2
 QUARTER = T // 4
 VECTOR_SHARE = 88
-VECTOR_SHARE_W1 = 64
 TURNED, SECOND, THIRD, LAST, LATE = (0, 512), (512, 256), (768, 128), (896, 128), (768, 256)
 
 
@@ -36,8 +36,10 @@ def tile_picked_wedgecv_relu_l_kernel(
     nc = tc.nc
     with ExitStack() as ctx:
         keep = ctx.enter_context(tc.tile_pool(name="keep", bufs=1))
-        ring = ctx.enter_context(tc.psum_pool(name="ring", bufs=4))
-        sums = ctx.enter_context(tc.psum_pool(name="sums", bufs=4))
+        psum = ctx.enter_context(tc.psum_pool(name="psum", bufs=1))
+
+        def bank(b, *shape):
+            return psum.tile([P, *shape], F32, name="bank%d" % b, tag="bank%d" % b)
 
         x_sc = keep.tile([P, T], U8, name="x_sc", align_bytes=64)
         w3_sc = keep.tile([P, N], U8, name="w3_sc", align_bytes=64)
@@ -47,8 +49,8 @@ def tile_picked_wedgecv_relu_l_kernel(
         make_identity(nc, ident[:])
 
         w2_raw = keep.tile([P, PACK, H], F32, name="w2_raw")
-        w1_raw = keep.tile([P, PACK, H], F32, name="w1_raw", tag="w1_raw")
-        x_cd = [keep.tile([P, HALF], U32, name="x_cd%d" % h, align_bytes=64) for h in range(2)]
+        w1_raw = [keep.tile([P, PACK, H // 2], F32, name="w1_raw%d" % h, tag="w1_raw%d" % h) for h in range(2)]
+        x_cd = [keep.tile([P, HALF], U32, name="x_cd%d" % h, tag="x_cd%d" % h, align_bytes=64) for h in range(2)]
         lists = [keep.tile([P, T // STRIPE], U16, name="list%d" % d) for d in range(2)]
         nc.sync.dma_start(out=w2_raw[:], in_=w2.rearrange("(p j) c -> p j c", j=PACK))
         for r in range(4):
@@ -57,40 +59,55 @@ def tile_picked_wedgecv_relu_l_kernel(
         for h in range(2):
             nc.sync.dma_start(out=x_cd[h][:].bitcast(I32), in_=x_src[:, h * HALF : (h + 1) * HALF])
         nc.sync.dma_start(lists[0][:], pos1)
-        nc.sync.dma_start(out=w1_raw[:], in_=w1.rearrange("(p j) c -> p j c", j=PACK))
+        for h in range(2):
+            cols = slice(h * H // 2, (h + 1) * H // 2)
+            nc.sync.dma_start(out=w1_raw[h][:], in_=w1.rearrange("(p j) c -> p j c", j=PACK)[:, :, cols])
         nc.sync.dma_start(lists[1][:], pos2)
         w3_cd = keep.tile([P, 2 * N], U8, name="w3_cd", align_bytes=64)
         nc.sync.dma_start(out=w3_cd[:].bitcast(I32), in_=w3_words[0].bitcast(I32))
         for r in range(4):
             nc.sync.dma_start(out=w3_sc[r:P:32, :].bitcast(I32), in_=w3_scales[0][r:16:4, :].bitcast(I32))
 
-        w_raw = {1: w1_raw, 2: w2_raw}
         w_bf, w_cd, w_sc = {}, {}, {}
 
-        def cast(w, u, on_vector=0):
-            w_bf[w, u] = keep.tile([P, 2 * H], BF16, name="w%d_bf%d" % (w, u), align_bytes=64)
-            dst = w_bf[w, u][:].rearrange("p (s m j) -> p m j s", s=2, j=PACK)
-            src = w_raw[w][:].rearrange("p j (m t) -> p m j t", t=PACK)[:, :, :, 2 * u : 2 * u + 2]
+        def cast_w2(u, on_vector=0):
+            w_bf[2, u] = keep.tile([P, 2 * H], BF16, name="w2_bf%d" % u, align_bytes=64)[:]
+            dst = w_bf[2, u].rearrange("p (s m j) -> p m j s", s=2, j=PACK)
+            src = w2_raw[:].rearrange("p j (m t) -> p m j t", t=PACK)[:, :, :, 2 * u : 2 * u + 2]
             if on_vector:
                 nc.vector.tensor_copy(out=dst[:, :on_vector], in_=src[:, :on_vector])
             nc.scalar.activation(out=dst[:, on_vector:], in_=src[:, on_vector:], func=COPY)
 
-        def quantise_w(w, u, step=2 * P):
-            w_cd[w, u] = keep.tile([P, 2 * P], U32, name="w%d_cd%d" % (w, u), tag="w%d_cd%d" % (w, u), align_bytes=64)
-            w_sc[w, u] = keep.tile([P, 2 * P], U8, name="w%d_sc%d" % (w, u), align_bytes=64)
+        w1_bf = keep.tile([P, PACK * H], BF16, name="w1_bf", align_bytes=64)
+
+        def cast_w1(h):
+            dst = w1_bf[:].rearrange("p (t m j) -> p m t j", t=PACK, j=PACK)[:, h * P // 2 : (h + 1) * P // 2]
+            src = w1_raw[h][:].rearrange("p j (m t) -> p m t j", t=PACK)
+            nc.gpsimd.tensor_scalar(dst, src, 1.0, 0.0, MULT, ADD)
+
+        def quantise_w2(u, step=2 * P):
+            w_cd[2, u] = keep.tile([P, 2 * P], U32, name="w2_cd%d" % u, tag="w2_cd%d" % u, align_bytes=64)[:]
+            w_sc[2, u] = keep.tile([P, 2 * P], U8, name="w2_sc%d" % u, tag="w2_sc%d" % u, align_bytes=64)[:]
             for a in range(0, 2 * P, step):
                 nc.vector.quantize_mx(
-                    out=w_cd[w, u][:, a : a + step].bitcast(FP8X4),
-                    scales=w_sc[w, u][:, a : a + step],
-                    in_=w_bf[w, u][:, PACK * a : PACK * (a + step)],
+                    out=w_cd[2, u][:, a : a + step].bitcast(FP8X4),
+                    scales=w_sc[2, u][:, a : a + step],
+                    in_=w_bf[2, u][:, PACK * a : PACK * (a + step)],
                 )
+
+        def quantise_w1():
+            codes = keep.tile([P, H], U32, name="w1_cd", tag="w1_cd", align_bytes=64)
+            scales = keep.tile([P, H], U8, name="w1_sc", tag="w1_sc", align_bytes=64)
+            nc.vector.quantize_mx(out=codes[:].bitcast(FP8X4), scales=scales[:], in_=w1_bf[:])
+            for u in range(2):
+                w_cd[1, u], w_sc[1, u] = codes[:, 2 * P * u : 2 * P * (u + 1)], scales[:, 2 * P * u : 2 * P * (u + 1)]
 
         e = [keep.tile([P, T], F32, name="e%d" % t) for t in range(PACK)]
         y = [keep.tile([P, T], F32, name="y%d" % t) for t in range(PACK)]
 
-        def product(w, t, v0, n):
+        def product(w, t, v0, n, b):
             m = slice((t % 2) * P, (t % 2 + 1) * P)
-            acc = ring.tile([P, n], F32, name="acc", tag="acc")
+            acc = bank(b, n)
             nc.tensor.matmul_mx(
                 out=acc[:],
                 lhsT=w_cd[w, t // 2][:, m].bitcast(FP8X4),
@@ -102,9 +119,9 @@ def tile_picked_wedgecv_relu_l_kernel(
             )
             return acc
 
-        def make_e(t, n=HALF, copies=(nc.scalar.copy,), start=0, stop=T):
-            for q, v0 in enumerate(range(start, stop, n)):
-                acc = product(2, t, v0, n)
+        def make_e(t, first_bank, n=HALF, copies=(nc.scalar.copy,)):
+            for q, v0 in enumerate(range(0, T, n)):
+                acc = product(2, t, v0, n, first_bank + q)
                 copies[q % len(copies)](out=e[t][:, v0 : v0 + n], in_=acc[:])
 
         y_bank = {}
@@ -122,7 +139,6 @@ def tile_picked_wedgecv_relu_l_kernel(
             nc.vector.tensor_copy(g[t], looked_up(t, 0, 0, HALF))
 
         def gather_diff(t):
-            diff[t] = keep.tile([P, HALF], F32, name="diff%d" % t)[:]
             nc.vector.tensor_tensor(diff[t], looked_up(t, 1, 0, HALF), g[t], SUB)
 
         def relu_diff(t):
@@ -132,7 +148,7 @@ def tile_picked_wedgecv_relu_l_kernel(
             u, s = divmod(t, 2)
             for b0 in range(0, HALF // P, 2):
                 if opens:
-                    turned[u, b0] = sums.tile([P, 2, 2, P], F32, name="turned")
+                    turned[u, b0] = bank(4 + 2 * u + b0 // 2, 2, 2, P)
                 for b in range(2):
                     cols = slice((b0 + b) * P, (b0 + b + 1) * P)
                     nc.tensor.matmul(
@@ -158,14 +174,14 @@ def tile_picked_wedgecv_relu_l_kernel(
             z[TURNED] = keep.tile([P, PACK * HALF], BF16, name="z_turned", tag="z_turned", align_bytes=64)
             words = z[TURNED][:].bitcast(F32).rearrange("p (b v u) -> p b v u", v=P, u=2)
             for b0 in range(0, HALF // P, 2):
-                acc = ring.tile([P, 2, 2, P], F32, name="words", tag="acc")
+                acc = bank(2 + b0 // 2, 2, 2, P)
                 for b in range(2):
                     for u in range(2):
                         nc.tensor.transpose(acc[:, b, u, :], z_t[:, b0 + b, u, :].bitcast(F32), ident[:])
                 nc.scalar.copy(out=words[:, b0 : b0 + 2], in_=acc[:].rearrange("p b u v -> p b v u"))
 
         def edge_tile(span, d, tag):
-            return keep.tile([P, PACK, span[1]], F32, name="edge%d_%d" % (span[0], d), tag=tag)
+            return keep.tile([P, PACK, span[1]], F32, name="edge%d_%d" % (span[0], d), tag=tag, align_bytes=64)
 
         def gather_edges(edges, span, d, tiles=range(PACK)):
             v0, n = span
@@ -175,7 +191,7 @@ def tile_picked_wedgecv_relu_l_kernel(
         def round_edges(dst, edges):
             nc.scalar.activation(
                 out=dst.rearrange("p (c i t) -> p c t i", i=4, t=PACK),
-                in_=edges[:].rearrange("p t (c i) -> p c t i", i=4),
+                in_=edges.rearrange("p t (c i) -> p c t i", i=4),
                 func=RELU,
             )
 
@@ -201,76 +217,62 @@ def tile_picked_wedgecv_relu_l_kernel(
                 stop=True,
             )
 
-        def finish_by_rows(span, copies):
+        def finish_by_rows(span, first_bank, copies):
             v0, n = span
             for a in range(N // P):
                 res = keep.tile([P, n], F32, name="res%d_%d" % (v0, a))
-                acc = ring.tile([P, n], F32, name="acc_out", tag="acc")
+                acc = bank(first_bank + a, n)
                 last_product(span, a, acc[:])
                 copies[a](out=res[:], in_=acc[:])
                 nc.sync.dma_start(out=out_v[:, a, v0 : v0 + n], in_=res[:])
 
-        def finish(span):
+        def finish(span, b):
             v0, n = span
             res = keep.tile([P, N // P, n], F32, name="res%d" % v0)
-            acc = ring.tile([P, N // P, n], F32, name="acc_out", tag="acc")
+            acc = bank(b, N // P, n)
             for a in range(N // P):
                 last_product(span, a, acc[:, a, :])
             nc.scalar.copy(out=res[:], in_=acc[:])
             nc.sync.dma_start(out=out_v[:, :, v0 : v0 + n], in_=res[:])
 
-        cast(2, 0, on_vector=VECTOR_SHARE)
-        cast(2, 1)
-        quantise_w(2, 0, step=P)
-        make_e(0, QUARTER, (nc.scalar.copy, nc.vector.tensor_copy))
-        quantise_w(2, 1)
+        cast_w2(0, on_vector=VECTOR_SHARE)
+        cast_w2(1)
+        quantise_w2(0, step=P)
+        make_e(0, 0, QUARTER, (nc.scalar.copy, nc.vector.tensor_copy))
+        quantise_w2(1)
 
-        for t in range(2):
+        for t in range(PACK - 1):
             g[t] = keep.tile([P, HALF], F32, name="g%d" % t)[:]
-        gather_first(0)
-        make_e(1)
-        gather_first(1)
-        make_e(2)
-        make_e(3, stop=HALF)
-        cast(1, 0, on_vector=VECTOR_SHARE_W1)
-        gather_diff(0)
-        gather_diff(1)
-        cast(1, 1)
-        quantise_w(1, 0)
-        quantise_w(1, 1)
-        make_e(3, start=HALF)
-        g_late = keep.tile([P, 2, HALF], F32, name="g_late", tag="w1_raw")
-        g[2], g[3] = g_late[:, 0, :], g_late[:, 1, :]
-        gather_first(2)
+            gather_first(t)
+            make_e(t + 1, (0, 4, 2)[t])
+        cast_w1(0)
+        cast_w1(1)
+        quantise_w1()
+        late = keep.tile([P, 1 + PACK, HALF], F32, name="late", tag="w1_raw1")
+        g[3] = late[:, PACK, :]
         gather_first(3)
-        gather_diff(2)
-        gather_diff(3)
-
-        for h in (1, 0):
-            for t in range(PACK):
-                y_bank[t, h] = product(1, t, h * HALF, HALF)
         for t in range(PACK):
-            bring_y(t, 1)
-        gain[0] = keep.tile([P, HALF], F32, name="gain0")[:]
-        relu_diff(0)
-        bring_y(0, 0)
-        bring_y(1, 0)
-        gain[1] = keep.tile([P, HALF], F32, name="gain1")[:]
-        relu_diff(1)
-        bring_y(2, 0)
-        bring_y(3, 0)
+            diff[t] = late[:, t, :]
+            gather_diff(t)
+
+        for q, (u, h, s) in enumerate((u, h, s) for u in range(2) for h in (1, 0) for s in range(2)):
+            y_bank[2 * u + s, h] = product(1, 2 * u + s, h * HALF, HALF, q % 4)
+            bring_y(2 * u + s, h)
+        for t in range(2):
+            gain[t] = keep.tile([P, HALF], F32, name="gain%d" % t)[:]
+            relu_diff(t)
 
         add_turned(g, 0, opens=True)
         add_turned(g, 1)
-        add_turned(gain, 0)
         add_turned(y, 0)
         add_turned(y, 1)
-        add_turned(gain, 1, closes=True)
         add_turned(g, 2, opens=True)
         add_turned(g, 3)
         add_turned(y, 2)
         add_turned(y, 3)
-        gain_late = keep.tile([P, 2, HALF], F32, name="gain_late", tag="w1_cd1", align_bytes=64)
+        add_turned(gain, 0)
+        add_turned(gain, 1, closes=True)
+        gain_late = keep.tile([P, 2, HALF], F32, name="gain_late", tag="w1_cd", align_bytes=64)
         gain[2], gain[3] = gain_late[:, 0, :], gain_late[:, 1, :]
         relu_diff(2)
         add_turned(gain, 2)
@@ -281,35 +283,36 @@ def tile_picked_wedgecv_relu_l_kernel(
 
         second0 = edge_tile(SECOND, 0, "edge_a")
         gather_edges(second0, SECOND, 0)
-        second0_bf = keep.tile([P, PACK * SECOND[1]], BF16, name="second0_bf", tag="w1_cd1", align_bytes=64)
-        round_edges(second0_bf[:], second0)
+        second0_bf = keep.tile([P, PACK * SECOND[1]], BF16, name="second0_bf", tag="w1_cd", align_bytes=64)
+        round_edges(second0_bf[:], second0[:])
         turn_back()
-        second1 = edge_tile(SECOND, 1, "edge_b")
+        second1 = edge_tile(SECOND, 1, "w1_sc")
         gather_edges(second1, SECOND, 1)
-        late0 = edge_tile(LATE, 0, "edge_c")
+        late0 = edge_tile(LATE, 0, "x_cd1")
         gather_edges(late0, LATE, 0)
         quantise_z(TURNED)
-        second1_bf = keep.tile([P, PACK * SECOND[1]], BF16, name="second1_bf", tag="z_t", align_bytes=64)
-        late_bf = keep.tile([P, 3, PACK * THIRD[1]], BF16, name="late_bf", tag="z_turned", align_bytes=64)
+        rounded = keep.tile([P, PACK * HALF], BF16, name="rounded", tag="z_t", align_bytes=64)
+        second1_bf, late0_bf = rounded[:, : PACK * SECOND[1]], rounded[:, PACK * SECOND[1] :]
+        third1_bf = keep.tile([P, PACK * THIRD[1]], BF16, name="third1_bf", align_bytes=64)
         last1_bf = keep.tile([P, PACK * LAST[1]], BF16, name="last1_bf", align_bytes=64)
-        round_edges(second1_bf[:], second1)
-        round_edges(late_bf[:, 0:2, :].rearrange("p a b -> p (a b)"), late0)
-        finish_by_rows(TURNED, (nc.scalar.copy, nc.scalar.copy))
+        round_edges(second1_bf, second1[:])
+        round_edges(late0_bf, late0[:])
+        finish_by_rows(TURNED, 0, (nc.scalar.copy, nc.scalar.copy))
 
-        largest(SECOND, second0_bf[:], second1_bf[:])
-        third1 = edge_tile(THIRD, 1, "edge_b")
+        largest(SECOND, second0_bf[:], second1_bf)
+        third1 = edge_tile(THIRD, 1, "w1_sc")
         gather_edges(third1, THIRD, 1, range(1))
         quantise_z(SECOND)
         gather_edges(third1, THIRD, 1, range(1, PACK))
-        finish(SECOND)
-        round_edges(late_bf[:, 2, :], third1)
-        last1 = edge_tile(LAST, 1, "edge_c")
+        finish(SECOND, 4)
+        round_edges(third1_bf[:], third1[:])
+        last1 = edge_tile(LAST, 1, "x_cd1")
         gather_edges(last1, LAST, 1)
-        round_edges(last1_bf[:], last1)
+        round_edges(last1_bf[:], last1[:])
 
-        largest(THIRD, late_bf[:, 0, :], late_bf[:, 2, :])
+        largest(THIRD, late0_bf[:, : PACK * THIRD[1]], third1_bf[:])
         quantise_z(THIRD)
-        finish(THIRD)
-        largest(LAST, late_bf[:, 1, :], last1_bf[:])
+        finish(THIRD, 5)
+        largest(LAST, late0_bf[:, PACK * THIRD[1] :], last1_bf[:])
         quantise_z(LAST)
-        finish_by_rows(LAST, (nc.scalar.copy, nc.vector.tensor_copy))
+        finish_by_rows(LAST, 6, (nc.scalar.copy, nc.vector.tensor_copy))

@@ -195,12 +195,12 @@ def tile_picked_wedgecv_relu_l_kernel(
                 func=RELU,
             )
 
-        def largest(span, a, b):
-            z[span] = keep.tile([P, PACK * span[1]], BF16, name="z%d" % span[0], align_bytes=64)
+        def largest(span, a, b, tag):
+            z[span] = keep.tile([P, PACK * span[1]], BF16, name="z%d" % span[0], tag=tag, align_bytes=64)
             nc.vector.tensor_tensor(z[span][:], a, b, MAX)
 
-        def quantise_z(span):
-            z_cd[span] = keep.tile([P, span[1]], U32, name="z_cd%d" % span[0], align_bytes=64)
+        def quantise_z(span, tag=None):
+            z_cd[span] = keep.tile([P, span[1]], U32, name="z_cd%d" % span[0], tag=tag or "z_cd%d" % span[0], align_bytes=64)
             z_sc[span] = keep.tile([P, span[1]], U8, name="z_sc%d" % span[0], align_bytes=64)
             nc.vector.quantize_mx(out=z_cd[span][:].bitcast(FP8X4), scales=z_sc[span][:], in_=z[span][:])
 
@@ -217,14 +217,13 @@ def tile_picked_wedgecv_relu_l_kernel(
                 stop=True,
             )
 
-        def finish_by_rows(span, first_bank, copies):
+        def finish_rows(span, a, b, copy):
             v0, n = span
-            for a in range(N // P):
-                res = keep.tile([P, n], F32, name="res%d_%d" % (v0, a))
-                acc = bank(first_bank + a, n)
-                last_product(span, a, acc[:])
-                copies[a](out=res[:], in_=acc[:])
-                nc.sync.dma_start(out=out_v[:, a, v0 : v0 + n], in_=res[:])
+            res = keep.tile([P, n], F32, name="res%d_%d" % (v0, a))
+            acc = bank(b, n)
+            last_product(span, a, acc[:])
+            copy(out=res[:], in_=acc[:])
+            nc.sync.dma_start(out=out_v[:, a, v0 : v0 + n], in_=res[:])
 
         def finish(span, b):
             v0, n = span
@@ -297,22 +296,24 @@ def tile_picked_wedgecv_relu_l_kernel(
         last1_bf = keep.tile([P, PACK * LAST[1]], BF16, name="last1_bf", align_bytes=64)
         round_edges(second1_bf, second1[:])
         round_edges(late0_bf, late0[:])
-        finish_by_rows(TURNED, 0, (nc.scalar.copy, nc.scalar.copy))
+        finish_rows(TURNED, 0, 0, nc.scalar.copy)
 
-        largest(SECOND, second0_bf[:], second1_bf)
         third1 = edge_tile(THIRD, 1, "w1_sc")
-        gather_edges(third1, THIRD, 1, range(1))
-        quantise_z(SECOND)
-        gather_edges(third1, THIRD, 1, range(1, PACK))
-        finish(SECOND, 4)
+        gather_edges(third1, THIRD, 1)
         round_edges(third1_bf[:], third1[:])
+        finish_rows(TURNED, 1, 1, nc.scalar.copy)
         last1 = edge_tile(LAST, 1, "x_cd1")
         gather_edges(last1, LAST, 1)
         round_edges(last1_bf[:], last1[:])
 
-        largest(THIRD, late0_bf[:, : PACK * THIRD[1]], third1_bf[:])
-        quantise_z(THIRD)
-        finish(THIRD, 5)
-        largest(LAST, late0_bf[:, PACK * THIRD[1] :], last1_bf[:])
+        largest(SECOND, second0_bf[:], second1_bf, "w1_sc")
+        largest(THIRD, late0_bf[:, : PACK * THIRD[1]], third1_bf[:], "z_third")
+        quantise_z(SECOND)
+        largest(LAST, late0_bf[:, PACK * THIRD[1] :], last1_bf[:], "z_last")
+        quantise_z(THIRD, "x_cd1")
         quantise_z(LAST)
-        finish_by_rows(LAST, 6, (nc.scalar.copy, nc.vector.tensor_copy))
+        finish_rows(SECOND, 0, 4, nc.scalar.copy)
+        finish_rows(SECOND, 1, 5, nc.scalar.copy)
+        finish(THIRD, 2)
+        finish_rows(LAST, 0, 6, nc.vector.tensor_copy)
+        finish_rows(LAST, 1, 7, nc.vector.tensor_copy)

@@ -25,7 +25,6 @@ P = 128
 PACK = 4
 STRIPE = 16
 HALF = T // 2
-QUARTER = T // 4
 VECTOR_SHARE = 88
 TURNED, SECOND, THIRD, LAST, LATE = (0, 512), (512, 256), (768, 128), (896, 128), (768, 256)
 
@@ -119,9 +118,11 @@ def tile_picked_wedgecv_relu_l_kernel(
             )
             return acc
 
-        def make_e(t, first_bank, n=HALF, copies=(nc.scalar.copy,)):
-            for q, v0 in enumerate(range(0, T, n)):
-                acc = product(2, t, v0, n, first_bank + q)
+        def make_e(t, banks, copies=(nc.scalar.copy,), first=0):
+            n = T // len(banks)
+            for q, b in enumerate(banks):
+                v0 = (first + q * n) % T
+                acc = product(2, t, v0, n, b)
                 copies[q % len(copies)](out=e[t][:, v0 : v0 + n], in_=acc[:])
 
         y_bank = {}
@@ -237,13 +238,13 @@ def tile_picked_wedgecv_relu_l_kernel(
         cast_w2(0, on_vector=VECTOR_SHARE)
         cast_w2(1)
         quantise_w2(0, step=P)
-        make_e(0, 0, QUARTER, (nc.scalar.copy, nc.vector.tensor_copy))
+        make_e(0, (0, 1, 2, 3), (nc.scalar.copy, nc.vector.tensor_copy))
         quantise_w2(1)
 
         for t in range(PACK - 1):
             g[t] = keep.tile([P, HALF], F32, name="g%d" % t)[:]
             gather_first(t)
-            make_e(t + 1, (0, 4, 2)[t])
+            make_e(t + 1, ((4, 5, 0, 1), (2, 3), (0, 1))[t], first=HALF)
         cast_w1(0)
         cast_w1(1)
         quantise_w1()
@@ -255,7 +256,7 @@ def tile_picked_wedgecv_relu_l_kernel(
             gather_diff(t)
 
         for q, (u, h, s) in enumerate((u, h, s) for u in range(2) for h in (1, 0) for s in range(2)):
-            y_bank[2 * u + s, h] = product(1, 2 * u + s, h * HALF, HALF, q % 4)
+            y_bank[2 * u + s, h] = product(1, 2 * u + s, h * HALF, HALF, (q + 2) % 4)
             bring_y(2 * u + s, h)
         for t in range(2):
             gain[t] = keep.tile([P, HALF], F32, name="gain%d" % t)[:]

@@ -244,7 +244,7 @@ def tile_picked_wedgecv_relu_l_kernel(
         for t in range(PACK - 1):
             g[t] = keep.tile([P, HALF], F32, name="g%d" % t)[:]
             gather_first(t)
-            make_e(t + 1, ((4, 5, 0, 1), (2, 3), (0, 1))[t], first=HALF)
+            make_e(t + 1, ((6, 7, 0, 1), (4, 5), (2, 3))[t], first=HALF)
         cast_w1(0)
         cast_w1(1)
         quantise_w1()
@@ -256,7 +256,7 @@ def tile_picked_wedgecv_relu_l_kernel(
             gather_diff(t)
 
         for q, (u, h, s) in enumerate((u, h, s) for u in range(2) for h in (1, 0) for s in range(2)):
-            y_bank[2 * u + s, h] = product(1, 2 * u + s, h * HALF, HALF, (q + 2) % 4)
+            y_bank[2 * u + s, h] = product(1, 2 * u + s, h * HALF, HALF, q % 4)
             bring_y(2 * u + s, h)
         for t in range(2):
             gain[t] = keep.tile([P, HALF], F32, name="gain%d" % t)[:]

@@ -42,7 +42,7 @@ def tile_picked_wedgecv_relu_l_kernel(
 
         x_sc = keep.tile([P, T], U8, name="x_sc", align_bytes=64)
         w3_sc = keep.tile([P, N], U8, name="w3_sc", align_bytes=64)
-        ident = keep.tile([P, P], F32, name="ident")
+        ident = keep.tile([P, P], F32, name="ident", tag="ident", align_bytes=64)
         nc.vector.memset(x_sc[:].bitcast(U32), 0)
         nc.gpsimd.memset(w3_sc[:].bitcast(U32), 0)
         make_identity(nc, ident[:])
@@ -97,9 +97,11 @@ def tile_picked_wedgecv_relu_l_kernel(
         def quantise_w1():
             codes = keep.tile([P, H], U32, name="w1_cd", tag="w1_cd", align_bytes=64)
             scales = keep.tile([P, H], U8, name="w1_sc", tag="w1_sc", align_bytes=64)
-            nc.vector.quantize_mx(out=codes[:].bitcast(FP8X4), scales=scales[:], in_=w1_bf[:])
             for u in range(2):
                 w_cd[1, u], w_sc[1, u] = codes[:, 2 * P * u : 2 * P * (u + 1)], scales[:, 2 * P * u : 2 * P * (u + 1)]
+                nc.vector.quantize_mx(
+                    out=w_cd[1, u].bitcast(FP8X4), scales=w_sc[1, u], in_=w1_bf[:, 2 * H * u : 2 * H * (u + 1)]
+                )
 
         e = [keep.tile([P, T], F32, name="e%d" % t) for t in range(PACK)]
         y = [keep.tile([P, T], F32, name="y%d" % t) for t in range(PACK)]
@@ -125,16 +127,10 @@ def tile_picked_wedgecv_relu_l_kernel(
                 acc = product(2, t, v0, n, b)
                 copies[q % len(copies)](out=e[t][:, v0 : v0 + n], in_=acc[:])
 
-        y_bank = {}
-
-        def bring_y(t, h):
-            nc.scalar.copy(out=y[t][:, h * HALF : (h + 1) * HALF], in_=y_bank[t, h][:])
-
         def looked_up(t, d, v0, n):
             return e[t][:].indirect(lists[d][:, v0 // STRIPE : (v0 + n) // STRIPE])
 
-        g, diff, gain, turned = {}, {}, {}, {}
-        z_t = keep.tile([P, HALF // P, 2, 2 * P], BF16, name="z_t", tag="z_t", align_bytes=64)
+        g, diff, gain, turned, z_t = {}, {}, {}, {}, {}
 
         def gather_first(t):
             nc.vector.tensor_copy(g[t], looked_up(t, 0, 0, HALF))
@@ -163,23 +159,28 @@ def tile_picked_wedgecv_relu_l_kernel(
 
         def round_turned(u):
             for b0 in range(0, HALF // P, 2):
+                name = "z_t%d%d" % (u, b0)
+                z_t[u, b0] = keep.tile([P, 2, 2 * P], BF16, name=name, tag=name, align_bytes=64)
                 nc.scalar.activation(
-                    out=z_t[:, b0 : b0 + 2, u, :].rearrange("v b (p s) -> v b p s", s=2),
+                    out=z_t[u, b0][:].rearrange("v b (p s) -> v b p s", s=2),
                     in_=turned[u, b0][:].rearrange("v b s p -> v b p s"),
                     func=RELU,
                 )
 
-        z, z_cd, z_sc = {}, {}, {}
+        z, z_cd, z_sc, back = {}, {}, {}, {}
 
-        def turn_back():
-            z[TURNED] = keep.tile([P, PACK * HALF], BF16, name="z_turned", tag="z_turned", align_bytes=64)
+        def turn_back(u):
+            for b0 in range(0, HALF // P, 2):
+                if u == 0:
+                    back[b0] = bank(2 + b0 // 2, 2, 2, P)
+                for b in range(2):
+                    nc.tensor.transpose(back[b0][:, b, u, :], z_t[u, b0][:, b, :].bitcast(F32), ident[:])
+
+        def bring_back():
+            z[TURNED] = keep.tile([P, PACK * HALF], BF16, name="z_turned", align_bytes=64)
             words = z[TURNED][:].bitcast(F32).rearrange("p (b v u) -> p b v u", v=P, u=2)
             for b0 in range(0, HALF // P, 2):
-                acc = bank(2 + b0 // 2, 2, 2, P)
-                for b in range(2):
-                    for u in range(2):
-                        nc.tensor.transpose(acc[:, b, u, :], z_t[:, b0 + b, u, :].bitcast(F32), ident[:])
-                nc.scalar.copy(out=words[:, b0 : b0 + 2], in_=acc[:].rearrange("p b u v -> p b v u"))
+                nc.scalar.copy(out=words[:, b0 : b0 + 2], in_=back[b0][:].rearrange("p b u v -> p b v u"))
 
         def edge_tile(span, d, tag):
             return keep.tile([P, PACK, span[1]], F32, name="edge%d_%d" % (span[0], d), tag=tag, align_bytes=64)
@@ -255,9 +256,11 @@ def tile_picked_wedgecv_relu_l_kernel(
             diff[t] = late[:, t, :]
             gather_diff(t)
 
-        for q, (u, h, s) in enumerate((u, h, s) for u in range(2) for h in (1, 0) for s in range(2)):
-            y_bank[2 * u + s, h] = product(1, 2 * u + s, h * HALF, HALF, q % 4)
-            bring_y(2 * u + s, h)
+        pieces = [(0, HALF, HALF // 2), (0, HALF + HALF // 2, HALF // 2)]
+        pieces.extend([(2 * u + s, h * HALF, HALF) for u in range(2) for h in (1, 0) for s in range(2)][1:])
+        for q, (t, v0, n) in enumerate(pieces):
+            acc = product(1, t, v0, n, q % 4)
+            nc.scalar.copy(out=y[t][:, v0 : v0 + n], in_=acc[:])
         for t in range(2):
             gain[t] = keep.tile([P, HALF], F32, name="gain%d" % t)[:]
             relu_diff(t)
@@ -278,25 +281,26 @@ def tile_picked_wedgecv_relu_l_kernel(
         add_turned(gain, 2)
         relu_diff(3)
         add_turned(gain, 3, closes=True)
-        round_turned(0)
-        round_turned(1)
+        for u in range(2):
+            round_turned(u)
+            turn_back(u)
+        bring_back()
 
         second0 = edge_tile(SECOND, 0, "edge_a")
         gather_edges(second0, SECOND, 0)
-        second0_bf = keep.tile([P, PACK * SECOND[1]], BF16, name="second0_bf", tag="w1_cd", align_bytes=64)
+        second0_bf = keep.tile([P, PACK * SECOND[1]], BF16, name="second0_bf", tag="z_t10", align_bytes=64)
         round_edges(second0_bf[:], second0[:])
-        turn_back()
         second1 = edge_tile(SECOND, 1, "w1_sc")
         gather_edges(second1, SECOND, 1)
+        second1_bf = keep.tile([P, PACK * SECOND[1]], BF16, name="second1_bf", tag="ident", align_bytes=64)
+        round_edges(second1_bf[:], second1[:])
         late0 = edge_tile(LATE, 0, "x_cd1")
         gather_edges(late0, LATE, 0)
         quantise_z(TURNED)
-        rounded = keep.tile([P, PACK * HALF], BF16, name="rounded", tag="z_t", align_bytes=64)
-        second1_bf, late0_bf = rounded[:, : PACK * SECOND[1]], rounded[:, PACK * SECOND[1] :]
+        late0_bf = keep.tile([P, PACK * LATE[1]], BF16, name="late0_bf", tag="z_t12", align_bytes=64)
         third1_bf = keep.tile([P, PACK * THIRD[1]], BF16, name="third1_bf", align_bytes=64)
         last1_bf = keep.tile([P, PACK * LAST[1]], BF16, name="last1_bf", align_bytes=64)
-        round_edges(second1_bf, second1[:])
-        round_edges(late0_bf, late0[:])
+        round_edges(late0_bf[:], late0[:])
         finish_rows(TURNED, 0, 0, nc.scalar.copy)
 
         third1 = edge_tile(THIRD, 1, "w1_sc")
@@ -307,7 +311,7 @@ def tile_picked_wedgecv_relu_l_kernel(
         gather_edges(last1, LAST, 1)
         round_edges(last1_bf[:], last1[:])
 
-        largest(SECOND, second0_bf[:], second1_bf, "w1_sc")
+        largest(SECOND, second0_bf[:], second1_bf[:], "w1_sc")
         largest(THIRD, late0_bf[:, : PACK * THIRD[1]], third1_bf[:], "z_third")
         quantise_z(SECOND)
         largest(LAST, late0_bf[:, PACK * THIRD[1] :], last1_bf[:], "z_last")

@@ -192,8 +192,8 @@ def tile_picked_wedgecv_relu_l_kernel(
 
         def round_edges(dst, edges):
             nc.scalar.activation(
-                out=dst.rearrange("p (c i t) -> p c t i", i=4, t=PACK),
-                in_=edges.rearrange("p t (c i) -> p c t i", i=4),
+                out=dst.rearrange("p (c i t) -> p c t i", i=2, t=PACK),
+                in_=edges.rearrange("p t (c i) -> p c t i", i=2),
                 func=RELU,
             )
 

@@ -52,11 +52,11 @@ def tile_picked_wedgecv_relu_l_kernel(
         x_cd = [keep.tile([P, HALF], U32, name="x_cd%d" % h, tag="x_cd%d" % h, align_bytes=64) for h in range(2)]
         lists = [keep.tile([P, T // STRIPE], U16, name="list%d" % d) for d in range(2)]
         nc.sync.dma_start(out=w2_raw[:], in_=w2.rearrange("(p j) c -> p j c", j=PACK))
+        x_src = x_words[0].rearrange("p n r -> p (n r)").bitcast(I32)
+        nc.sync.dma_start(out=x_cd[0][:].bitcast(I32), in_=x_src[:, :HALF])
         for r in range(4):
             nc.sync.dma_start(out=x_sc[r:P:32, :].bitcast(I32), in_=x_scales[0][r:16:4, :].bitcast(I32))
-        x_src = x_words[0].rearrange("p n r -> p (n r)").bitcast(I32)
-        for h in range(2):
-            nc.sync.dma_start(out=x_cd[h][:].bitcast(I32), in_=x_src[:, h * HALF : (h + 1) * HALF])
+        nc.sync.dma_start(out=x_cd[1][:].bitcast(I32), in_=x_src[:, HALF:])
         nc.sync.dma_start(lists[0][:], pos1)
         for h in range(2):
             cols = slice(h * H // 2, (h + 1) * H // 2)
@@ -192,8 +192,8 @@ def tile_picked_wedgecv_relu_l_kernel(
 
         def round_edges(dst, edges):
             nc.scalar.activation(
-                out=dst.rearrange("p (c i t) -> p c t i", i=2, t=PACK),
-                in_=edges.rearrange("p t (c i) -> p c t i", i=2),
+                out=dst.rearrange("p (c i t) -> p c t i", i=4, t=PACK),
+                in_=edges.rearrange("p t (c i) -> p c t i", i=4),
                 func=RELU,
             )
 

@@ -48,7 +48,9 @@ def tile_picked_wedgecv_relu_l_kernel(
         make_identity(nc, ident[:])
 
         w2_raw = keep.tile([P, PACK, H], F32, name="w2_raw")
-        w1_raw = [keep.tile([P, PACK, H // 2], F32, name="w1_raw%d" % h, tag="w1_raw%d" % h) for h in range(2)]
+        late = keep.tile([P, 3 * HALF], F32, name="late")
+        w1_first = keep.tile([P, PACK, H // 2], F32, name="w1_first")
+        w1_raw = [w1_first[:], late[:, HALF // 2 : HALF // 2 + 2 * H].rearrange("p (j c) -> p j c", j=PACK)]
         x_cd = [keep.tile([P, HALF], U32, name="x_cd%d" % h, tag="x_cd%d" % h, align_bytes=64) for h in range(2)]
         lists = [keep.tile([P, T // STRIPE], U16, name="list%d" % d) for d in range(2)]
         nc.sync.dma_start(out=w2_raw[:], in_=w2.rearrange("(p j) c -> p j c", j=PACK))
@@ -60,7 +62,7 @@ def tile_picked_wedgecv_relu_l_kernel(
         nc.sync.dma_start(lists[0][:], pos1)
         for h in range(2):
             cols = slice(h * H // 2, (h + 1) * H // 2)
-            nc.sync.dma_start(out=w1_raw[h][:], in_=w1.rearrange("(p j) c -> p j c", j=PACK)[:, :, cols])
+            nc.sync.dma_start(out=w1_raw[h], in_=w1.rearrange("(p j) c -> p j c", j=PACK)[:, :, cols])
         nc.sync.dma_start(lists[1][:], pos2)
         w3_cd = keep.tile([P, 2 * N], U8, name="w3_cd", align_bytes=64)
         nc.sync.dma_start(out=w3_cd[:].bitcast(I32), in_=w3_words[0].bitcast(I32))
@@ -77,11 +79,11 @@ def tile_picked_wedgecv_relu_l_kernel(
                 nc.vector.tensor_copy(out=dst[:, :on_vector], in_=src[:, :on_vector])
             nc.scalar.activation(out=dst[:, on_vector:], in_=src[:, on_vector:], func=COPY)
 
-        w1_bf = keep.tile([P, PACK * H], BF16, name="w1_bf", align_bytes=64)
+        w1_bf = keep.tile([P, PACK * H], BF16, name="w1_bf", tag="w1_bf", align_bytes=64)
 
         def cast_w1(h):
             dst = w1_bf[:].rearrange("p (t m j) -> p m t j", t=PACK, j=PACK)[:, h * P // 2 : (h + 1) * P // 2]
-            src = w1_raw[h][:].rearrange("p j (m t) -> p m t j", t=PACK)
+            src = w1_raw[h].rearrange("p j (m t) -> p m t j", t=PACK)
             nc.gpsimd.tensor_scalar(dst, src, 1.0, 0.0, MULT, ADD)
 
         def quantise_w2(u, step=2 * P):
@@ -132,8 +134,8 @@ def tile_picked_wedgecv_relu_l_kernel(
 
         g, diff, gain, turned, z_t = {}, {}, {}, {}, {}
 
-        def gather_first(t):
-            nc.vector.tensor_copy(g[t], looked_up(t, 0, 0, HALF))
+        def gather_first(t, v0=0, n=HALF):
+            nc.vector.tensor_copy(g[t][:, v0 : v0 + n], looked_up(t, 0, v0, n))
 
         def gather_diff(t):
             nc.vector.tensor_tensor(diff[t], looked_up(t, 1, 0, HALF), g[t], SUB)
@@ -242,18 +244,21 @@ def tile_picked_wedgecv_relu_l_kernel(
         make_e(0, (0, 1, 2, 3), (nc.scalar.copy, nc.vector.tensor_copy))
         quantise_w2(1)
 
-        for t in range(PACK - 1):
+        for t in range(2):
             g[t] = keep.tile([P, HALF], F32, name="g%d" % t)[:]
-            gather_first(t)
+        g[2], g[3], diff[0] = (late[:, q * HALF : (q + 1) * HALF] for q in range(3))
+        for t in range(PACK - 1):
+            gather_first(t, 0, HALF if t < 2 else HALF // 2)
             make_e(t + 1, ((6, 7, 0, 1), (4, 5), (2, 3))[t], first=HALF)
         cast_w1(0)
         cast_w1(1)
         quantise_w1()
-        late = keep.tile([P, 1 + PACK, HALF], F32, name="late", tag="w1_raw1")
-        g[3] = late[:, PACK, :]
+        gather_first(2, HALF // 2, HALF // 2)
         gather_first(3)
+        diffs = keep.tile([P, PACK - 1, HALF], F32, name="diffs", tag="w1_bf", align_bytes=64)
         for t in range(PACK):
-            diff[t] = late[:, t, :]
+            if t:
+                diff[t] = diffs[:, t - 1, :]
             gather_diff(t)
 
         pieces = [(0, HALF, HALF // 2), (0, HALF + HALF // 2, HALF // 2)]

@@ -289,12 +289,12 @@ def tile_picked_wedgecv_relu_l_kernel(
         for u in range(2):
             round_turned(u)
             turn_back(u)
-        bring_back()
 
         second0 = edge_tile(SECOND, 0, "edge_a")
         gather_edges(second0, SECOND, 0)
-        second0_bf = keep.tile([P, PACK * SECOND[1]], BF16, name="second0_bf", tag="z_t10", align_bytes=64)
+        second0_bf = keep.tile([P, PACK * SECOND[1]], BF16, name="second0_bf", tag="w1_cd", align_bytes=64)
         round_edges(second0_bf[:], second0[:])
+        bring_back()
         second1 = edge_tile(SECOND, 1, "w1_sc")
         gather_edges(second1, SECOND, 1)
         second1_bf = keep.tile([P, PACK * SECOND[1]], BF16, name="second1_bf", tag="ident", align_bytes=64)

@@ -72,12 +72,13 @@ def tile_picked_wedgecv_relu_l_kernel(
         w_bf, w_cd, w_sc = {}, {}, {}
 
         def cast_w2(u, on_vector=0):
-            w_bf[2, u] = keep.tile([P, 2 * H], BF16, name="w2_bf%d" % u, align_bytes=64)[:]
+            w_bf[2, u] = keep.tile([P, 2 * H], BF16, name="w2_bf%d" % u, tag="w2_bf", align_bytes=64)[:]
             dst = w_bf[2, u].rearrange("p (s m j) -> p m j s", s=2, j=PACK)
             src = w2_raw[:].rearrange("p j (m t) -> p m j t", t=PACK)[:, :, :, 2 * u : 2 * u + 2]
             if on_vector:
                 nc.vector.tensor_copy(out=dst[:, :on_vector], in_=src[:, :on_vector])
-            nc.scalar.activation(out=dst[:, on_vector:], in_=src[:, on_vector:], func=COPY)
+            if on_vector < P:
+                nc.scalar.activation(out=dst[:, on_vector:], in_=src[:, on_vector:], func=COPY)
 
         w1_bf = keep.tile([P, PACK * H], BF16, name="w1_bf", tag="w1_bf", align_bytes=64)
 
@@ -239,9 +240,9 @@ def tile_picked_wedgecv_relu_l_kernel(
             nc.sync.dma_start(out=out_v[:, :, v0 : v0 + n], in_=res[:])
 
         cast_w2(0, on_vector=VECTOR_SHARE)
-        cast_w2(1)
         quantise_w2(0, step=P)
-        make_e(0, (0, 1, 2, 3), (nc.scalar.copy, nc.vector.tensor_copy))
+        cast_w2(1, on_vector=P)
+        make_e(0, (0, 1, 2, 3), (nc.scalar.copy, nc.scalar.copy, nc.vector.tensor_copy, nc.scalar.copy))
         quantise_w2(1)
 
         for t in range(2):

@@ -26,6 +26,7 @@ PACK = 4
 STRIPE = 16
 HALF = T // 2
 VECTOR_SHARE = 88
+FREE = 384
 TURNED, SECOND, THIRD, LAST, LATE = (0, 512), (512, 256), (768, 128), (896, 128), (768, 256)
 
 
@@ -50,7 +51,7 @@ def tile_picked_wedgecv_relu_l_kernel(
         w2_raw = keep.tile([P, PACK, H], F32, name="w2_raw")
         late = keep.tile([P, 3 * HALF], F32, name="late")
         w1_first = keep.tile([P, PACK, H // 2], F32, name="w1_first")
-        w1_raw = [w1_first[:], late[:, HALF // 2 : HALF // 2 + 2 * H].rearrange("p (j c) -> p j c", j=PACK)]
+        w1_raw = [w1_first[:], late[:, FREE : FREE + 2 * H].rearrange("p (j c) -> p j c", j=PACK)]
         x_cd = [keep.tile([P, HALF], U32, name="x_cd%d" % h, tag="x_cd%d" % h, align_bytes=64) for h in range(2)]
         lists = [keep.tile([P, T // STRIPE], U16, name="list%d" % d) for d in range(2)]
         nc.sync.dma_start(out=w2_raw[:], in_=w2.rearrange("(p j) c -> p j c", j=PACK))
@@ -249,12 +250,12 @@ def tile_picked_wedgecv_relu_l_kernel(
             g[t] = keep.tile([P, HALF], F32, name="g%d" % t)[:]
         g[2], g[3], diff[0] = (late[:, q * HALF : (q + 1) * HALF] for q in range(3))
         for t in range(PACK - 1):
-            gather_first(t, 0, HALF if t < 2 else HALF // 2)
+            gather_first(t, 0, HALF if t < 2 else FREE)
             make_e(t + 1, ((6, 7, 0, 1), (4, 5), (2, 3))[t], first=HALF)
         cast_w1(0)
         cast_w1(1)
         quantise_w1()
-        gather_first(2, HALF // 2, HALF // 2)
+        gather_first(2, FREE, HALF - FREE)
         gather_first(3)
         diffs = keep.tile([P, PACK - 1, HALF], F32, name="diffs", tag="w1_bf", align_bytes=64)
         for t in range(PACK):

@@ -1,7 +1,6 @@
 from contextlib import ExitStack
 
 import concourse.mybir as mybir
-from concourse.masks import make_identity
 
 K, T, H, N = 512, 1024, 512, 256
 FLOPS = 2 * K * H * T * 2 + 2 * H * N * T
@@ -15,10 +14,8 @@ U8 = mybir.dt.uint8
 FP8X4 = mybir.dt.float8_e4m3fn_x4
 FP4X4 = mybir.dt.float4_e2m1fn_x4
 ADD = mybir.AluOpType.add
-SUB = mybir.AluOpType.subtract
 MULT = mybir.AluOpType.mult
 MAX = mybir.AluOpType.max
-RELU = mybir.ActivationFunctionType.Relu
 COPY = mybir.ActivationFunctionType.Copy
 
 P = 128
@@ -26,8 +23,7 @@ PACK = 4
 STRIPE = 16
 HALF = T // 2
 VECTOR_SHARE = 88
-FREE = 384
-TURNED, SECOND, THIRD, LAST, LATE = (0, 512), (512, 256), (768, 128), (896, 128), (768, 256)
+FIRST, SECOND, THIRD, LAST = (0, 512), (512, 256), (768, 128), (896, 128)
 
 
 def tile_picked_wedgecv_relu_l_kernel(
@@ -43,16 +39,12 @@ def tile_picked_wedgecv_relu_l_kernel(
 
         x_sc = keep.tile([P, T], U8, name="x_sc", align_bytes=64)
         w3_sc = keep.tile([P, N], U8, name="w3_sc", align_bytes=64)
-        ident = keep.tile([P, P], F32, name="ident", tag="ident", align_bytes=64)
         nc.vector.memset(x_sc[:].bitcast(U32), 0)
         nc.gpsimd.memset(w3_sc[:].bitcast(U32), 0)
-        make_identity(nc, ident[:])
 
         w2_raw = keep.tile([P, PACK, H], F32, name="w2_raw")
-        late = keep.tile([P, 3 * HALF], F32, name="late")
-        w1_first = keep.tile([P, PACK, H // 2], F32, name="w1_first")
-        w1_raw = [w1_first[:], late[:, FREE : FREE + 2 * H].rearrange("p (j c) -> p j c", j=PACK)]
-        x_cd = [keep.tile([P, HALF], U32, name="x_cd%d" % h, tag="x_cd%d" % h, align_bytes=64) for h in range(2)]
+        w1_raw = [keep.tile([P, PACK, H // 2], F32, name="w1_raw%d" % h) for h in range(2)]
+        x_cd = [keep.tile([P, HALF], U32, name="x_cd%d" % h, align_bytes=64) for h in range(2)]
         lists = [keep.tile([P, T // STRIPE], U16, name="list%d" % d) for d in range(2)]
         nc.sync.dma_start(out=w2_raw[:], in_=w2.rearrange("(p j) c -> p j c", j=PACK))
         x_src = x_words[0].rearrange("p n r -> p (n r)").bitcast(I32)
@@ -61,10 +53,10 @@ def tile_picked_wedgecv_relu_l_kernel(
             nc.sync.dma_start(out=x_sc[r:P:32, :].bitcast(I32), in_=x_scales[0][r:16:4, :].bitcast(I32))
         nc.sync.dma_start(out=x_cd[1][:].bitcast(I32), in_=x_src[:, HALF:])
         nc.sync.dma_start(lists[0][:], pos1)
+        nc.sync.dma_start(lists[1][:], pos2)
         for h in range(2):
             cols = slice(h * H // 2, (h + 1) * H // 2)
-            nc.sync.dma_start(out=w1_raw[h], in_=w1.rearrange("(p j) c -> p j c", j=PACK)[:, :, cols])
-        nc.sync.dma_start(lists[1][:], pos2)
+            nc.sync.dma_start(out=w1_raw[h][:], in_=w1.rearrange("(p j) c -> p j c", j=PACK)[:, :, cols])
         w3_cd = keep.tile([P, 2 * N], U8, name="w3_cd", align_bytes=64)
         nc.sync.dma_start(out=w3_cd[:].bitcast(I32), in_=w3_words[0].bitcast(I32))
         for r in range(4):
@@ -85,12 +77,12 @@ def tile_picked_wedgecv_relu_l_kernel(
 
         def cast_w1(h):
             dst = w1_bf[:].rearrange("p (t m j) -> p m t j", t=PACK, j=PACK)[:, h * P // 2 : (h + 1) * P // 2]
-            src = w1_raw[h].rearrange("p j (m t) -> p m t j", t=PACK)
+            src = w1_raw[h][:].rearrange("p j (m t) -> p m t j", t=PACK)
             nc.gpsimd.tensor_scalar(dst, src, 1.0, 0.0, MULT, ADD)
 
         def quantise_w2(u, step=2 * P):
-            w_cd[2, u] = keep.tile([P, 2 * P], U32, name="w2_cd%d" % u, tag="w2_cd%d" % u, align_bytes=64)[:]
-            w_sc[2, u] = keep.tile([P, 2 * P], U8, name="w2_sc%d" % u, tag="w2_sc%d" % u, align_bytes=64)[:]
+            w_cd[2, u] = keep.tile([P, 2 * P], U32, name="w2_cd%d" % u, align_bytes=64)[:]
+            w_sc[2, u] = keep.tile([P, 2 * P], U8, name="w2_sc%d" % u, align_bytes=64)[:]
             for a in range(0, 2 * P, step):
                 nc.vector.quantize_mx(
                     out=w_cd[2, u][:, a : a + step].bitcast(FP8X4),
@@ -99,22 +91,18 @@ def tile_picked_wedgecv_relu_l_kernel(
                 )
 
         def quantise_w1():
-            codes = keep.tile([P, H], U32, name="w1_cd", tag="w1_cd", align_bytes=64)
-            scales = keep.tile([P, H], U8, name="w1_sc", tag="w1_sc", align_bytes=64)
+            codes = keep.tile([P, H], U32, name="w1_cd", align_bytes=64)
+            scales = keep.tile([P, H], U8, name="w1_sc", align_bytes=64)
             for u in range(2):
                 w_cd[1, u], w_sc[1, u] = codes[:, 2 * P * u : 2 * P * (u + 1)], scales[:, 2 * P * u : 2 * P * (u + 1)]
-                nc.vector.quantize_mx(
-                    out=w_cd[1, u].bitcast(FP8X4), scales=w_sc[1, u], in_=w1_bf[:, 2 * H * u : 2 * H * (u + 1)]
-                )
+            nc.vector.quantize_mx(out=codes[:].bitcast(FP8X4), scales=scales[:], in_=w1_bf[:])
 
         e = [keep.tile([P, T], F32, name="e%d" % t) for t in range(PACK)]
-        y = [keep.tile([P, T], F32, name="y%d" % t) for t in range(PACK)]
 
-        def product(w, t, v0, n, b):
+        def product(acc, w, t, v0, n):
             m = slice((t % 2) * P, (t % 2 + 1) * P)
-            acc = bank(b, n)
             nc.tensor.matmul_mx(
-                out=acc[:],
+                out=acc,
                 lhsT=w_cd[w, t // 2][:, m].bitcast(FP8X4),
                 lhsT_scale=w_sc[w, t // 2][:, m],
                 rhs=x_cd[v0 // HALF][:, v0 % HALF : v0 % HALF + n].bitcast(FP8X4),
@@ -122,91 +110,55 @@ def tile_picked_wedgecv_relu_l_kernel(
                 start=True,
                 stop=True,
             )
-            return acc
 
-        def make_e(t, banks, copies=(nc.scalar.copy,), first=0):
+        def make_e(t, banks, copies=(nc.scalar.copy,)):
             n = T // len(banks)
             for q, b in enumerate(banks):
-                v0 = (first + q * n) % T
-                acc = product(2, t, v0, n, b)
-                copies[q % len(copies)](out=e[t][:, v0 : v0 + n], in_=acc[:])
+                acc = bank(b, n)
+                product(acc[:], 2, t, q * n, n)
+                copies[q % len(copies)](out=e[t][:, q * n : (q + 1) * n], in_=acc[:])
 
-        def looked_up(t, d, v0, n):
-            return e[t][:].indirect(lists[d][:, v0 // STRIPE : (v0 + n) // STRIPE])
+        y = {}
 
-        g, diff, gain, turned, z_t = {}, {}, {}, {}, {}
+        def make_y(block, b):
+            y[block] = bank(b, PACK, P)
+            for t in range(PACK):
+                product(y[block][:, t, :], 1, t, block * P, P)
 
-        def gather_first(t, v0=0, n=HALF):
-            nc.vector.tensor_copy(g[t][:, v0 : v0 + n], looked_up(t, 0, v0, n))
+        g, top, summed, z, z_cd, z_sc = {}, {}, {}, {}, {}, {}
 
-        def gather_diff(t):
-            nc.vector.tensor_tensor(diff[t], looked_up(t, 1, 0, HALF), g[t], SUB)
+        def gather(span, t, on_vector=False):
+            v0, n = span
+            for d in range(2):
+                g[span, t, d] = keep.tile([P, n], F32, name="g%d_%d_%d" % (v0, t, d))
+                window = e[t][:].indirect(lists[d][:, v0 // STRIPE : (v0 + n) // STRIPE])
+                if on_vector:
+                    nc.vector.tensor_copy(g[span, t, d][:], window)
+                else:
+                    nc.scalar.activation(out=g[span, t, d][:], in_=window, func=COPY)
 
-        def relu_diff(t):
-            nc.scalar.activation(out=gain[t], in_=diff[t], func=RELU)
+        def largest(span, t, tag):
+            if span not in top:
+                top[span] = keep.tile([P, PACK, span[1]], F32, name="top%d" % span[0], tag=tag, align_bytes=64)
+            nc.vector.tensor_tensor(top[span][:, t, :], g[span, t, 0][:], g[span, t, 1][:], MAX)
 
-        def add_turned(src, t, opens=False, closes=False):
-            u, s = divmod(t, 2)
-            for b0 in range(0, HALF // P, 2):
-                if opens:
-                    turned[u, b0] = bank(4 + 2 * u + b0 // 2, 2, 2, P)
-                for b in range(2):
-                    cols = slice((b0 + b) * P, (b0 + b + 1) * P)
-                    nc.tensor.matmul(
-                        turned[u, b0][:, b, s, :],
-                        lhsT=src[t][:, cols],
-                        rhs=ident[:],
-                        is_transpose=True,
-                        start=(opens and b == 0),
-                        stop=(closes and b == 1),
-                    )
-
-        def round_turned(u):
-            for b0 in range(0, HALF // P, 2):
-                name = "z_t%d%d" % (u, b0)
-                z_t[u, b0] = keep.tile([P, 2, 2 * P], BF16, name=name, tag=name, align_bytes=64)
-                nc.scalar.activation(
-                    out=z_t[u, b0][:].rearrange("v b (p s) -> v b p s", s=2),
-                    in_=turned[u, b0][:].rearrange("v b s p -> v b p s"),
-                    func=RELU,
+        def add_y(span):
+            v0, n = span
+            summed[span] = keep.tile([P, PACK * n], BF16, name="summed%d" % v0, align_bytes=64)
+            for b in range(n // P):
+                nc.vector.tensor_tensor(
+                    summed[span][:, PACK * P * b : PACK * P * (b + 1)].rearrange("p (c i t) -> p c t i", i=2, t=PACK),
+                    top[span][:, :, P * b : P * (b + 1)].rearrange("p t (c i) -> p c t i", i=2),
+                    y[v0 // P + b][:].rearrange("p t (c i) -> p c t i", i=2),
+                    ADD,
                 )
 
-        z, z_cd, z_sc, back = {}, {}, {}, {}
+        def relu(span):
+            z[span] = keep.tile([P, PACK * span[1]], BF16, name="z%d" % span[0], align_bytes=64)
+            nc.vector.tensor_scalar_max(z[span][:], summed[span][:], 0.0)
 
-        def turn_back(u):
-            for b0 in range(0, HALF // P, 2):
-                if u == 0:
-                    back[b0] = bank(2 + b0 // 2, 2, 2, P)
-                for b in range(2):
-                    nc.tensor.transpose(back[b0][:, b, u, :], z_t[u, b0][:, b, :].bitcast(F32), ident[:])
-
-        def bring_back():
-            z[TURNED] = keep.tile([P, PACK * HALF], BF16, name="z_turned", align_bytes=64)
-            words = z[TURNED][:].bitcast(F32).rearrange("p (b v u) -> p b v u", v=P, u=2)
-            for b0 in range(0, HALF // P, 2):
-                nc.scalar.copy(out=words[:, b0 : b0 + 2], in_=back[b0][:].rearrange("p b u v -> p b v u"))
-
-        def edge_tile(span, d, tag):
-            return keep.tile([P, PACK, span[1]], F32, name="edge%d_%d" % (span[0], d), tag=tag, align_bytes=64)
-
-        def gather_edges(edges, span, d, tiles=range(PACK)):
-            v0, n = span
-            for t in tiles:
-                nc.vector.tensor_tensor(edges[:, t, :], looked_up(t, d, v0, n), y[t][:, v0 : v0 + n], ADD)
-
-        def round_edges(dst, edges):
-            nc.scalar.activation(
-                out=dst.rearrange("p (c i t) -> p c t i", i=4, t=PACK),
-                in_=edges.rearrange("p t (c i) -> p c t i", i=4),
-                func=RELU,
-            )
-
-        def largest(span, a, b, tag):
-            z[span] = keep.tile([P, PACK * span[1]], BF16, name="z%d" % span[0], tag=tag, align_bytes=64)
-            nc.vector.tensor_tensor(z[span][:], a, b, MAX)
-
-        def quantise_z(span, tag=None):
-            z_cd[span] = keep.tile([P, span[1]], U32, name="z_cd%d" % span[0], tag=tag or "z_cd%d" % span[0], align_bytes=64)
+        def quantise_z(span):
+            z_cd[span] = keep.tile([P, span[1]], U32, name="z_cd%d" % span[0], align_bytes=64)
             z_sc[span] = keep.tile([P, span[1]], U8, name="z_sc%d" % span[0], align_bytes=64)
             nc.vector.quantize_mx(out=z_cd[span][:].bitcast(FP8X4), scales=z_sc[span][:], in_=z[span][:])
 
@@ -245,87 +197,53 @@ def tile_picked_wedgecv_relu_l_kernel(
         cast_w2(1, on_vector=P)
         make_e(0, (0, 1, 2, 3), (nc.scalar.copy, nc.scalar.copy, nc.vector.tensor_copy, nc.scalar.copy))
         quantise_w2(1)
-
-        for t in range(2):
-            g[t] = keep.tile([P, HALF], F32, name="g%d" % t)[:]
-        g[2], g[3], diff[0] = (late[:, q * HALF : (q + 1) * HALF] for q in range(3))
-        for t in range(PACK - 1):
-            gather_first(t, 0, HALF if t < 2 else FREE)
-            make_e(t + 1, ((6, 7, 0, 1), (4, 5), (2, 3))[t], first=HALF)
+        gather(FIRST, 0, on_vector=True)
+        make_e(1, (4, 5))
+        gather(FIRST, 1, on_vector=True)
+        make_e(2, (6, 7))
+        make_e(3, (0, 1))
         cast_w1(0)
         cast_w1(1)
         quantise_w1()
-        gather_first(2, FREE, HALF - FREE)
-        gather_first(3)
-        diffs = keep.tile([P, PACK - 1, HALF], F32, name="diffs", tag="w1_bf", align_bytes=64)
+        for block in range(T // P):
+            make_y(block, (block + 2) % 8)
+        gather(FIRST, 2)
+        gather(FIRST, 3)
+        largest(FIRST, 0, "w1_bf")
+        largest(FIRST, 1, "w1_bf")
+        gather(SECOND, 0, on_vector=True)
+        largest(FIRST, 2, "w1_bf")
+        largest(FIRST, 3, "w1_bf")
+        add_y(FIRST)
+        for t in range(1, PACK):
+            gather(SECOND, t)
+        relu(FIRST)
+        largest(SECOND, 0, "w1_bf")
+        quantise_z(FIRST)
+        for t in range(1, PACK):
+            largest(SECOND, t, "w1_bf")
+        add_y(SECOND)
         for t in range(PACK):
-            if t:
-                diff[t] = diffs[:, t - 1, :]
-            gather_diff(t)
-
-        pieces = [(0, HALF, HALF // 2), (0, HALF + HALF // 2, HALF // 2)]
-        pieces.extend([(2 * u + s, h * HALF, HALF) for u in range(2) for h in (1, 0) for s in range(2)][1:])
-        for q, (t, v0, n) in enumerate(pieces):
-            acc = product(1, t, v0, n, q % 4)
-            nc.scalar.copy(out=y[t][:, v0 : v0 + n], in_=acc[:])
-        for t in range(2):
-            gain[t] = keep.tile([P, HALF], F32, name="gain%d" % t)[:]
-            relu_diff(t)
-
-        add_turned(g, 0, opens=True)
-        add_turned(g, 1)
-        add_turned(y, 0)
-        add_turned(y, 1)
-        add_turned(g, 2, opens=True)
-        add_turned(g, 3)
-        add_turned(y, 2)
-        add_turned(y, 3)
-        add_turned(gain, 0)
-        add_turned(gain, 1, closes=True)
-        gain_late = keep.tile([P, 2, HALF], F32, name="gain_late", tag="w1_cd", align_bytes=64)
-        gain[2], gain[3] = gain_late[:, 0, :], gain_late[:, 1, :]
-        relu_diff(2)
-        add_turned(gain, 2)
-        relu_diff(3)
-        add_turned(gain, 3, closes=True)
-        for u in range(2):
-            round_turned(u)
-            turn_back(u)
-
-        second0 = edge_tile(SECOND, 0, "edge_a")
-        gather_edges(second0, SECOND, 0)
-        second0_bf = keep.tile([P, PACK * SECOND[1]], BF16, name="second0_bf", tag="w1_cd", align_bytes=64)
-        round_edges(second0_bf[:], second0[:])
-        bring_back()
-        second1 = edge_tile(SECOND, 1, "w1_sc")
-        gather_edges(second1, SECOND, 1)
-        second1_bf = keep.tile([P, PACK * SECOND[1]], BF16, name="second1_bf", tag="ident", align_bytes=64)
-        round_edges(second1_bf[:], second1[:])
-        late0 = edge_tile(LATE, 0, "x_cd1")
-        gather_edges(late0, LATE, 0)
-        quantise_z(TURNED)
-        late0_bf = keep.tile([P, PACK * LATE[1]], BF16, name="late0_bf", tag="z_t12", align_bytes=64)
-        third1_bf = keep.tile([P, PACK * THIRD[1]], BF16, name="third1_bf", align_bytes=64)
-        last1_bf = keep.tile([P, PACK * LAST[1]], BF16, name="last1_bf", align_bytes=64)
-        round_edges(late0_bf[:], late0[:])
-        finish_rows(TURNED, 0, 0, nc.scalar.copy)
-
-        third1 = edge_tile(THIRD, 1, "w1_sc")
-        gather_edges(third1, THIRD, 1)
-        round_edges(third1_bf[:], third1[:])
-        finish_rows(TURNED, 1, 1, nc.scalar.copy)
-        last1 = edge_tile(LAST, 1, "x_cd1")
-        gather_edges(last1, LAST, 1)
-        round_edges(last1_bf[:], last1[:])
-
-        largest(SECOND, second0_bf[:], second1_bf[:], "w1_sc")
-        largest(THIRD, late0_bf[:, : PACK * THIRD[1]], third1_bf[:], "z_third")
+            gather(THIRD, t)
+        finish_rows(FIRST, 0, 2, nc.scalar.copy)
+        finish_rows(FIRST, 1, 3, nc.scalar.copy)
+        relu(SECOND)
+        largest(THIRD, 0, "w1_bf")
         quantise_z(SECOND)
-        largest(LAST, late0_bf[:, PACK * THIRD[1] :], last1_bf[:], "z_last")
-        quantise_z(THIRD, "x_cd1")
+        for t in range(1, PACK):
+            largest(THIRD, t, "w1_bf")
+        add_y(THIRD)
+        for t in range(PACK):
+            gather(LAST, t)
+        finish(SECOND, 4)
+        relu(THIRD)
+        largest(LAST, 0, "w1_bf")
+        quantise_z(THIRD)
+        for t in range(1, PACK):
+            largest(LAST, t, "w1_bf")
+        add_y(LAST)
+        finish(THIRD, 5)
+        relu(LAST)
         quantise_z(LAST)
-        finish_rows(SECOND, 0, 4, nc.scalar.copy)
-        finish_rows(SECOND, 1, 5, nc.scalar.copy)
-        finish(THIRD, 2)
         finish_rows(LAST, 0, 6, nc.vector.tensor_copy)
-        finish_rows(LAST, 1, 7, nc.vector.tensor_copy)
+        finish_rows(LAST, 1, 7, nc.scalar.copy)

@@ -23,7 +23,8 @@ PACK = 4
 STRIPE = 16
 HALF = T // 2
 VECTOR_SHARE = 88
-FIRST, SECOND, THIRD, LAST = (0, 512), (512, 256), (768, 128), (896, 128)
+SPANS = (0, 512), (512, 256), (768, 128), (896, 128)
+SHARE = (768, 768)
 
 
 def tile_picked_wedgecv_relu_l_kernel(
@@ -40,10 +41,10 @@ def tile_picked_wedgecv_relu_l_kernel(
         x_sc = keep.tile([P, T], U8, name="x_sc", align_bytes=64)
         w3_sc = keep.tile([P, N], U8, name="w3_sc", align_bytes=64)
         nc.vector.memset(x_sc[:].bitcast(U32), 0)
-        nc.gpsimd.memset(w3_sc[:].bitcast(U32), 0)
+        nc.vector.memset(w3_sc[:].bitcast(U32), 0)
 
         w2_raw = keep.tile([P, PACK, H], F32, name="w2_raw")
-        w1_raw = [keep.tile([P, PACK, H // 2], F32, name="w1_raw%d" % h) for h in range(2)]
+        w1_raw = [keep.tile([P, PACK, H // 2], F32, name="w1_raw%d" % h, tag="w1_raw%d" % h, align_bytes=64) for h in range(2)]
         x_cd = [keep.tile([P, HALF], U32, name="x_cd%d" % h, align_bytes=64) for h in range(2)]
         lists = [keep.tile([P, T // STRIPE], U16, name="list%d" % d) for d in range(2)]
         nc.sync.dma_start(out=w2_raw[:], in_=w2.rearrange("(p j) c -> p j c", j=PACK))
@@ -125,37 +126,39 @@ def tile_picked_wedgecv_relu_l_kernel(
             for t in range(PACK):
                 product(y[block][:, t, :], 1, t, block * P, P)
 
-        g, top, summed, z, z_cd, z_sc = {}, {}, {}, {}, {}, {}
+        top, summed, z, z_cd, z_sc = {}, {}, {}, {}, {}
 
-        def gather(span, t, on_vector=False):
-            v0, n = span
-            for d in range(2):
-                g[span, t, d] = keep.tile([P, n], F32, name="g%d_%d_%d" % (v0, t, d))
-                window = e[t][:].indirect(lists[d][:, v0 // STRIPE : (v0 + n) // STRIPE])
-                if on_vector:
-                    nc.vector.tensor_copy(g[span, t, d][:], window)
-                else:
-                    nc.scalar.activation(out=g[span, t, d][:], in_=window, func=COPY)
+        def pair_tile(name, tiles, n):
+            return keep.tile([P, tiles, n], F32, name=name)
 
-        def largest(span, t, tag):
+        def gather(dst, t, d, v0, n, on_vector=False):
+            window = e[t][:].indirect(lists[d][:, v0 // STRIPE : (v0 + n) // STRIPE])
+            if on_vector:
+                nc.vector.tensor_copy(dst, window)
+            else:
+                nc.scalar.activation(out=dst, in_=window, func=COPY)
+
+        def largest(span, tag, t0, c0, a, b):
             if span not in top:
                 top[span] = keep.tile([P, PACK, span[1]], F32, name="top%d" % span[0], tag=tag, align_bytes=64)
-            nc.vector.tensor_tensor(top[span][:, t, :], g[span, t, 0][:], g[span, t, 1][:], MAX)
+            nc.vector.tensor_tensor(top[span][:, t0 : t0 + a.shape[1], c0 : c0 + a.shape[2]], a, b, MAX)
 
-        def add_y(span):
-            v0, n = span
-            summed[span] = keep.tile([P, PACK * n], BF16, name="summed%d" % v0, align_bytes=64)
-            for b in range(n // P):
-                nc.vector.tensor_tensor(
-                    summed[span][:, PACK * P * b : PACK * P * (b + 1)].rearrange("p (c i t) -> p c t i", i=2, t=PACK),
-                    top[span][:, :, P * b : P * (b + 1)].rearrange("p t (c i) -> p c t i", i=2),
-                    y[v0 // P + b][:].rearrange("p t (c i) -> p c t i", i=2),
-                    ADD,
-                )
+        def add_y(span, whole, c0, n=P):
+            if span not in summed:
+                summed[span] = keep.tile([P, PACK * span[1]], BF16, name="summed%d" % span[0], tag="summed%d" % span[0], align_bytes=64)
+            block, b0 = divmod(span[0] + c0, P)
+            nc.vector.tensor_tensor(
+                summed[span][:, PACK * c0 : PACK * (c0 + n)].rearrange("p (c i t) -> p c t i", i=2, t=PACK),
+                top[whole][:, :, span[0] - whole[0] + c0 : span[0] - whole[0] + c0 + n].rearrange("p t (c i) -> p c t i", i=2),
+                y[block][:, :, b0 : b0 + n].rearrange("p t (c i) -> p c t i", i=2),
+                ADD,
+            )
 
-        def relu(span):
-            z[span] = keep.tile([P, PACK * span[1]], BF16, name="z%d" % span[0], align_bytes=64)
-            nc.vector.tensor_scalar_max(z[span][:], summed[span][:], 0.0)
+        def relu(span, c0=0, n=None):
+            if span not in z:
+                z[span] = keep.tile([P, PACK * span[1]], BF16, name="z%d" % span[0], align_bytes=64)
+            cols = slice(PACK * c0, PACK * (c0 + (n or span[1])))
+            nc.vector.tensor_scalar_max(z[span][:, cols], summed[span][:, cols], 0.0)
 
         def quantise_z(span):
             z_cd[span] = keep.tile([P, span[1]], U32, name="z_cd%d" % span[0], align_bytes=64)
@@ -175,75 +178,84 @@ def tile_picked_wedgecv_relu_l_kernel(
                 stop=True,
             )
 
-        def finish_rows(span, a, b, copy):
-            v0, n = span
+        def finish(spans, a, b, copy=nc.scalar.copy):
+            v0, n = spans[0][0], sum(span[1] for span in spans)
             res = keep.tile([P, n], F32, name="res%d_%d" % (v0, a))
             acc = bank(b, n)
-            last_product(span, a, acc[:])
+            for span in spans:
+                last_product(span, a, acc[:, span[0] - v0 : span[0] - v0 + span[1]])
             copy(out=res[:], in_=acc[:])
             nc.sync.dma_start(out=out_v[:, a, v0 : v0 + n], in_=res[:])
-
-        def finish(span, b):
-            v0, n = span
-            res = keep.tile([P, N // P, n], F32, name="res%d" % v0)
-            acc = bank(b, N // P, n)
-            for a in range(N // P):
-                last_product(span, a, acc[:, a, :])
-            nc.scalar.copy(out=res[:], in_=acc[:])
-            nc.sync.dma_start(out=out_v[:, :, v0 : v0 + n], in_=res[:])
 
         cast_w2(0, on_vector=VECTOR_SHARE)
         quantise_w2(0, step=P)
         cast_w2(1, on_vector=P)
         make_e(0, (0, 1, 2, 3), (nc.scalar.copy, nc.scalar.copy, nc.vector.tensor_copy, nc.scalar.copy))
         quantise_w2(1)
-        gather(FIRST, 0, on_vector=True)
+        first, second, third, last = SPANS
+        mid = (second[0], second[1] + third[1])
+        low = [pair_tile("low%d" % d, 2, last[0]) for d in range(2)]
         make_e(1, (4, 5))
-        gather(FIRST, 1, on_vector=True)
+        for d in range(2):
+            gather(low[d][:, 0, : SHARE[d]], 0, d, 0, SHARE[d], on_vector=True)
+        for d in range(2):
+            gather(low[d][:, 1, : first[1]], 1, d, *first, on_vector=True)
         make_e(2, (6, 7))
         make_e(3, (0, 1))
         cast_w1(0)
         cast_w1(1)
+        got = {}
+
+        def on_scalar(t, v0, n):
+            got[t, v0] = [pair_tile("got%d_%d_%d" % (t, v0, d), 1, n) for d in range(2)]
+            for d in range(2):
+                gather(got[t, v0][d][:, 0, :], t, d, v0, n)
+
+        on_scalar(2, *first)
+        on_scalar(3, 0, 256)
+        on_scalar(3, 256, 256)
+        for d in range(2):
+            gather(low[d][:, 1, mid[0] :], 1, d, *mid)
+        on_scalar(2, *mid)
+        on_scalar(3, *second)
+        for d in range(2):
+            gather(low[d][:, 0, SHARE[d] :], 0, d, SHARE[d], last[0] - SHARE[d])
+        on_scalar(3, *third)
+        late = [pair_tile("late%d" % d, PACK, last[1]) for d in range(2)]
+        for t in range(PACK):
+            for d in range(2):
+                gather(late[d][:, t, :], t, d, *last)
         quantise_w1()
         for block in range(T // P):
             make_y(block, (block + 2) % 8)
-        gather(FIRST, 2)
-        gather(FIRST, 3)
-        largest(FIRST, 0, "w1_bf")
-        largest(FIRST, 1, "w1_bf")
-        gather(SECOND, 0, on_vector=True)
-        largest(FIRST, 2, "w1_bf")
-        largest(FIRST, 3, "w1_bf")
-        add_y(FIRST)
-        for t in range(1, PACK):
-            gather(SECOND, t)
-        relu(FIRST)
-        largest(SECOND, 0, "w1_bf")
-        quantise_z(FIRST)
-        for t in range(1, PACK):
-            largest(SECOND, t, "w1_bf")
-        add_y(SECOND)
-        for t in range(PACK):
-            gather(THIRD, t)
-        finish_rows(FIRST, 0, 2, nc.scalar.copy)
-        finish_rows(FIRST, 1, 3, nc.scalar.copy)
-        relu(SECOND)
-        largest(THIRD, 0, "w1_bf")
-        quantise_z(SECOND)
-        for t in range(1, PACK):
-            largest(THIRD, t, "w1_bf")
-        add_y(THIRD)
-        for t in range(PACK):
-            gather(LAST, t)
-        finish(SECOND, 4)
-        relu(THIRD)
-        largest(LAST, 0, "w1_bf")
-        quantise_z(THIRD)
-        for t in range(1, PACK):
-            largest(LAST, t, "w1_bf")
-        add_y(LAST)
-        finish(THIRD, 5)
-        relu(LAST)
-        quantise_z(LAST)
-        finish_rows(LAST, 0, 6, nc.vector.tensor_copy)
-        finish_rows(LAST, 1, 7, nc.scalar.copy)
+        largest(first, "w1_raw1", 0, 0, low[0][:, :, :512], low[1][:, :, :512])
+        largest(first, "w1_raw1", 2, 0, *[x[:] for x in got[2, 0]])
+        largest(first, "w1_raw1", 3, 0, *[x[:] for x in got[3, 0]])
+        largest(first, "w1_raw1", 3, 256, *[x[:] for x in got[3, 256]])
+        for b in range(4):
+            add_y(first, first, b * P)
+        largest(mid, "w1_raw1", 0, 0, low[0][:, :, 512:768], low[1][:, :, 512:768])
+        relu(first)
+        largest(mid, "w1_raw1", 2, 0, *[x[:] for x in got[2, mid[0]]])
+        quantise_z(first)
+        finish((first,), 0, 2)
+        finish((first,), 1, 3)
+        largest(mid, "w1_raw1", 3, 0, *[x[:] for x in got[3, second[0]]])
+        add_y(second, mid, 0)
+        add_y(second, mid, P)
+        largest(mid, "w1_raw1", 0, second[1], low[0][:, :, 768:], low[1][:, :, 768:])
+        relu(second)
+        largest(mid, "w1_raw1", 3, second[1], *[x[:] for x in got[3, third[0]]])
+        quantise_z(second)
+        add_y(third, mid, 0)
+        largest(last, "summed512", 0, 0, late[0][:, :3], late[1][:, :3])
+        relu(third)
+        largest(last, "summed512", 3, 0, late[0][:, 3:], late[1][:, 3:])
+        quantise_z(third)
+        finish((second, third), 0, 4)
+        finish((second, third), 1, 5)
+        add_y(last, last, 0)
+        relu(last)
+        quantise_z(last)
+        finish((last,), 0, 6, nc.vector.tensor_copy)
+        finish((last,), 1, 7)

@@ -24,7 +24,7 @@ STRIPE = 16
 HALF = T // 2
 VECTOR_SHARE = 88
 SPANS = (0, 512), (512, 256), (768, 128), (896, 128)
-SHARE = (768, 768)
+SHARE = (768, 640)
 
 
 def tile_picked_wedgecv_relu_l_kernel(
@@ -216,10 +216,10 @@ def tile_picked_wedgecv_relu_l_kernel(
         on_scalar(3, 256, 256)
         for d in range(2):
             gather(low[d][:, 1, mid[0] :], 1, d, *mid)
+        gather(low[1][:, 0, SHARE[1] :], 0, 1, SHARE[1], last[0] - SHARE[1])
         on_scalar(2, *mid)
         on_scalar(3, *second)
-        for d in range(2):
-            gather(low[d][:, 0, SHARE[d] :], 0, d, SHARE[d], last[0] - SHARE[d])
+        gather(low[0][:, 0, SHARE[0] :], 0, 0, SHARE[0], last[0] - SHARE[0])
         on_scalar(3, *third)
         late = [pair_tile("late%d" % d, PACK, last[1]) for d in range(2)]
         for t in range(PACK):

@@ -22,9 +22,9 @@ P = 128
 PACK = 4
 STRIPE = 16
 HALF = T // 2
-VECTOR_SHARE = 88
+VECTOR_SHARE = 44
 SPANS = (0, 512), (512, 256), (768, 128), (896, 128)
-SHARE = (768, 640)
+SHARE = (896, 768)
 
 
 def tile_picked_wedgecv_relu_l_kernel(
@@ -43,15 +43,17 @@ def tile_picked_wedgecv_relu_l_kernel(
         nc.vector.memset(x_sc[:].bitcast(U32), 0)
         nc.vector.memset(w3_sc[:].bitcast(U32), 0)
 
-        w2_raw = keep.tile([P, PACK, H], F32, name="w2_raw")
+        w2_raw = [keep.tile([P, PACK, H // 2], F32, name="w2_raw%d" % h) for h in range(2)]
         w1_raw = [keep.tile([P, PACK, H // 2], F32, name="w1_raw%d" % h, tag="w1_raw%d" % h, align_bytes=64) for h in range(2)]
         x_cd = [keep.tile([P, HALF], U32, name="x_cd%d" % h, align_bytes=64) for h in range(2)]
         lists = [keep.tile([P, T // STRIPE], U16, name="list%d" % d) for d in range(2)]
-        nc.sync.dma_start(out=w2_raw[:], in_=w2.rearrange("(p j) c -> p j c", j=PACK))
+        for h in range(2):
+            cols = slice(h * H // 2, (h + 1) * H // 2)
+            nc.sync.dma_start(out=w2_raw[h][:], in_=w2.rearrange("(p j) c -> p j c", j=PACK)[:, :, cols])
         x_src = x_words[0].rearrange("p n r -> p (n r)").bitcast(I32)
-        nc.sync.dma_start(out=x_cd[0][:].bitcast(I32), in_=x_src[:, :HALF])
         for r in range(4):
             nc.sync.dma_start(out=x_sc[r:P:32, :].bitcast(I32), in_=x_scales[0][r:16:4, :].bitcast(I32))
+        nc.sync.dma_start(out=x_cd[0][:].bitcast(I32), in_=x_src[:, :HALF])
         nc.sync.dma_start(out=x_cd[1][:].bitcast(I32), in_=x_src[:, HALF:])
         nc.sync.dma_start(lists[0][:], pos1)
         nc.sync.dma_start(lists[1][:], pos2)
@@ -65,13 +67,13 @@ def tile_picked_wedgecv_relu_l_kernel(
 
         w_bf, w_cd, w_sc = {}, {}, {}
 
-        def cast_w2(u, on_vector=0):
-            w_bf[2, u] = keep.tile([P, 2 * H], BF16, name="w2_bf%d" % u, tag="w2_bf", align_bytes=64)[:]
-            dst = w_bf[2, u].rearrange("p (s m j) -> p m j s", s=2, j=PACK)
-            src = w2_raw[:].rearrange("p j (m t) -> p m j t", t=PACK)[:, :, :, 2 * u : 2 * u + 2]
+        def cast_w2(u, h, tag, on_vector=P // 2):
+            w_bf[u, h] = keep.tile([P, H], BF16, name="w2_bf%d%d" % (u, h), tag=tag, align_bytes=64)[:]
+            dst = w_bf[u, h].rearrange("p (s m j) -> p m j s", s=2, j=PACK)
+            src = w2_raw[h][:].rearrange("p j (m t) -> p m j t", t=PACK)[:, :, :, 2 * u : 2 * u + 2]
             if on_vector:
                 nc.vector.tensor_copy(out=dst[:, :on_vector], in_=src[:, :on_vector])
-            if on_vector < P:
+            if on_vector < P // 2:
                 nc.scalar.activation(out=dst[:, on_vector:], in_=src[:, on_vector:], func=COPY)
 
         w1_bf = keep.tile([P, PACK * H], BF16, name="w1_bf", tag="w1_bf", align_bytes=64)
@@ -81,14 +83,17 @@ def tile_picked_wedgecv_relu_l_kernel(
             src = w1_raw[h][:].rearrange("p j (m t) -> p m t j", t=PACK)
             nc.gpsimd.tensor_scalar(dst, src, 1.0, 0.0, MULT, ADD)
 
-        def quantise_w2(u, step=2 * P):
+        for u in range(2):
             w_cd[2, u] = keep.tile([P, 2 * P], U32, name="w2_cd%d" % u, align_bytes=64)[:]
             w_sc[2, u] = keep.tile([P, 2 * P], U8, name="w2_sc%d" % u, align_bytes=64)[:]
-            for a in range(0, 2 * P, step):
+
+        def quantise_w2(u, h):
+            for s in range(2):
+                cols = slice(s * P + h * P // 2, s * P + (h + 1) * P // 2)
                 nc.vector.quantize_mx(
-                    out=w_cd[2, u][:, a : a + step].bitcast(FP8X4),
-                    scales=w_sc[2, u][:, a : a + step],
-                    in_=w_bf[2, u][:, PACK * a : PACK * (a + step)],
+                    out=w_cd[2, u][:, cols].bitcast(FP8X4),
+                    scales=w_sc[2, u][:, cols],
+                    in_=w_bf[u, h][:, s * H // 2 : (s + 1) * H // 2],
                 )
 
         def quantise_w1():
@@ -112,12 +117,13 @@ def tile_picked_wedgecv_relu_l_kernel(
                 stop=True,
             )
 
-        def make_e(t, banks, copies=(nc.scalar.copy,)):
+        def make_e(t, banks):
             n = T // len(banks)
             for q, b in enumerate(banks):
+                v0 = (HALF + q * n) % T
                 acc = bank(b, n)
-                product(acc[:], 2, t, q * n, n)
-                copies[q % len(copies)](out=e[t][:, q * n : (q + 1) * n], in_=acc[:])
+                product(acc[:], 2, t, v0, n)
+                nc.scalar.copy(out=e[t][:, v0 : v0 + n], in_=acc[:])
 
         y = {}
 
@@ -187,21 +193,39 @@ def tile_picked_wedgecv_relu_l_kernel(
             copy(out=res[:], in_=acc[:])
             nc.sync.dma_start(out=out_v[:, a, v0 : v0 + n], in_=res[:])
 
-        cast_w2(0, on_vector=VECTOR_SHARE)
-        quantise_w2(0, step=P)
-        cast_w2(1, on_vector=P)
-        make_e(0, (0, 1, 2, 3), (nc.scalar.copy, nc.scalar.copy, nc.vector.tensor_copy, nc.scalar.copy))
-        quantise_w2(1)
+        def finish_both(span, b):
+            v0, n = span
+            res = keep.tile([P, N // P, n], F32, name="res%d" % v0)
+            acc = bank(b, N // P, n)
+            for a in range(N // P):
+                last_product(span, a, acc[:, a, :])
+            nc.scalar.copy(out=res[:], in_=acc[:])
+            nc.sync.dma_start(out=out_v[:, :, v0 : v0 + n], in_=res[:])
+
+        cast_w2(0, 0, "w2_bf0")
+        cast_w2(1, 0, "w2_bf1", on_vector=0)
+        quantise_w2(0, 0)
+        cast_w2(0, 1, "w2_bf2", on_vector=VECTOR_SHARE)
+        quantise_w2(0, 1)
+        quantise_w2(1, 0)
+        cast_w2(1, 1, "w2_bf2")
+        quantise_w2(1, 1)
+        v0 = 0
+        for q, n in enumerate((256, 256, 256, 128, 128)):
+            acc = bank((0, 1, 2, 6, 3)[q], n)
+            product(acc[:], 2, 0, v0, n)
+            (nc.scalar.copy, nc.vector.tensor_copy)[q % 2](out=e[0][:, v0 : v0 + n], in_=acc[:])
+            v0 = v0 + n
         first, second, third, last = SPANS
         mid = (second[0], second[1] + third[1])
         low = [pair_tile("low%d" % d, 2, last[0]) for d in range(2)]
-        make_e(1, (4, 5))
+        make_e(1, (4, 5, 0, 1))
         for d in range(2):
             gather(low[d][:, 0, : SHARE[d]], 0, d, 0, SHARE[d], on_vector=True)
         for d in range(2):
             gather(low[d][:, 1, : first[1]], 1, d, *first, on_vector=True)
-        make_e(2, (6, 7))
-        make_e(3, (0, 1))
+        make_e(2, (7, 2))
+        make_e(3, (6, 3))
         cast_w1(0)
         cast_w1(1)
         got = {}
@@ -216,10 +240,9 @@ def tile_picked_wedgecv_relu_l_kernel(
         on_scalar(3, 256, 256)
         for d in range(2):
             gather(low[d][:, 1, mid[0] :], 1, d, *mid)
-        gather(low[1][:, 0, SHARE[1] :], 0, 1, SHARE[1], last[0] - SHARE[1])
         on_scalar(2, *mid)
         on_scalar(3, *second)
-        gather(low[0][:, 0, SHARE[0] :], 0, 0, SHARE[0], last[0] - SHARE[0])
+        gather(low[1][:, 0, SHARE[1] :], 0, 1, SHARE[1], last[0] - SHARE[1])
         on_scalar(3, *third)
         late = [pair_tile("late%d" % d, PACK, last[1]) for d in range(2)]
         for t in range(PACK):
@@ -247,14 +270,14 @@ def tile_picked_wedgecv_relu_l_kernel(
         relu(second)
         largest(mid, "w1_raw1", 3, second[1], *[x[:] for x in got[3, third[0]]])
         quantise_z(second)
+        finish_both(second, 4)
         add_y(third, mid, 0)
         largest(last, "summed512", 0, 0, late[0][:, :3], late[1][:, :3])
-        relu(third)
         largest(last, "summed512", 3, 0, late[0][:, 3:], late[1][:, 3:])
-        quantise_z(third)
-        finish((second, third), 0, 4)
-        finish((second, third), 1, 5)
+        relu(third)
         add_y(last, last, 0)
+        quantise_z(third)
+        finish_both(third, 5)
         relu(last)
         quantise_z(last)
         finish((last,), 0, 6, nc.vector.tensor_copy)

@@ -16,8 +16,10 @@ FP4X4 = mybir.dt.float4_e2m1fn_x4
 ADD = mybir.AluOpType.add
 MULT = mybir.AluOpType.mult
 MAX = mybir.AluOpType.max
+MIN = mybir.AluOpType.min
 COPY = mybir.ActivationFunctionType.Copy
 
+LARGEST = (2.0 - 2.0**-23) * 2.0**127
 P = 128
 PACK = 4
 STRIPE = 16
@@ -160,11 +162,14 @@ def tile_picked_wedgecv_relu_l_kernel(
                 ADD,
             )
 
-        def relu(span, c0=0, n=None):
+        def relu(span, c0=0, n=None, on_gpsimd=False):
             if span not in z:
                 z[span] = keep.tile([P, PACK * span[1]], BF16, name="z%d" % span[0], align_bytes=64)
             cols = slice(PACK * c0, PACK * (c0 + (n or span[1])))
-            nc.vector.tensor_scalar_max(z[span][:, cols], summed[span][:, cols], 0.0)
+            if on_gpsimd:
+                nc.gpsimd.tensor_scalar(z[span][:, cols], summed[span][:, cols], LARGEST, 0.0, MIN, MAX)
+            else:
+                nc.vector.tensor_scalar_max(z[span][:, cols], summed[span][:, cols], 0.0)
 
         def quantise_z(span):
             z_cd[span] = keep.tile([P, span[1]], U32, name="z_cd%d" % span[0], align_bytes=64)
@@ -257,8 +262,10 @@ def tile_picked_wedgecv_relu_l_kernel(
         largest(first, "w1_raw1", 3, 256, *[x[:] for x in got[3, 256]])
         for b in range(4):
             add_y(first, first, b * P)
+            if b < 2:
+                relu(first, b * P, P, on_gpsimd=True)
         largest(mid, "w1_raw1", 0, 0, low[0][:, :, 512:768], low[1][:, :, 512:768])
-        relu(first)
+        relu(first, 2 * P, 2 * P)
         largest(mid, "w1_raw1", 2, 0, *[x[:] for x in got[2, mid[0]]])
         quantise_z(first)
         finish((first,), 0, 2)

@@ -254,8 +254,8 @@ def tile_picked_wedgecv_relu_l_kernel(
             for d in range(2):
                 gather(late[d][:, t, :], t, d, *last)
         quantise_w1()
-        for block in range(T // P):
-            make_y(block, (block + 2) % 8)
+        for block in range(6):
+            make_y(block, block + 2)
         largest(first, "w1_raw1", 0, 0, low[0][:, :, :512], low[1][:, :, :512])
         largest(first, "w1_raw1", 2, 0, *[x[:] for x in got[2, 0]])
         largest(first, "w1_raw1", 3, 0, *[x[:] for x in got[3, 0]])
@@ -269,16 +269,18 @@ def tile_picked_wedgecv_relu_l_kernel(
         largest(mid, "w1_raw1", 2, 0, *[x[:] for x in got[2, mid[0]]])
         quantise_z(first)
         finish((first,), 0, 2)
-        finish((first,), 1, 3)
         largest(mid, "w1_raw1", 3, 0, *[x[:] for x in got[3, second[0]]])
         add_y(second, mid, 0)
+        make_y(6, 6)
         add_y(second, mid, P)
+        make_y(7, 7)
         largest(mid, "w1_raw1", 0, second[1], low[0][:, :, 768:], low[1][:, :, 768:])
         relu(second)
         largest(mid, "w1_raw1", 3, second[1], *[x[:] for x in got[3, third[0]]])
         quantise_z(second)
         finish_both(second, 4)
         add_y(third, mid, 0)
+        finish((first,), 1, 6)
         largest(last, "summed512", 0, 0, late[0][:, :3], late[1][:, :3])
         largest(last, "summed512", 3, 0, late[0][:, 3:], late[1][:, 3:])
         relu(third)
@@ -287,5 +289,5 @@ def tile_picked_wedgecv_relu_l_kernel(
         finish_both(third, 5)
         relu(last)
         quantise_z(last)
-        finish((last,), 0, 6, nc.vector.tensor_copy)
-        finish((last,), 1, 7)
+        finish((last,), 0, 0, nc.vector.tensor_copy)
+        finish((last,), 1, 1)

@@ -24,7 +24,7 @@ P = 128
 PACK = 4
 STRIPE = 16
 HALF = T // 2
-VECTOR_SHARE = 44
+VECTOR_SHARE = 24
 SPANS = (0, 512), (512, 256), (768, 128), (896, 128)
 SHARE = (896, 768)
 
@@ -45,13 +45,11 @@ def tile_picked_wedgecv_relu_l_kernel(
         nc.vector.memset(x_sc[:].bitcast(U32), 0)
         nc.vector.memset(w3_sc[:].bitcast(U32), 0)
 
-        w2_raw = [keep.tile([P, PACK, H // 2], F32, name="w2_raw%d" % h) for h in range(2)]
+        w2_raw = keep.tile([P, PACK, H], F32, name="w2_raw")
         w1_raw = [keep.tile([P, PACK, H // 2], F32, name="w1_raw%d" % h, tag="w1_raw%d" % h, align_bytes=64) for h in range(2)]
         x_cd = [keep.tile([P, HALF], U32, name="x_cd%d" % h, align_bytes=64) for h in range(2)]
         lists = [keep.tile([P, T // STRIPE], U16, name="list%d" % d) for d in range(2)]
-        for h in range(2):
-            cols = slice(h * H // 2, (h + 1) * H // 2)
-            nc.sync.dma_start(out=w2_raw[h][:], in_=w2.rearrange("(p j) c -> p j c", j=PACK)[:, :, cols])
+        nc.sync.dma_start(out=w2_raw[:], in_=w2.rearrange("(p j) c -> p j c", j=PACK))
         x_src = x_words[0].rearrange("p n r -> p (n r)").bitcast(I32)
         for r in range(4):
             nc.sync.dma_start(out=x_sc[r:P:32, :].bitcast(I32), in_=x_scales[0][r:16:4, :].bitcast(I32))
@@ -72,7 +70,7 @@ def tile_picked_wedgecv_relu_l_kernel(
         def cast_w2(u, h, tag, on_vector=P // 2):
             w_bf[u, h] = keep.tile([P, H], BF16, name="w2_bf%d%d" % (u, h), tag=tag, align_bytes=64)[:]
             dst = w_bf[u, h].rearrange("p (s m j) -> p m j s", s=2, j=PACK)
-            src = w2_raw[h][:].rearrange("p j (m t) -> p m j t", t=PACK)[:, :, :, 2 * u : 2 * u + 2]
+            src = w2_raw[:].rearrange("p j (m t) -> p m j t", t=PACK)[:, h * P // 2 : (h + 1) * P // 2, :, 2 * u : 2 * u + 2]
             if on_vector:
                 nc.vector.tensor_copy(out=dst[:, :on_vector], in_=src[:, :on_vector])
             if on_vector < P // 2:
@@ -89,14 +87,15 @@ def tile_picked_wedgecv_relu_l_kernel(
             w_cd[2, u] = keep.tile([P, 2 * P], U32, name="w2_cd%d" % u, align_bytes=64)[:]
             w_sc[2, u] = keep.tile([P, 2 * P], U8, name="w2_sc%d" % u, align_bytes=64)[:]
 
-        def quantise_w2(u, h):
+        def quantise_w2(u):
             for s in range(2):
-                cols = slice(s * P + h * P // 2, s * P + (h + 1) * P // 2)
-                nc.vector.quantize_mx(
-                    out=w_cd[2, u][:, cols].bitcast(FP8X4),
-                    scales=w_sc[2, u][:, cols],
-                    in_=w_bf[u, h][:, s * H // 2 : (s + 1) * H // 2],
-                )
+                for h in range(2):
+                    cols = slice(s * P + h * P // 2, s * P + (h + 1) * P // 2)
+                    nc.vector.quantize_mx(
+                        out=w_cd[2, u][:, cols].bitcast(FP8X4),
+                        scales=w_sc[2, u][:, cols],
+                        in_=w_bf[u, h][:, s * H // 2 : (s + 1) * H // 2],
+                    )
 
         def quantise_w1():
             codes = keep.tile([P, H], U32, name="w1_cd", align_bytes=64)
@@ -208,13 +207,11 @@ def tile_picked_wedgecv_relu_l_kernel(
             nc.sync.dma_start(out=out_v[:, :, v0 : v0 + n], in_=res[:])
 
         cast_w2(0, 0, "w2_bf0")
-        cast_w2(1, 0, "w2_bf1", on_vector=0)
-        quantise_w2(0, 0)
-        cast_w2(0, 1, "w2_bf2", on_vector=VECTOR_SHARE)
-        quantise_w2(0, 1)
-        quantise_w2(1, 0)
-        cast_w2(1, 1, "w2_bf2")
-        quantise_w2(1, 1)
+        cast_w2(0, 1, "w2_bf1", on_vector=VECTOR_SHARE)
+        cast_w2(1, 0, "w2_bf2", on_vector=0)
+        quantise_w2(0)
+        cast_w2(1, 1, "w2_bf1")
+        quantise_w2(1)
         v0 = 0
         for q, n in enumerate((256, 256, 256, 128, 128)):
             acc = bank((0, 1, 2, 6, 3)[q], n)

@@ -25,8 +25,10 @@ PACK = 4
 STRIPE = 16
 HALF = T // 2
 VECTOR_SHARE = 24
-SPANS = (0, 512), (512, 256), (768, 128), (896, 128)
+FIRST, SECOND, THIRD, LAST = (0, 512), (512, 256), (768, 128), (896, 128)
+MIDDLE = (512, 384)
 SHARE = (896, 768)
+PITCH = 576
 
 
 def tile_picked_wedgecv_relu_l_kernel(
@@ -46,7 +48,7 @@ def tile_picked_wedgecv_relu_l_kernel(
         nc.vector.memset(w3_sc[:].bitcast(U32), 0)
 
         w2_raw = keep.tile([P, PACK, H], F32, name="w2_raw")
-        w1_raw = [keep.tile([P, PACK, H // 2], F32, name="w1_raw%d" % h, tag="w1_raw%d" % h, align_bytes=64) for h in range(2)]
+        w1_raw = [keep.tile([P, PACK, H // 2], F32, name="w1_raw%d" % h, tag="w1_raw%d" % h) for h in range(2)]
         x_cd = [keep.tile([P, HALF], U32, name="x_cd%d" % h, align_bytes=64) for h in range(2)]
         lists = [keep.tile([P, T // STRIPE], U16, name="list%d" % d) for d in range(2)]
         nc.sync.dma_start(out=w2_raw[:], in_=w2.rearrange("(p j) c -> p j c", j=PACK))
@@ -76,7 +78,7 @@ def tile_picked_wedgecv_relu_l_kernel(
             if on_vector < P // 2:
                 nc.scalar.activation(out=dst[:, on_vector:], in_=src[:, on_vector:], func=COPY)
 
-        w1_bf = keep.tile([P, PACK * H], BF16, name="w1_bf", tag="w1_bf", align_bytes=64)
+        w1_bf = keep.tile([P, PACK * H], BF16, name="w1_bf", align_bytes=64)
 
         def cast_w1(h):
             dst = w1_bf[:].rearrange("p (t m j) -> p m t j", t=PACK, j=PACK)[:, h * P // 2 : (h + 1) * P // 2]
@@ -134,21 +136,22 @@ def tile_picked_wedgecv_relu_l_kernel(
                 product(y[block][:, t, :], 1, t, block * P, P)
 
         top, summed, z, z_cd, z_sc = {}, {}, {}, {}, {}
+        got = [keep.tile([P, PACK, T], F32, name="got%d" % d) for d in range(2)]
 
-        def pair_tile(name, tiles, n):
-            return keep.tile([P, tiles, n], F32, name=name)
+        def fetched(d, t0, t1, v0, n):
+            return got[d][:, t0:t1, v0 : v0 + n]
 
-        def gather(dst, t, d, v0, n, on_vector=False):
+        def gather(t, d, v0, n, on_vector=False):
             window = e[t][:].indirect(lists[d][:, v0 // STRIPE : (v0 + n) // STRIPE])
+            dst = fetched(d, t, t + 1, v0, n)[:, 0, :]
             if on_vector:
                 nc.vector.tensor_copy(dst, window)
             else:
                 nc.scalar.activation(out=dst, in_=window, func=COPY)
 
-        def largest(span, tag, t0, c0, a, b):
-            if span not in top:
-                top[span] = keep.tile([P, PACK, span[1]], F32, name="top%d" % span[0], tag=tag, align_bytes=64)
-            nc.vector.tensor_tensor(top[span][:, t0 : t0 + a.shape[1], c0 : c0 + a.shape[2]], a, b, MAX)
+        def largest(span, t0, t1, v0, n):
+            c0 = v0 - span[0]
+            nc.vector.tensor_tensor(top[span][:, t0:t1, c0 : c0 + n], fetched(0, t0, t1, v0, n), fetched(1, t0, t1, v0, n), MAX)
 
         def add_y(span, whole, c0, n=P):
             if span not in summed:
@@ -188,12 +191,11 @@ def tile_picked_wedgecv_relu_l_kernel(
                 stop=True,
             )
 
-        def finish(spans, a, b, copy=nc.scalar.copy):
-            v0, n = spans[0][0], sum(span[1] for span in spans)
+        def finish(span, a, b, copy=nc.scalar.copy):
+            v0, n = span
             res = keep.tile([P, n], F32, name="res%d_%d" % (v0, a))
             acc = bank(b, n)
-            for span in spans:
-                last_product(span, a, acc[:, span[0] - v0 : span[0] - v0 + span[1]])
+            last_product(span, a, acc[:])
             copy(out=res[:], in_=acc[:])
             nc.sync.dma_start(out=out_v[:, a, v0 : v0 + n], in_=res[:])
 
@@ -218,73 +220,70 @@ def tile_picked_wedgecv_relu_l_kernel(
             product(acc[:], 2, 0, v0, n)
             (nc.scalar.copy, nc.vector.tensor_copy)[q % 2](out=e[0][:, v0 : v0 + n], in_=acc[:])
             v0 = v0 + n
-        first, second, third, last = SPANS
-        mid = (second[0], second[1] + third[1])
-        low = [pair_tile("low%d" % d, 2, last[0]) for d in range(2)]
         make_e(1, (4, 5, 0, 1))
+        gather(0, 1, *THIRD)
         for d in range(2):
-            gather(low[d][:, 0, : SHARE[d]], 0, d, 0, SHARE[d], on_vector=True)
+            gather(0, d, 0, SHARE[d], on_vector=True)
         for d in range(2):
-            gather(low[d][:, 1, : first[1]], 1, d, *first, on_vector=True)
+            gather(1, d, *FIRST, on_vector=True)
         make_e(2, (7, 2))
         make_e(3, (6, 3))
         cast_w1(0)
         cast_w1(1)
-        got = {}
-
-        def on_scalar(t, v0, n):
-            got[t, v0] = [pair_tile("got%d_%d_%d" % (t, v0, d), 1, n) for d in range(2)]
-            for d in range(2):
-                gather(got[t, v0][d][:, 0, :], t, d, v0, n)
-
-        on_scalar(2, *first)
-        on_scalar(3, 0, 256)
-        on_scalar(3, 256, 256)
         for d in range(2):
-            gather(low[d][:, 1, mid[0] :], 1, d, *mid)
-        on_scalar(2, *mid)
-        on_scalar(3, *second)
-        gather(low[1][:, 0, SHARE[1] :], 0, 1, SHARE[1], last[0] - SHARE[1])
-        on_scalar(3, *third)
-        late = [pair_tile("late%d" % d, PACK, last[1]) for d in range(2)]
-        for t in range(PACK):
+            gather(2, d, *FIRST)
+        gather(3, 0, *FIRST)
+        for v0 in (0, 256):
+            gather(3, 1, v0, 256)
+        for t in (1, 2):
             for d in range(2):
-                gather(late[d][:, t, :], t, d, *last)
+                gather(t, d, *MIDDLE)
+        for d in range(2):
+            gather(3, d, *SECOND)
+        gather(3, 0, THIRD[0], THIRD[1] + LAST[1])
+        gather(3, 1, *THIRD)
+        for t in range(3):
+            for d in range(2):
+                gather(t, d, *LAST)
+        gather(3, 1, *LAST)
         quantise_w1()
         for block in range(6):
             make_y(block, block + 2)
-        largest(first, "w1_raw1", 0, 0, low[0][:, :, :512], low[1][:, :, :512])
-        largest(first, "w1_raw1", 2, 0, *[x[:] for x in got[2, 0]])
-        largest(first, "w1_raw1", 3, 0, *[x[:] for x in got[3, 0]])
-        largest(first, "w1_raw1", 3, 256, *[x[:] for x in got[3, 256]])
+        rows = keep.tile([P, PACK * PITCH], F32, name="rows", tag="w1_raw1")
+        top[FIRST] = rows[:, : PACK * FIRST[1]].rearrange("p (t c) -> p t c", t=PACK)
+        top[MIDDLE] = rows[:].rearrange("p (t c) -> p t c", t=PACK)[:, :, : MIDDLE[1]]
+        largest(FIRST, 0, 3, *FIRST)
+        largest(FIRST, 3, 4, 0, 256)
+        largest(FIRST, 3, 4, 256, 256)
         for b in range(4):
-            add_y(first, first, b * P)
+            add_y(FIRST, FIRST, b * P)
             if b < 2:
-                relu(first, b * P, P, on_gpsimd=True)
-        largest(mid, "w1_raw1", 0, 0, low[0][:, :, 512:768], low[1][:, :, 512:768])
-        relu(first, 2 * P, 2 * P)
-        largest(mid, "w1_raw1", 2, 0, *[x[:] for x in got[2, mid[0]]])
-        quantise_z(first)
-        finish((first,), 0, 2)
-        largest(mid, "w1_raw1", 3, 0, *[x[:] for x in got[3, second[0]]])
-        add_y(second, mid, 0)
+                relu(FIRST, b * P, P, on_gpsimd=True)
+        largest(MIDDLE, 0, 2, *SECOND)
+        relu(FIRST, 2 * P, 2 * P)
+        largest(MIDDLE, 2, 3, *MIDDLE)
+        quantise_z(FIRST)
+        finish(FIRST, 0, 2)
+        largest(MIDDLE, 3, 4, *SECOND)
+        largest(MIDDLE, 0, 2, *THIRD)
+        add_y(SECOND, MIDDLE, 0)
         make_y(6, 6)
-        add_y(second, mid, P)
+        add_y(SECOND, MIDDLE, P)
         make_y(7, 7)
-        largest(mid, "w1_raw1", 0, second[1], low[0][:, :, 768:], low[1][:, :, 768:])
-        relu(second)
-        largest(mid, "w1_raw1", 3, second[1], *[x[:] for x in got[3, third[0]]])
-        quantise_z(second)
-        finish_both(second, 4)
-        add_y(third, mid, 0)
-        finish((first,), 1, 6)
-        largest(last, "summed512", 0, 0, late[0][:, :3], late[1][:, :3])
-        largest(last, "summed512", 3, 0, late[0][:, 3:], late[1][:, 3:])
-        relu(third)
-        add_y(last, last, 0)
-        quantise_z(third)
-        finish_both(third, 5)
-        relu(last)
-        quantise_z(last)
-        finish((last,), 0, 0, nc.vector.tensor_copy)
-        finish((last,), 1, 1)
+        largest(MIDDLE, 3, 4, *THIRD)
+        relu(SECOND)
+        add_y(THIRD, MIDDLE, 0)
+        quantise_z(SECOND)
+        finish_both(SECOND, 4)
+        finish(FIRST, 1, 6)
+        top[LAST] = keep.tile([P, PACK, LAST[1]], F32, name="top_last", tag="summed512", align_bytes=64)
+        largest(LAST, 0, 3, *LAST)
+        largest(LAST, 3, 4, *LAST)
+        relu(THIRD)
+        add_y(LAST, LAST, 0)
+        quantise_z(THIRD)
+        finish_both(THIRD, 5)
+        relu(LAST)
+        quantise_z(LAST)
+        finish(LAST, 0, 0, nc.vector.tensor_copy)
+        finish(LAST, 1, 1)

from contextlib import ExitStack

import concourse.mybir as mybir

K, T, H, N = 512, 1024, 512, 256
FLOPS = 2 * K * H * T * 2 + 2 * H * N * T

F32 = mybir.dt.float32
BF16 = mybir.dt.bfloat16
I32 = mybir.dt.int32
U32 = mybir.dt.uint32
U16 = mybir.dt.uint16
U8 = mybir.dt.uint8
FP8X4 = mybir.dt.float8_e4m3fn_x4
FP4X4 = mybir.dt.float4_e2m1fn_x4
ADD = mybir.AluOpType.add
MULT = mybir.AluOpType.mult
MAX = mybir.AluOpType.max
MIN = mybir.AluOpType.min
COPY = mybir.ActivationFunctionType.Copy

LARGEST = (2.0 - 2.0**-23) * 2.0**127
P = 128
PACK = 4
STRIPE = 16
HALF = T // 2
VECTOR_SHARE = 24
FIRST, SECOND, THIRD, LAST = (0, 512), (512, 256), (768, 128), (896, 128)
MIDDLE = (512, 384)
SHARE = (896, 768)
PITCH = 576


def tile_picked_wedgecv_relu_l_kernel(
    tc, x_words, x_scales, w1, w2, w3_words, w3_scales, pos1, pos2, out
):
    nc = tc.nc
    with ExitStack() as ctx:
        keep = ctx.enter_context(tc.tile_pool(name="keep", bufs=1))
        psum = ctx.enter_context(tc.psum_pool(name="psum", bufs=1))

        def bank(b, *shape):
            return psum.tile([P, *shape], F32, name="bank%d" % b, tag="bank%d" % b)

        x_sc = keep.tile([P, T], U8, name="x_sc", align_bytes=64)
        w3_sc = keep.tile([P, N], U8, name="w3_sc", align_bytes=64)
        nc.vector.memset(x_sc[:].bitcast(U32), 0)
        nc.vector.memset(w3_sc[:].bitcast(U32), 0)

        w2_raw = keep.tile([P, PACK, H], F32, name="w2_raw")
        w1_raw = [keep.tile([P, PACK, H // 2], F32, name="w1_raw%d" % h, tag="w1_raw%d" % h) for h in range(2)]
        x_cd = [keep.tile([P, HALF], U32, name="x_cd%d" % h, align_bytes=64) for h in range(2)]
        lists = [keep.tile([P, T // STRIPE], U16, name="list%d" % d) for d in range(2)]
        nc.sync.dma_start(out=w2_raw[:], in_=w2.rearrange("(p j) c -> p j c", j=PACK))
        x_src = x_words[0].rearrange("p n r -> p (n r)").bitcast(I32)
        for r in range(4):
            nc.sync.dma_start(out=x_sc[r:P:32, :].bitcast(I32), in_=x_scales[0][r:16:4, :].bitcast(I32))
        nc.sync.dma_start(out=x_cd[0][:].bitcast(I32), in_=x_src[:, :HALF])
        nc.sync.dma_start(out=x_cd[1][:].bitcast(I32), in_=x_src[:, HALF:])
        nc.sync.dma_start(lists[0][:], pos1)
        nc.sync.dma_start(lists[1][:], pos2)
        for h in range(2):
            cols = slice(h * H // 2, (h + 1) * H // 2)
            nc.sync.dma_start(out=w1_raw[h][:], in_=w1.rearrange("(p j) c -> p j c", j=PACK)[:, :, cols])
        w3_cd = keep.tile([P, 2 * N], U8, name="w3_cd", align_bytes=64)
        nc.sync.dma_start(out=w3_cd[:].bitcast(I32), in_=w3_words[0].bitcast(I32))
        for r in range(4):
            nc.sync.dma_start(out=w3_sc[r:P:32, :].bitcast(I32), in_=w3_scales[0][r:16:4, :].bitcast(I32))

        w_bf, w_cd, w_sc = {}, {}, {}

        def cast_w2(u, h, tag, on_vector=P // 2):
            w_bf[u, h] = keep.tile([P, H], BF16, name="w2_bf%d%d" % (u, h), tag=tag, align_bytes=64)[:]
            dst = w_bf[u, h].rearrange("p (s m j) -> p m j s", s=2, j=PACK)
            src = w2_raw[:].rearrange("p j (m t) -> p m j t", t=PACK)[:, h * P // 2 : (h + 1) * P // 2, :, 2 * u : 2 * u + 2]
            if on_vector:
                nc.vector.tensor_copy(out=dst[:, :on_vector], in_=src[:, :on_vector])
            if on_vector < P // 2:
                nc.scalar.activation(out=dst[:, on_vector:], in_=src[:, on_vector:], func=COPY)

        w1_bf = keep.tile([P, PACK * H], BF16, name="w1_bf", align_bytes=64)

        def cast_w1(h):
            dst = w1_bf[:].rearrange("p (t m j) -> p m t j", t=PACK, j=PACK)[:, h * P // 2 : (h + 1) * P // 2]
            src = w1_raw[h][:].rearrange("p j (m t) -> p m t j", t=PACK)
            nc.gpsimd.tensor_scalar(dst, src, 1.0, 0.0, MULT, ADD)

        for u in range(2):
            w_cd[2, u] = keep.tile([P, 2 * P], U32, name="w2_cd%d" % u, align_bytes=64)[:]
            w_sc[2, u] = keep.tile([P, 2 * P], U8, name="w2_sc%d" % u, align_bytes=64)[:]

        def quantise_w2(u):
            for s in range(2):
                for h in range(2):
                    cols = slice(s * P + h * P // 2, s * P + (h + 1) * P // 2)
                    nc.vector.quantize_mx(
                        out=w_cd[2, u][:, cols].bitcast(FP8X4),
                        scales=w_sc[2, u][:, cols],
                        in_=w_bf[u, h][:, s * H // 2 : (s + 1) * H // 2],
                    )

        def quantise_w1():
            codes = keep.tile([P, H], U32, name="w1_cd", align_bytes=64)
            scales = keep.tile([P, H], U8, name="w1_sc", align_bytes=64)
            for u in range(2):
                w_cd[1, u], w_sc[1, u] = codes[:, 2 * P * u : 2 * P * (u + 1)], scales[:, 2 * P * u : 2 * P * (u + 1)]
            nc.vector.quantize_mx(out=codes[:].bitcast(FP8X4), scales=scales[:], in_=w1_bf[:])

        e = [keep.tile([P, T], F32, name="e%d" % t) for t in range(PACK)]

        def product(acc, w, t, v0, n):
            m = slice((t % 2) * P, (t % 2 + 1) * P)
            nc.tensor.matmul_mx(
                out=acc,
                lhsT=w_cd[w, t // 2][:, m].bitcast(FP8X4),
                lhsT_scale=w_sc[w, t // 2][:, m],
                rhs=x_cd[v0 // HALF][:, v0 % HALF : v0 % HALF + n].bitcast(FP8X4),
                rhs_scale=x_sc[:, v0 : v0 + n],
                start=True,
                stop=True,
            )

        def make_e(t, banks):
            n = T // len(banks)
            for q, b in enumerate(banks):
                v0 = (HALF + q * n) % T
                acc = bank(b, n)
                product(acc[:], 2, t, v0, n)
                nc.scalar.copy(out=e[t][:, v0 : v0 + n], in_=acc[:])

        y = {}

        def make_y(block, b):
            y[block] = bank(b, PACK, P)
            for t in range(PACK):
                product(y[block][:, t, :], 1, t, block * P, P)

        top, summed, z, z_cd, z_sc = {}, {}, {}, {}, {}
        got = [keep.tile([P, PACK, T], F32, name="got%d" % d) for d in range(2)]

        def fetched(d, t0, t1, v0, n):
            return got[d][:, t0:t1, v0 : v0 + n]

        def gather(t, d, v0, n, on_vector=False):
            window = e[t][:].indirect(lists[d][:, v0 // STRIPE : (v0 + n) // STRIPE])
            dst = fetched(d, t, t + 1, v0, n)[:, 0, :]
            if on_vector:
                nc.vector.tensor_copy(dst, window)
            else:
                nc.scalar.activation(out=dst, in_=window, func=COPY)

        def largest(span, t0, t1, v0, n):
            c0 = v0 - span[0]
            nc.vector.tensor_tensor(top[span][:, t0:t1, c0 : c0 + n], fetched(0, t0, t1, v0, n), fetched(1, t0, t1, v0, n), MAX)

        def add_y(span, whole, c0, n=P):
            if span not in summed:
                summed[span] = keep.tile([P, PACK * span[1]], BF16, name="summed%d" % span[0], tag="summed%d" % span[0], align_bytes=64)
            block, b0 = divmod(span[0] + c0, P)
            nc.vector.tensor_tensor(
                summed[span][:, PACK * c0 : PACK * (c0 + n)].rearrange("p (c i t) -> p c t i", i=2, t=PACK),
                top[whole][:, :, span[0] - whole[0] + c0 : span[0] - whole[0] + c0 + n].rearrange("p t (c i) -> p c t i", i=2),
                y[block][:, :, b0 : b0 + n].rearrange("p t (c i) -> p c t i", i=2),
                ADD,
            )

        def relu(span, c0=0, n=None, on_gpsimd=False):
            if span not in z:
                z[span] = keep.tile([P, PACK * span[1]], BF16, name="z%d" % span[0], align_bytes=64)
            cols = slice(PACK * c0, PACK * (c0 + (n or span[1])))
            if on_gpsimd:
                nc.gpsimd.tensor_scalar(z[span][:, cols], summed[span][:, cols], LARGEST, 0.0, MIN, MAX)
            else:
                nc.vector.tensor_scalar_max(z[span][:, cols], summed[span][:, cols], 0.0)

        def quantise_z(span):
            z_cd[span] = keep.tile([P, span[1]], U32, name="z_cd%d" % span[0], align_bytes=64)
            z_sc[span] = keep.tile([P, span[1]], U8, name="z_sc%d" % span[0], align_bytes=64)
            nc.vector.quantize_mx(out=z_cd[span][:].bitcast(FP8X4), scales=z_sc[span][:], in_=z[span][:])

        out_v = out.rearrange("(a p) v -> p a v", p=P)

        def last_product(span, a, acc):
            nc.tensor.matmul_mx(
                out=acc,
                lhsT=w3_cd[:, 2 * P * a : 2 * P * (a + 1)].bitcast(FP4X4),
                lhsT_scale=w3_sc[:, P * a : P * (a + 1)],
                rhs=z_cd[span][:].bitcast(FP8X4),
                rhs_scale=z_sc[span][:],
                start=True,
                stop=True,
            )

        def finish(span, a, b, copy=nc.scalar.copy):
            v0, n = span
            res = keep.tile([P, n], F32, name="res%d_%d" % (v0, a))
            acc = bank(b, n)
            last_product(span, a, acc[:])
            copy(out=res[:], in_=acc[:])
            nc.sync.dma_start(out=out_v[:, a, v0 : v0 + n], in_=res[:])

        def finish_both(span, b):
            v0, n = span
            res = keep.tile([P, N // P, n], F32, name="res%d" % v0)
            acc = bank(b, N // P, n)
            for a in range(N // P):
                last_product(span, a, acc[:, a, :])
            nc.scalar.copy(out=res[:], in_=acc[:])
            nc.sync.dma_start(out=out_v[:, :, v0 : v0 + n], in_=res[:])

        cast_w2(0, 0, "w2_bf0")
        cast_w2(0, 1, "w2_bf1", on_vector=VECTOR_SHARE)
        cast_w2(1, 0, "w2_bf2", on_vector=0)
        quantise_w2(0)
        cast_w2(1, 1, "w2_bf1")
        quantise_w2(1)
        v0 = 0
        for q, n in enumerate((256, 256, 256, 128, 128)):
            acc = bank((0, 1, 2, 6, 3)[q], n)
            product(acc[:], 2, 0, v0, n)
            (nc.scalar.copy, nc.vector.tensor_copy)[q % 2](out=e[0][:, v0 : v0 + n], in_=acc[:])
            v0 = v0 + n
        make_e(1, (4, 5, 0, 1))
        gather(0, 1, *THIRD)
        for d in range(2):
            gather(0, d, 0, SHARE[d], on_vector=True)
        for d in range(2):
            gather(1, d, *FIRST, on_vector=True)
        make_e(2, (7, 2))
        make_e(3, (6, 3))
        cast_w1(0)
        cast_w1(1)
        for d in range(2):
            gather(2, d, *FIRST)
        gather(3, 0, *FIRST)
        for v0 in (0, 256):
            gather(3, 1, v0, 256)
        for t in (1, 2):
            for d in range(2):
                gather(t, d, *MIDDLE)
        for d in range(2):
            gather(3, d, *SECOND)
        gather(3, 0, THIRD[0], THIRD[1] + LAST[1])
        gather(3, 1, *THIRD)
        for t in range(3):
            for d in range(2):
                gather(t, d, *LAST)
        gather(3, 1, *LAST)
        quantise_w1()
        for block in range(6):
            make_y(block, block + 2)
        rows = keep.tile([P, PACK * PITCH], F32, name="rows", tag="w1_raw1")
        top[FIRST] = rows[:, : PACK * FIRST[1]].rearrange("p (t c) -> p t c", t=PACK)
        top[MIDDLE] = rows[:].rearrange("p (t c) -> p t c", t=PACK)[:, :, : MIDDLE[1]]
        largest(FIRST, 0, 3, *FIRST)
        largest(FIRST, 3, 4, 0, 256)
        largest(FIRST, 3, 4, 256, 256)
        for b in range(4):
            add_y(FIRST, FIRST, b * P)
            if b < 2:
                relu(FIRST, b * P, P, on_gpsimd=True)
        largest(MIDDLE, 0, 2, *SECOND)
        relu(FIRST, 2 * P, 2 * P)
        largest(MIDDLE, 2, 3, *MIDDLE)
        quantise_z(FIRST)
        finish(FIRST, 0, 2)
        largest(MIDDLE, 3, 4, *SECOND)
        largest(MIDDLE, 0, 2, *THIRD)
        add_y(SECOND, MIDDLE, 0)
        make_y(6, 6)
        add_y(SECOND, MIDDLE, P)
        make_y(7, 7)
        largest(MIDDLE, 3, 4, *THIRD)
        relu(SECOND)
        add_y(THIRD, MIDDLE, 0)
        quantise_z(SECOND)
        finish_both(SECOND, 4)
        finish(FIRST, 1, 6)
        top[LAST] = keep.tile([P, PACK, LAST[1]], F32, name="top_last", tag="summed512", align_bytes=64)
        largest(LAST, 0, 3, *LAST)
        largest(LAST, 3, 4, *LAST)
        relu(THIRD)
        add_y(LAST, LAST, 0)
        quantise_z(THIRD)
        finish_both(THIRD, 5)
        relu(LAST)
        quantise_z(LAST)
        finish(LAST, 0, 0, nc.vector.tensor_copy)
        finish(LAST, 1, 1)
